import numpy as np, ml_dtypes
CORES = [16,18,20,22]
N = 4
import mx_ref
BF = ml_dtypes.bfloat16
def gcols(t, e):
    v = np.concatenate([t.reshape(8, 16, -1, 4), np.zeros((8, 16, 1, 4), BF)], axis=2)
    return np.ascontiguousarray(np.stack([v[g][:, e[g]] for g in range(8)])).reshape(128, -1)
def tile(rs):
    return np.stack(rs, axis=2).reshape(128, -1).astype(BF)
def pick(q, e):
    c = np.concatenate([q[0].reshape(128, -1, 4), np.zeros((128, 1, 4), np.uint8)], axis=1); s = np.concatenate([q[1], np.ones((16, 1), np.uint8)], axis=1)
    return (np.ascontiguousarray(c[:, e].reshape(128, -1)), np.ascontiguousarray(s[:, e]))
def join(*qs):
    return (np.concatenate([q[0] for q in qs], axis=1), np.concatenate([q[1] for q in qs], axis=1))
def put(q, e, v):
    c, s = q[0].reshape(128, -1, 4).copy(), q[1].copy(); c[:, e] = v[0].reshape(128, -1, 4); s[:, e] = v[1]
    return (c.reshape(128, -1), s)
def pk(c, s):
    return (np.ascontiguousarray(c), mx_ref.live(s))
def emit(q):
    return q[0], q[1]
def packed(v, rng):
    q = [mx_ref.quantize(np.ascontiguousarray(v[r])) for r in range(N)]
    return np.stack([a for a, b in q]), np.stack([mx_ref.plane(b, rng) for a, b in q])
def values_of_codes():
    e, c = np.zeros((128, 128, 4), np.float32), np.zeros((128, 2, 4), np.uint8)
    e[np.arange(128), np.arange(128), 0] = 1
    c[:127, :, 0] = np.arange(256).reshape(2, 128).T[:127]
    return mx_ref.matmul(mx_ref.quantize(e.reshape(128, 512).astype(BF)), (c.reshape(128, 8), np.full((16, 2), 127, np.uint8))).T.reshape(-1).astype(np.float64)
CODE_VALUE, SCALE_VALUE = values_of_codes(), 2.0 ** (np.arange(256) - 127.0)
def decode(q):
    return (CODE_VALUE[q[0]].reshape(16, 8, -1, 4) * SCALE_VALUE[q[1]][:, None, :, None] + 0.0).reshape(128, -1).astype(np.float32)
def f(rng, *shape):
    return mx_ref.flush((rng.standard_normal(shape, dtype=np.float32) * np.exp2(rng.integers(-2, 3, shape[:-1] + (1,)))).astype(BF))
def wide(rng, *shape, cols=0):
    v = rng.standard_normal(shape, dtype=np.float32) * np.exp2(rng.integers(-12, 13, shape)).astype(np.float32)
    if cols: v *= np.repeat(np.exp2(rng.integers(-cols, cols + 1, shape[:-2] + (1, shape[-1] // 4))) * (rng.random(shape[:-2] + (1, shape[-1] // 4)) > 0.0625), 4, axis=-1).astype(np.float32)
    return mx_ref.flush(v.astype(BF))
C, P, R = 384, 96, 2
def big(v):
    v = v.astype(np.float32)
    v[np.abs(v) < np.float32(2.0 ** -16)] = 0
    return v.astype(BF)
def numbers_of(rng):
    return {"x": big(f(rng, N, 128, 4 * C)), "u": np.array(f(rng, N, 128, 512)), "v": np.array(f(rng, N, 128, 512))}
def layers(rng):
    return big(f(rng, N, 128, 2048)).reshape(N, 8, 16, 4, 8, 16, 4)
def weights(rng, w):
    c, p = packed(np.ascontiguousarray(w).reshape(N, 128, 2048), rng)
    return {"wc": c, "ws": p}
def setup_inputs(rng):
    return {**numbers_of(rng), **weights(rng, layers(rng))}
def setup_inputs_ties(rng):
    d = numbers_of(rng)
    e = rng.permutation(N)
    x = d["x"].reshape(N, 8, 16, C, 4)
    for r in range(N):
        k = rng.permutation(C) % 3
        if r == e[0]: k = np.zeros(C, int)
        elif r in e[2::2]: k = rng.permutation(3)[np.arange(C) % 3]
        a = x[r][:, :8, :3].copy()
        a[:, :, 2] = 0
        x[r][:, :8] = a[:, :, k]
    x[e[1]] = 0
    u = d["u"].reshape(N, 8, 16, 128, 4)
    for i in range(5): u[:, :, 8:, i::16] = 0
    w = layers(rng)
    w[:, :, :, :, :, :8] = 0
    return {"x": x.reshape(N, 128, 4 * C), "u": u.reshape(N, 128, 512), "v": d["v"], **weights(rng, w)}
def setup_inputs_near(rng):
    d = numbers_of(rng)
    x = d["x"].astype(np.float32).reshape(N, 8, 16, C, 4)
    x[:, :, :9] = 0
    u = d["u"].reshape(N, 128, 128, 4)
    for i in range(5): u[:, :, i::16] = 0
    o = rng.permutation(N) % 4
    for r in range(N):
        k = 2.0 ** -30 if o[r] else 1.0
        c = rng.integers(0, 2, (8, 1)) * 2.0 - 1.0
        s = rng.integers(-1, 2, (8, C, 4))
        if o[r] < 2:
            n = rng.integers(0, 16, (8, C))
            x[r, :, 0] = ((n[:, :, None] >> np.arange(4)) & 1) * np.exp2(np.arange(4) - 23.0)
            x[r, :, 1, :, 0] = 2.0 ** -10
            x[r, :, 2] = s * 2.0 ** -10
            x[r, :, 8, :, 0] = c
        else:
            x[r, :, 0, :, 0] = c * rng.integers(1, 16, (8, C)) * 2.0 ** -29
            x[r, :, 2] = s * 2.0 ** -29
        for g in rng.permutation(8)[:4]: x[r, g, 8 if o[r] < 2 else 0, rng.integers(C), 0] = 2.0 ** 29 * (rng.integers(0, 2) * 2.0 - 1.0)
        for h in range(0, 128, 16):
            u[r, h, h + 4] = k
            u[r, h + 1, h + 4, 0] = k
            u[r, h + 8, h + 4, 0] = k
            for i in range(4): u[r, h + 2, h + i, i] = k
    w = layers(rng)
    w[:, :, :9] = 0
    w[:, :, :, :, :, :9] = 0
    return {"x": x.reshape(N, 128, 4 * C).astype(BF), "u": u.reshape(N, 128, 512), "v": d["v"], **weights(rng, w)}
def setup_inputs_skew(rng):
    d = numbers_of(rng)
    x = d["x"].astype(np.float32).reshape(N, 8, 16, C, 4)
    t = (1 + (2 * rng.integers(0, 64, (N, 8, 8, C // 2, 4)) + 1) / 128) * np.exp2(-rng.integers(8, 15, (N, 8, 8, C // 2, 4)).astype(float)) * (rng.integers(0, 2, (N, 8, 8, C // 2, 4)) * 2.0 - 1.0)
    t[:, :, 3, :, 1] = 1.96875
    x[:, :, 8:, ::2] = t * np.exp2(rng.integers(-2, 3, (N, 8, 1, C // 2, 1)).astype(float))
    u = d["u"].reshape(N, 128, 128, 4)
    for i in range(5): u[:, :, i::16] = 0
    for h in range(0, 128, 16):
        for b in range(12): u[:, h + b // 4, h + 4, b % 4] = 2.0 ** b
        for i in range(4): u[:, h + 3, h + i, i] = 1
    n = -(-C // 7)
    n2 = n - (-(C - n) // 5)
    n3 = n2 - (-(C - n2) // 3)
    down = C - 1 - np.arange(C)
    for r in range(N):
        for j, g in enumerate(rng.permutation(8)):
            a = np.append(rng.permutation(np.delete(np.arange(4), j % 4)), j % 4)
            two = np.zeros((C, 4), int)
            if j < 6:
                two[:n, a[0]] = 1
                two[n:n2, a[1]] = 1
            if j < 4: two[n2:n3, a[2]] = 1
            if j >= 6: two[-(-2 * C // 5):] = 1
            o = rng.permutation(C)
            x[r, g][:3, o] = (down[None, :, None] >> (4 * np.arange(3)[:, None, None] + np.arange(4))) & 1
            x[r, g][3, o] = np.where(two > 0, 1, -rng.integers(0, 2, (C, 4)))
    w = layers(rng)
    w[:, :, :, :, :, :4] = 0
    return {"x": x.reshape(N, 128, 4 * C).astype(BF), "u": u.reshape(N, 128, 512), "v": d["v"], **weights(rng, w)}
def setup_inputs_huge(rng):
    d = numbers_of(rng)
    o = rng.permutation(N)
    h = rng.permutation(8)
    x = -0.95 - 0.05 * rng.random((N, 8, 16, C, 4))
    x[:, h[4:]] = (0.75 + 0.1 * rng.random((N, 4, 16, C, 4))) * rng.choice([-1.0, 1.0], (N, 4, 1, C, 1))
    u = d["u"].reshape(N, 128, 128, 4)
    for i in range(5): u[:, :, i::16] = 0
    for r in range(N):
        if o[r] < N // 2: x[r] = (0.8 + 0.1 * rng.random((8, 16, C, 4))) * rng.choice([-1.0, 1.0], (1, 1, C, 1))
        for g in range(8):
            for i in range(5):
                a, n = 16 * int(rng.choice(h[4:])), 16
                if i == 4 and o[r] < N // 2: a, n = 0, 128
                u[r, a:a + n, 16 * g + i] = (2.0 ** 30 * (1 - 0.05 * rng.random((n, 4))) * rng.choice([-1.0, 1.0])).astype(np.float32).astype(BF)
    w = np.zeros((N, 128, 4, 128, 4), np.float32)
    i = np.arange(128)
    for b in range(4): w[:, i, b, i, b] = -1
    return {"x": (2.0 ** 30 * x).astype(np.float32).reshape(N, 128, 4 * C).astype(BF), "u": u.reshape(N, 128, 512), "v": d["v"], **weights(rng, w.astype(BF))}
def setup_inputs_spread(rng):
    d = setup_inputs(rng)
    d["x"] = big(wide(rng, N, 128, 4 * C, cols=6))
    return d
def check_inputs(d):
    b = []
    for k in ("x", "u", "v"):
        a = np.abs(d[k].astype(np.float32))
        if not (np.isfinite(a).all() and ((a == 0) | (a >= 2.0 ** -30) & (a <= 2.0 ** 30)).all()): b.append("a value of " + k)
    none, least, most = [emit(mx_ref.quantize(np.full((128, 16), k, np.float32).astype(BF)))[1][0, 0] for k in (0.0, 2.0 ** -30, 2.0 ** 30)]
    for r in range(N):
        if ((d["wc"][r] == 0x7F) | (d["wc"][r] == 0xFF)).any(): b.append("wc: a code that is no number")
        s = mx_ref.live(d["ws"][r])
        if ((s != none) & ((s < least) | (s > most))).any(): b.append("ws: a scale out of range")
    return b
def divide(sums):
    g = np.arange(8)
    first, end = np.zeros((4, 8), np.int64), np.full((4, 8), C)
    a, left = np.zeros(8, np.int64), np.ones((4, 8), bool)
    for m in (4, 3, 2):
        worth = sums - np.stack([sums[k, g, a] for k in range(4)])[:, :, None]
        e = np.sum(m * worth < worth[:, :, -1:], axis=2)
        e[~left] = C + 1
        k = np.argmin(e, axis=0)
        first[k, g] = a
        a = e[k, g]
        end[k, g] = a
        left[k, g] = False
    first[np.argmax(left, axis=0), g] = a
    return first, end
def reference(x, u, v, wc, ws):
    qu = [mx_ref.quantize(u[r]) for r in range(N)]
    lay = [pk(wc[r], ws[r]) for r in range(N)]
    now = [x[r] for r in range(N)]
    of = [np.arange(k * P, k * P + P) for k in range(4)]
    slot_of = np.zeros((N, 8, C), np.int64)
    for t in range(R):
        sent, best, made = [], [], []
        slot_of[:] = -1
        for r in range(N):
            s = mx_ref.matmul(qu[r], mx_ref.quantize(now[r])) + np.float32(0.0)
            o = np.argsort(-s[4::16], axis=1, kind="stable")
            worth = np.stack([1 + (np.take_along_axis(s[k::16], o, axis=1) > 0) for k in range(4)])
            first, end = divide(np.concatenate([np.zeros((4, 8, 1), np.int64), np.cumsum(worth, axis=2)], axis=2))
            slots = []
            for k in range(4):
                i = first[k][:, None] + np.arange(P)
                slots.append(np.where(i < end[k][:, None], np.take_along_axis(o, np.minimum(i, C - 1), axis=1), -1))
            slots = np.concatenate(slots, axis=1)
            for g in range(8):
                j = np.nonzero(slots[g] >= 0)[0]
                slot_of[r, g, slots[g, j]] = j
            sent.append(mx_ref.quantize(gcols(now[r], slots)))
            best.append(gcols(now[r], o[:, :P]))
        for r in range(N):
            came = decode(join(*[pick(sent[(r - k) % N], of[k]) for k in range(4)]))
            z = mx_ref.quantize(((came + np.tile(best[r].astype(np.float32), (1, 4))) * np.float32(0.5)).astype(BF))
            made.append(mx_ref.quantize(tile([mx_ref.matmul(pick(lay[r], np.arange(128 * b, 128 * b + 128)), z) * np.float32(0.03125) for b in range(4)])))
        for r in range(N):
            back = decode(join(*[pick(made[(r + k) % N], of[k]) for k in range(4)])).astype(BF)
            now[r] = (now[r].astype(np.float32) + gcols(back, slot_of[r]).astype(np.float32)).astype(BF)
    y, sl = np.zeros((N, 128, C), np.float32), np.zeros((N, 8, C), np.float32)
    oc, osc = np.zeros((N, 128, 4 * C), np.uint8), np.zeros((N, 16, C), np.uint8)
    for r in range(N):
        q = mx_ref.quantize(now[r])
        y[r] = mx_ref.matmul(mx_ref.quantize(v[r]), q)
        sl[r] = slot_of[r]
        oc[r], osc[r] = emit(q)
    return {"y": y, "sl": sl, "oc": oc, "osc": osc}

@@ -1,0 +1,503 @@
+from concourse.bass import DstId, RemoteDMATransfer
+from concourse.mybir import dt, AluOpType as ALU, AxisListType, ActivationFunctionType as ACT
+
+C, P = 384, 96
+R3 = 3 * P
+HALF = R3 // 2
+BIG = 1.0e28
+DUMP = 480
+POS = DUMP * 5
+NB0 = 1024
+XW = NB0 + C
+
+SCRATCH = {}
+SEMAPHORES = ["sv", "ss", "st", "sp"]
+WIDTH = {}
+HOME = {}
+
+
+def _b(name, n, dtype="float32", where="sbuf"):
+    SCRATCH[name] = (where, [128, n], dtype)
+    WIDTH[name] = n
+    HOME[name] = (name, 0)
+
+
+def _q(name, n):
+    _b("q" + name, n, "float8_e4m3fn_x4")
+    _b("s" + name, n, "uint8")
+
+
+def _pack(buf, pieces):
+    at = 0
+    for name, n in pieces:
+        WIDTH[name] = n
+        HOME[name] = (buf, at)
+        at += -(-n // 8) * 8
+    SCRATCH[buf] = ("sbuf", [128, at], "float32")
+
+
+for _i in range(8):
+    _b("ps%d" % _i, 512, "float32", "psum")
+for _r in range(2):
+    _b("xw%d" % _r, 4 * XW, "bfloat16")
+    _b("srt%d" % _r, POS)
+    for _n, _w in (("x", C), ("b", C), ("lb", R3), ("h", R3), ("lh", R3)):
+        _q("%s%d" % (_n, _r), _w)
+    SEMAPHORES += ["ab%d" % _r, "ah%d" % _r, "lb%d" % _r, "lh%d" % _r]
+_b("xf", 4 * C, "bfloat16")
+for _n, _w in (("xf", C), ("u", 128), ("ua", 128), ("v", 128), ("w", 512), ("e1", 512), ("eh", 512), ("g", 128), ("z0", 128), ("z", R3), ("h0k", 128)):
+    _q(_n, _w)
+for _n, _w in (("ut", 512), ("vt", 512), ("eone", 2048), ("ebt", 2048), ("ebth", 2048), ("gt", 512), ("gt1", 512), ("bt", 4 * C),
+               ("e3", 4 * R3), ("zt0", 512), ("zt", 4 * R3), ("ht0", 512), ("ht", 4 * R3), ("jk", 4416), ("fs", C), ("fb", C), ("rz16", C), ("cm", 160)):
+    _b(_n, _w, "bfloat16")
+MTN = (384, 320, 256, 192, 128, 128)
+for _i in range(6):
+    _b("mt%d" % _i, 4 * MTN[_i], "bfloat16")
+    _q("m%d" % _i, MTN[_i])
+_b("wsc", 392)
+_b("yt", C)
+_pack("consts", [(_n, C) for _n in ("r16", "r4", "ij", "rs1", "nm1", "nm2", "rs4", "n41", "n42", "nm16", "rst16", "nm4", "rst4", "ioj", "ni")]
+      + [(_n, 24) for _n in ("c24", "ct", "ki", "si", "st", "koff")] + [("cols", 16), ("hm", 32), ("hm1", 32), ("msk", 40), ("rc", 8)])
+_pack("wide", [(_n, C) for _n in ("vm", "zz", "dg", "cx", "z2", "rl", "fj", "gm", "zs", "gm2", "zs2", "slg", "sl1", "sl2")] + [("ge", P), ("ze", P)])
+_pack("small", [(_n, 24) for _n in ("rsum", "cd", "pd", "pf")] + [("ky", 40), ("kt", 32), ("wa", 48), ("tmp", 24 * 16)]
+      + [(_n, 8) for _n in ("kk", "cnt", "th", "rm", "rr", "aa", "a8", "am", "w3", "w4")])
+for _n, _w in (("icol", 16), ("ilist", 8)):
+    _b(_n, _w, "int32")
+for _n, _w in (("ulist", 8), ("pl", 24), ("of", 8), ("pu", 24), ("l1", 96), ("l2", 96), ("l3", 24)):
+    _b(_n, _w, "uint16")
+NDMA = 24
+SEMAPHORES += ["d%d" % _i for _i in range(NDMA)]
+
+
+def rank_program(g, core, T, topo):
+    rank = T.rank_of(core)
+    if rank is None:
+        return
+    V, S, PE, G, SY = "v", "s", "t", "p", "y"
+    eng = {V: g.vector, S: g.scalar, PE: g.tensor, G: g, SY: g.sync}
+    count = {V: 0, S: 0, PE: 0, G: 0}
+    clock = {q: {} for q in eng}
+    evclock = {}
+    hist = {}
+    used = []
+
+    def A(n, lo=None, hi=None, st=1):
+        if lo is None:
+            lo, hi = 0, WIDTH[n]
+        buf, at = HOME[n]
+        lo, hi = lo + at, hi + at
+        return (T[buf][:, lo:hi] if st == 1 else T[buf][:, lo:hi:st], (buf, lo, hi, st))
+
+    def meet(a, b):
+        if a[0].startswith("ps"):
+            return True
+        if a[2] <= b[1] or b[2] <= a[1]:
+            return False
+        if a[3] == b[3] and a[3] > 1 and (a[1] - b[1]) % a[3]:
+            return False
+        return True
+
+    def need(q, outs, ins):
+        want = {}
+        for kind, regs in (("w", outs), ("r", ins)):
+            for r in regs:
+                for (r2, k2, ev) in hist.get(r[0], ()):
+                    bank = r[0].startswith("ps") and ev[2] != q
+                    if (kind == "w" or k2 == "w" or bank) and meet(r, r2):
+                        want[ev[0]] = max(want.get(ev[0], 0), ev[1])
+        ck = clock[q]
+        for s in sorted(want):
+            n = want[s]
+            if ck.get(s, 0) >= n:
+                continue
+            eng[q].wait_ge(T.sem[s], n)
+            ck[s] = n
+            for s2, n2 in evclock.get((s, n), {}).items():
+                ck[s2] = max(ck.get(s2, 0), n2)
+
+    def note(outs, ins, ev):
+        for r in outs:
+            h = hist.setdefault(r[0], [])
+            if r[3] == 1:
+                h[:] = [e for e in h if not (e[0][1] >= r[1] and e[0][2] <= r[2])]
+            h.append((r, "w", ev))
+        for r in ins:
+            hist.setdefault(r[0], []).append((r, "r", ev))
+
+    def op(q, fn, outs, ins):
+        need(q, outs, ins)
+        count[q] += 1
+        s = "s" + q
+        fn(eng[q]).then_inc(T.sem[s], 1)
+        evclock[(s, count[q])] = dict(clock[q])
+        note(outs, ins, (s, count[q], q))
+
+    def dma(q, out, in_, outs, ins):
+        need(q, outs, ins)
+        s = "d%d" % len(used)
+        used.append(s)
+        eng[q].dma_start(out, in_).then_inc(T.sem[s], 16)
+        evclock[(s, 16)] = dict(clock[q])
+        note(outs, ins, (s, 16, s))
+
+    def sc(x):
+        return (x[0], [x[1]]) if isinstance(x, tuple) else (x, [])
+
+    def ts(o, i, s1, s2, op0, op1=None):
+        a, ra = sc(s1)
+        b, rb = sc(s2)
+        if op1 is None:
+            op(V, lambda e: e.tensor_scalar(o[0], i[0], a, None, op0), [o[1]], [i[1]] + ra)
+        else:
+            op(V, lambda e: e.tensor_scalar(o[0], i[0], a, b, op0, op1), [o[1]], [i[1]] + ra + rb)
+
+    def tt(o, i, j, o_):
+        op(V, lambda e: e.tensor_tensor(o[0], i[0], j[0], o_), [o[1]], [i[1], j[1]])
+
+    def scan(o, i, j, a, b):
+        op(V, lambda e: e.tensor_tensor_scan(o[0], i[0], j[0], 0.0, a, b), [o[1]], [i[1], j[1]])
+
+    def red(o, i, o_):
+        op(V, lambda e: e.tensor_reduce(o[0], i[0], AxisListType.X, o_), [o[1]], [i[1]])
+
+    def cp(o, i):
+        op(V, lambda e: e.tensor_copy(o[0], i[0]), [o[1]], [i[1]])
+
+    def ms(o, c):
+        op(V, lambda e: e.memset(o[0], c), [o[1]], [])
+
+    def act(o, i, f, scale=1.0, bias=None, acc=None):
+        if acc is not None:
+            op(S, lambda e: e.activation(o[0], i[0], f, accum_out=acc[0]), [o[1], acc[1]], [i[1]])
+        elif bias is None:
+            op(S, lambda e: e.activation(o[0], i[0], f, scale=scale), [o[1]], [i[1]])
+        else:
+            b, rb = sc(bias)
+            op(S, lambda e: e.activation(o[0], i[0], f, bias=b, scale=scale), [o[1]], [i[1]] + rb)
+
+    def pick(q, o, w, l, scale=1.0):
+        x = w[0].indirect(l[0])
+        if q == V:
+            op(V, lambda e: e.tensor_copy(o[0], x), [o[1]], [w[1], l[1]])
+        else:
+            op(S, lambda e: e.activation(o[0], x, ACT.Copy, scale=scale), [o[1]], [w[1], l[1]])
+
+    def picktt(o, w, l, j, o_):
+        x = w[0].indirect(l[0])
+        op(V, lambda e: e.tensor_tensor(o[0], x, j[0], o_), [o[1]], [w[1], l[1], j[1]])
+
+    def put(w, l, i):
+        x = w[0].indirect(l[0])
+        op(V, lambda e: e.tensor_copy(x, i[0]), [w[1]], [l[1], i[1]])
+
+    def quant(n, lo, hi, i):
+        o, s = A("q" + n, lo, hi), A("s" + n, lo, hi)
+        op(V, lambda e: e.quantize_mx(o[0], s[0], i[0]), [o[1], s[1]], [i[1]])
+
+    def mm(bank, n, ln, llo, rn, rlo, start=True, stop=True):
+        o = A("ps%d" % bank, 0, n)
+        l, ls = A("q" + ln, llo, llo + 128), A("s" + ln, llo, llo + 128)
+        r, rs = A("q" + rn, rlo, rlo + n), A("s" + rn, rlo, rlo + n)
+        ins = [l[1], ls[1], r[1], rs[1]]
+        op(PE, lambda e: e.matmul_mx(o[0], l[0], ls[0], r[0], rs[0], start, stop), [o[1]] if start else [], ins)
+        if not start:
+            note([o[1]], [], ("st", count[PE], PE))
+
+    def iota(o, pattern, base, cm):
+        op(G, lambda e: e.iota(o[0], pattern, base, cm, allow_small_or_imprecise_dtypes=True), [o[1]], [])
+
+    def asel(o, i, pattern, cmp, base, cm):
+        op(G, lambda e: e.affine_select(o[0], i[0], pattern, cmp, 0.0, base, cm), [o[1]], [i[1]])
+
+    def load(q, name, lo, hi, src):
+        a = A(name, lo, hi)
+        dma(q, a[0], src, [a[1]], [])
+
+    load(SY, "xw0", 0, 4 * C, T.x[:])
+    load(S, "ut", 0, 512, T.u[:])
+    load(SY, "xw0", 2048, 2048 + 4 * C, T.x[:])
+    wq = A("qw")
+    dma(SY, wq[0].bitcast(dt.uint8), T.wc[:], [wq[1]], [])
+    load(SY, "sw", 0, 512, T.ws[:])
+    load(SY, "vt", 0, 512, T.v[:])
+
+    icol = lambda k: A("icol", k, k + 1)
+    col = lambda k: A("cols", k, k + 1)
+    op(G, lambda e: e.iota(icol(0)[0], [[1, 1]], 0, 1), [icol(0)[1]], [])
+    iota(A("r16"), [[0, 24], [1, 16]], 0, 0)
+    op(G, lambda e: e.iota(A("ilist")[0], [[16, 8]], 4, 0), [A("ilist")[1]], [])
+    iota(A("ct"), [[-16, 24]], 368, 0)
+    iota(A("ki"), [[1, 4], [0, 6]], 0, 0)
+    iota(A("st"), [[0, 4], [16, 6]], -C, 0)
+    iota(A("koff"), [[DUMP, 4], [0, 6]], DUMP, 0)
+    iota(A("hm"), [[1, 2], [0, 16]], 0, 0)
+    iota(A("ij"), [[1, C]], 0, 0)
+    ms(A("eone"), 1.0)
+    asel(A("gt1"), A("eone", 0, 512), [[-16, 8], [0, 64]], ALU.is_ge, 0, 1)
+    asel(A("gt"), A("gt1"), [[16, 8], [0, 64]], ALU.is_ge, 15, -1)
+    iota(A("r4"), [[0, 96], [1, 4]], 0, 0)
+    asel(A("ebt"), A("eone"), [[1000, 4], [-1, 128], [-1000, 4]], ALU.is_equal, 0, 1)
+    iota(A("xw0", 3584, 4096), [[0, 512]], 0, 0)
+    iota(A("xw1", 1536, 2048), [[0, 512]], 0, 0)
+    iota(A("xw1", 3584, 4096), [[0, 512]], 0, 0)
+    iota(A("zt0", 384, 512), [[0, 128]], 0, 0)
+    iota(A("ht0", 384, 512), [[0, 128]], 0, 0)
+
+    ts(icol(1), icol(0), 15, None, ALU.bitwise_and)
+    ts(icol(2), icol(0), 3, None, ALU.bitwise_and)
+    ts(icol(3), icol(0), 2, 3, ALU.logical_shift_right, ALU.bitwise_and)
+    ts(icol(4), icol(0), 4, 1, ALU.logical_shift_right, ALU.bitwise_and)
+    cp(A("cols", 1, 5), A("icol", 1, 5))
+    ts(col(5), col(1), -1.0, None, ALU.mult)
+    ts(col(6), col(3), -1.0, None, ALU.mult)
+    act(A("nm1"), A("r16"), ACT.Abs, bias=col(5))
+    ts(A("rs1"), A("r16"), 0.5, -2 * BIG, ALU.is_gt, ALU.mult)
+    ts(A("rst16"), A("rs1"), BIG, None, ALU.add)
+    cp(A("ulist"), A("ilist"))
+    ts(A("nm2"), A("nm1"), 0.5, 2 * BIG, ALU.is_gt, ALU.mult)
+    ts(A("nm16"), A("nm2"), -BIG, None, ALU.add)
+    act(A("rz16"), A("r16"), ACT.Sign)
+    act(A("ioj"), A("ij"), ACT.Copy, scale=1.0 / 512)
+    act(A("srt0", C, POS), A("eone", 0, POS - C), ACT.Copy, scale=0.75)
+    quant("u", 0, 128, A("ut"))
+    ul = A("ulist")
+    qa, qb, sa, sb = A("qua"), A("qu"), A("sua"), A("su")
+    op(V, lambda e: e.tensor_copy(qa[0].bitcast(dt.uint32), qb[0].bitcast(dt.uint32).indirect(ul[0])), [qa[1]], [qb[1], ul[1]])
+    op(V, lambda e: e.tensor_copy(sa[0], sb[0].indirect(ul[0])), [sa[1]], [sb[1], ul[1]])
+    for i in range(6):
+        ms(A("mt%d" % i, 4 * (336 - 64 * i), 4 * MTN[i]), 0.0)
+    ms(A("rsum", 0, 1), 0.0)
+    ms(A("wsc", 0, 8), 0.0)
+    ms(A("xw0", 1536, 2048), 0.0)
+    ts(A("c24"), A("ct"), col(1), None, ALU.add)
+    ts(A("si"), A("st"), col(1), None, ALU.add)
+    ts(A("hm1"), A("hm"), col(4), 8.0 - 1.0e6, ALU.is_equal, ALU.mult)
+    ts(A("msk", 0, 32), A("hm1"), 1.0e6, None, ALU.add)
+    ms(A("msk", 32, 33), 8.0)
+    ts(A("rc", 1, 2), col(1), 3.5, 1.0e6, ALU.is_gt, ALU.mult)
+    ts(A("rc", 0, 1), A("rc", 1, 2), col(1), 8.0 * 54, ALU.add, ALU.add)
+
+    def scalar_constants():
+        act(A("n41"), A("r4"), ACT.Abs, bias=col(6))
+        act(A("n42"), A("n41"), ACT.Sign, bias=-0.5)
+        act(A("nm4"), A("n42"), ACT.Copy, scale=BIG)
+        act(A("rs4"), A("r4"), ACT.Sign, bias=-0.5)
+        act(A("rst4"), A("rs4"), ACT.Copy, scale=-BIG)
+        act(A("ni"), A("ij"), ACT.Identity, scale=1.0 / 512, bias=NB0 / 512.0)
+        act(A("ebth"), A("ebt"), ACT.Copy, scale=0.5)
+
+    cores = list(T.cores)
+    n = len(cores)
+    peers = [cores[(rank + k) % n] for k in range(1, n)]
+    E = topo.engines(core, peers[0])
+    quads = [E[0::4], E[2::4], E[1::4], E[3::4]]
+    order = sorted(peers, key=lambda c: topo.die(c) == topo.die(core))
+    codes_of = {order[0]: 0, order[1]: 1, order[2]: 2}
+    plane_of = {order[0]: 3, order[1]: 2, order[2]: 0}
+    bits = lambda k: sum(1 << e for e in quads[k])
+
+    def send(src, base, dst, back, rsem, lsem):
+        need(G, [], [A("q" + src)[1], A("s" + src)[1]])
+        for kind, table in (("q", codes_of), ("s", plane_of)):
+            tr = []
+            for k in range(1, n):
+                c = cores[(rank - k) % n] if back else cores[(rank + k) % n]
+                lo = base + P * (k - 1)
+                a = T[kind + src][:, lo:lo + P]
+                b = T[kind + dst][:, P * (k - 1):P * k]
+                if kind == "q":
+                    a, b = a.bitcast(dt.uint8), b.bitcast(dt.uint8)
+                rid, pid, _ = topo.addr(c)
+                tr.append(RemoteDMATransfer(dst_ids=[DstId(rid=rid, pnc=pid)], dma_engine_mask=bits(table[c]), remote_sem=T.sem[rsem], src=a, dst=b))
+            g.remote_dma_fused(tr, local_sem=T.sem[lsem])
+
+    def arrived(dst, sem):
+        note([A("q" + dst)[1], A("s" + dst)[1]], [], (sem, 8 * (n - 1), "far"))
+
+    ps = lambda b, m: A("ps%d" % b, 0, m)
+    slots = {}
+    for i, t in enumerate([None] + list(range(23, 0, -1))):
+        slots[t] = (i // 4, i % 4)
+    jk = [0]
+    for t in range(1, 24):
+        jk.append(jk[-1] + 16 * t)
+
+    def one_round(r):
+        xw, srt, last = "xw%d" % r, "srt%d" % r, r == 1
+        quant("x%d" % r, 0, C, A(xw, 0, 4 * C))
+        mm(0, C, "ua", 0, "x%d" % r, 0)
+        mm(1, C, "u", 0, "x%d" % r, 0)
+        tt(A("vm"), ps(0, C), A("nm16"), ALU.max)
+        act(A("rl"), ps(1, C), ACT.Relu)
+        act(A("fb"), A("rl"), ACT.Sign)
+        scan(A("zz"), A("rst16"), A("vm"), ALU.max, ALU.min)
+        tt(A("mt0", 0, 4 * C, 4), ps(0, C), A("zz"), ALU.is_gt)
+        for t in range(23, 0, -1):
+            i, f = slots[t]
+            w = 16 * t
+            m = A("mt%d" % i, f, 4 * w, 4)
+            ts(m, ps(0, w), A("zz", w + 15, w + 16), None, ALU.is_ge)
+            act(A("jk", jk[t - 1], jk[t - 1] + w), m, ACT.Copy, acc=A("rsum", t, t + 1))
+            if f == 3:
+                if r == 0 and i == 0:
+                    quant("g", 0, 128, A("gt"))
+                quant("m%d" % i, 0, MTN[i], A("mt%d" % i))
+                mm(2, MTN[i], "g", 0, "m%d" % i, 0, i == 0, i == 5)
+            if t == 12:
+                tt(A("fj"), A("fb"), A("ioj"), ALU.add)
+                scan(A("dg"), A("rz16"), A("mt0", 0, 4 * C, 4), ALU.mult, ALU.add)
+                tt(A("cd"), A("c24"), A("dg", 15, C, 16), ALU.add)
+        if r == 0:
+            scalar_constants()
+        tt(A("cx"), ps(2, C), A("nm16"), ALU.max)
+        scan(A("z2"), A("rst16"), A("cx"), ALU.max, ALU.min)
+        tt(A("pd"), A("cd"), A("z2", 15, C, 16), ALU.subtract)
+        tt(A("pf"), A("pd"), A("rsum"), ALU.add)
+        cp(A("pl"), A("pf"))
+        put(A(srt, 0, C), A("pl"), A("fj"))
+        ts(A("fs"), A(srt, 0, C), 1.0, 1.0, ALU.is_ge, ALU.add)
+        scan(A("wsc", 8, 8 + C), A("fs"), A("fs"), ALU.add, ALU.max)
+        tot = A("wsc", 7 + C, 8 + C)
+        thr, rem = tot, A("rc", 0, 1)
+        for m, (mult, lo, hi, nxt) in enumerate(((4.0, 54, 154, 119), (3.0, 119, 271, 207), (2.0, 207, 348, None))):
+            ts(A("cm", 0, hi - lo), A("wsc", 7 + lo, 7 + hi), mult, thr, ALU.mult, ALU.is_lt)
+            c, k = A("cnt", m, m + 1), A("kk", m, m + 1)
+            red(c, A("cm", 0, hi - lo), ALU.add)
+            ts(A("ky", 0, 33), A("msk", 0, 33), c, rem, ALU.mult, ALU.add)
+            kt, ky = A("kt"), A("ky", 0, 32)
+            op(V, lambda e: e.transpose(kt[0], ky[0]), [kt[1]], [ky[1]])
+            red(k, kt, ALU.min)
+            of = A("of", 2 * m, 2 * m + 1)
+            ts(of, k, 0.125, 7.0, ALU.mult, ALU.add)
+            if nxt is not None:
+                wa = A("wa", 16 * m, 16 * m + 16)
+                pick(V, wa, A("wsc", 0, 392), of)
+                ts(A("rm", m, m + 1), A("ky", 32, 33), k, 1.0e6, ALU.is_equal, ALU.mult)
+                ts(A("rr", m, m + 1), A("rm", m, m + 1), rem, 8.0 * (nxt - lo), ALU.add, ALU.add)
+                rem = A("rr", m, m + 1)
+                ts(A("th", m, m + 1), A("wa", 16 * m, 16 * m + 1), mult - 2.0, tot, ALU.mult, ALU.add)
+                thr = A("th", m, m + 1)
+        tmp = lambda k: A("tmp", 24 * k, 24 * k + 24)
+        c1 = lambda b, k: A(b, k, k + 1)
+        ts(A("aa", 0, 3), A("of", 0, 6, 2), -7.0, None, ALU.add)
+        ts(A("a8", 0, 3), A("aa", 0, 3), -8.0, None, ALU.mult)
+        ts(A("am", 0, 3), A("aa", 0, 3), -float(C), None, ALU.add)
+        tt(A("w3", 0, 3), A("a8", 0, 3), A("kk", 0, 3), ALU.add)
+        red(A("w4", 0, 1), A("w3", 0, 3), ALU.add)
+        ts(tmp(3), A("ki"), c1("w3", 1), c1("aa", 0), ALU.is_equal, ALU.mult)
+        ts(A("w4", 1, 2), A("w4", 0, 1), -1.0, 6.0, ALU.mult, ALU.add)
+        ts(tmp(4), A("ki"), c1("w3", 2), c1("aa", 1), ALU.is_equal, ALU.mult)
+        tt(tmp(7), A("si"), tmp(3), ALU.add)
+        ts(tmp(5), A("ki"), c1("w4", 1), c1("aa", 2), ALU.is_equal, ALU.mult)
+        ts(tmp(0), A("ki"), c1("w3", 0), c1("am", 0), ALU.is_equal, ALU.mult)
+        ts(tmp(1), A("ki"), c1("w3", 1), c1("am", 1), ALU.is_equal, ALU.mult)
+        tt(tmp(8), tmp(4), tmp(5), ALU.add)
+        ts(tmp(2), A("ki"), c1("w3", 2), c1("am", 2), ALU.is_equal, ALU.mult)
+        tt(tmp(6), tmp(0), tmp(1), ALU.add)
+        tt(tmp(10), tmp(7), tmp(8), ALU.add)
+        tt(tmp(9), tmp(6), tmp(2), ALU.add)
+        tt(tmp(11), tmp(10), tmp(9), ALU.is_ge)
+        tt(tmp(12), tmp(11), A("koff"), ALU.mult)
+        tt(tmp(13), tmp(10), tmp(12), ALU.add)
+        ts(A("pu"), tmp(13), float(C), None, ALU.add)
+        picktt(A("gm"), A(srt), A("pu"), A("nm4"), ALU.max)
+        scan(A("zs"), A("rst4"), A("gm"), ALU.max, ALU.min)
+        ts(A("l1"), A("zs", 3, C, 4), 2048.0, col(2), ALU.mult, ALU.add)
+        win = A(xw, 0, 3584)
+        pick(V, A("bt", 0, 768), win, A("l1", 0, 48))
+        pick(S, A("bt", 768, 1536), win, A("l1", 48, 96))
+        quant("b%d" % r, 0, C, A("bt"))
+        send("b%d" % r, P, "lb%d" % r, False, "ab%d" % r, "lb%d" % r)
+        arrived("lb%d" % r, "ab%d" % r)
+        if r == 0:
+            quant("eh", 0, 512, A("ebth"))
+        for b in range(4):
+            mm(4 + b, 128, "eh", 128 * b, "b%d" % r, 0)
+        tt(A("ge"), A(srt, 0, P), A("nm4", 0, P), ALU.max)
+        scan(A("ze"), A("rst4", 0, P), A("ge"), ALU.max, ALU.min)
+        ts(A("l3"), A("ze", 3, P, 4), 2048.0, col(2), ALU.mult, ALU.add)
+        pick(S, A("e3", 0, 384), win, A("l3"), scale=0.5)
+        act(A("e3", 384, 768), A("e3", 0, 384), ACT.Copy)
+        act(A("e3", 768, 1152), A("e3", 0, 384), ACT.Copy)
+        if r == 0:
+            quant("e1", 0, 512, A("ebt"))
+        for b in range(4):
+            tt(A("zt0", b, 384, 4), ps(4 + b, P), A("e3", b, 384, 4), ALU.add)
+        quant("z0", 0, 128, A("zt0"))
+        for b in range(4):
+            mm(b, 128, "w", 128 * b, "z0", 0)
+        for b in range(4):
+            act(A("ht0", b, 384, 4), ps(b, P), ACT.Copy, scale=0.03125)
+        put(A(srt), A("pu"), A("ni"))
+        for c in range(2):
+            for b in range(4):
+                mm(b + 4 - 4 * c, HALF, "eh", 128 * b, "lb%d" % r, HALF * c)
+        for c in range(2):
+            lo, hi = 4 * HALF * c, 4 * HALF * (c + 1)
+            for b in range(4):
+                tt(A("zt", lo + b, hi, 4), ps(b + 4 - 4 * c, HALF), A("e3", lo + b, hi, 4), ALU.add)
+            quant("z", HALF * c, HALF * (c + 1), A("zt", lo, hi))
+            for b in (0, 2, 1, 3):
+                mm(b + 4 - 4 * c, HALF, "w", 128 * b, "z", HALF * c)
+        for c in range(2):
+            lo, hi = 4 * HALF * c, 4 * HALF * (c + 1)
+            for b in range(2):
+                ts(A("ht", lo + b, hi, 4), ps(b + 4 - 4 * c, HALF), 0.03125, None, ALU.mult)
+            for b in range(2, 4):
+                act(A("ht", lo + b, hi, 4), ps(b + 4 - 4 * c, HALF), ACT.Copy, scale=0.03125)
+        quant("h%d" % r, 0, R3, A("ht"))
+        send("h%d" % r, 0, "lh%d" % r, True, "ah%d" % r, "lh%d" % r)
+        arrived("lh%d" % r, "ah%d" % r)
+        quant("h0k", 0, 128, A("ht0"))
+        for b in range(4):
+            mm(4 + b, 128, "e1", 128 * b, "h0k", 0)
+        picktt(A("gm2"), A(srt, 0, C), A("pl"), A("nm4"), ALU.max)
+        scan(A("zs2"), A("rst4"), A("gm2"), ALU.max, ALU.min)
+        ts(A("l2"), A("zs2", 3, C, 4), 2048.0, col(2), ALU.mult, ALU.add)
+        base = 4 * NB0
+        for b in range(4):
+            tt(A(xw, base + b, base + 384, 4), ps(4 + b, P), A("bt", b, 384, 4), ALU.add)
+        if last:
+            pick(S, A("slg"), A(srt, 0, C), A("pl"))
+            act(A("sl1"), A("slg"), ACT.Relu, scale=512.0, bias=1.0 - NB0)
+            act(A("sl2"), A("sl1"), ACT.Identity, bias=-1.0)
+            buf, at = HOME["sl2"]
+            dma(SY, T.sl[:], T[buf][0:128:16, at:at + C], [], [A("sl2")[1]])
+        else:
+            act(A("srt1", C, POS), A("eone", 0, POS - C), ACT.Copy, scale=0.75)
+            quant("v", 0, 128, A("vt"))
+        for b in range(4):
+            mm(4 + b, R3, "e1", 128 * b, "lh%d" % r, 0)
+        for b in range(4):
+            tt(A(xw, base + 384 + b, base + 1536, 4), ps(4 + b, R3), A("bt", 384 + b, 1536, 4), ALU.add)
+        xn = "xf" if last else "xw1"
+        full = A(xw, 0, 4 * XW)
+        pick(V, A(xn, 0, 768), full, A("l2", 0, 48))
+        pick(S, A(xn, 768, 1536), full, A("l2", 48, 96))
+        if not last:
+            a, b = A(xn, 2048, 2048 + 4 * C), A(xn, 0, 4 * C)
+            dma(SY, a[0], b[0], [a[1]], [b[1]])
+
+    one_round(0)
+    one_round(1)
+
+    h = C // 2
+    quant("xf", 0, C, A("xf"))
+    mm(3, h, "v", 0, "xf", 0)
+    mm(2, h, "v", 0, "xf", h)
+    qf = A("qxf")
+    dma(SY, T.oc[:], qf[0].bitcast(dt.uint8), [], [qf[1]])
+    for k in range(4):
+        dma(SY, T.osc[4 * k:4 * k + 4, :], T["sxf"][32 * k:32 * k + 4, :], [], [A("sxf")[1]])
+    y0, y1 = A("yt", 0, h), A("yt", h, C)
+    cp(y0, ps(3, h))
+    act(y1, ps(2, h), ACT.Copy)
+    dma(SY, T.y[:, 0:h], y0[0], [], [y0[1]])
+    dma(S, T.y[:, h:C], y1[0], [], [y1[1]])
+    for q in (V, S, PE, G):
+        g.sync.wait_ge(T.sem["s" + q], count[q])
+    for s in used:
+        g.sync.wait_ge(T.sem[s], 16)
+    for r in range(2):
+        g.wait_ge(T.sem["lb%d" % r], 8 * (n - 1))
+        g.wait_ge(T.sem["lh%d" % r], 8 * (n - 1))

@@ -4,11 +4,15 @@ from concourse.mybir import dt, AluOpType as ALU, AxisListType, ActivationFuncti
 C, P = 384, 96
 R3 = 3 * P
 HALF = R3 // 2
-BIG = 1.0e28
-DUMP = 480
-POS = DUMP * 5
-NB0 = 1024
+BIG = 2.0 ** 93
+NB0 = 400
 XW = NB0 + C
+EO = 336
+TOP = 2.0 ** 23
+D16, A16 = 1024.0, 14848.0
+D4, A4 = 8192.0, 20480.0
+CUTS = ((4.0 / 3.0, 230, 330), (1.5, 114, 264), (2.0, 38, 176))
+GONE = -4096.0
 
 SCRATCH = {}
 SEMAPHORES = ["sv", "ss", "st", "sp"]
@@ -27,43 +31,48 @@ def _q(name, n):
     _b("s" + name, n, "uint8")
 
 
-def _pack(buf, pieces):
+def _pack(buf, pieces, dtype="float32"):
     at = 0
     for name, n in pieces:
         WIDTH[name] = n
         HOME[name] = (buf, at)
-        at += -(-n // 8) * 8
-    SCRATCH[buf] = ("sbuf", [128, at], "float32")
+        at += -(-n // 16) * 16
+    SCRATCH[buf] = ("sbuf", [128, at], dtype)
 
 
 for _i in range(8):
     _b("ps%d" % _i, 512, "float32", "psum")
 for _r in range(2):
     _b("xw%d" % _r, 4 * XW, "bfloat16")
-    _b("srt%d" % _r, POS)
-    for _n, _w in (("x", C), ("b", C), ("lb", R3), ("h", R3), ("lh", R3)):
+    for _n, _w in (("x", C), ("b", C + 32), ("lb", R3), ("h", R3), ("lh", R3)):
         _q("%s%d" % (_n, _r), _w)
     SEMAPHORES += ["ab%d" % _r, "ah%d" % _r, "lb%d" % _r, "lh%d" % _r]
 _b("xf", 4 * C, "bfloat16")
-for _n, _w in (("xf", C), ("u", 128), ("ua", 128), ("v", 128), ("w", 512), ("e1", 512), ("eh", 512), ("g", 128), ("z0", 128), ("z", R3), ("h0k", 128)):
+for _n, _w in (("xf", C), ("u", 128), ("ua", 128), ("uc", 128), ("v", 128), ("w", 512), ("e1", 512), ("eh", 512), ("g", 128),
+               ("z0", 128), ("z", R3), ("h0k", 128)):
     _q(_n, _w)
-for _n, _w in (("ut", 512), ("vt", 512), ("eone", 2048), ("ebt", 2048), ("ebth", 2048), ("gt", 512), ("gt1", 512), ("bt", 4 * C),
-               ("e3", 4 * R3), ("zt0", 512), ("zt", 4 * R3), ("ht0", 512), ("ht", 4 * R3), ("jk", 4416), ("fs", C), ("fb", C), ("rz16", C), ("cm", 160)):
+for _n, _w in (("ut", 512), ("vt", 512), ("eone", 2048), ("ebt", 2048), ("ebth", 2048), ("gt", 512), ("bt", 4 * C + 128),
+               ("e3", 4 * R3), ("zt0", 512), ("zt", 4 * R3), ("ht0", 512), ("ht", 4 * R3), ("jk", 4416), ("sgn", 4416)):
     _b(_n, _w, "bfloat16")
 MTN = (384, 320, 256, 192, 128, 128)
 for _i in range(6):
     _b("mt%d" % _i, 4 * MTN[_i], "bfloat16")
     _q("m%d" % _i, MTN[_i])
-_b("wsc", 392)
 _b("yt", C)
-_pack("consts", [(_n, C) for _n in ("r16", "r4", "ij", "rs1", "nm1", "nm2", "rs4", "n41", "n42", "nm16", "rst16", "nm4", "rst4", "ioj", "ni")]
-      + [(_n, 24) for _n in ("c24", "ct", "ki", "si", "st", "koff")] + [("cols", 16), ("hm", 32), ("hm1", 32), ("msk", 40), ("rc", 8)])
-_pack("wide", [(_n, C) for _n in ("vm", "zz", "dg", "cx", "z2", "rl", "fj", "gm", "zs", "gm2", "zs2", "slg", "sl1", "sl2")] + [("ge", P), ("ze", P)])
-_pack("small", [(_n, 24) for _n in ("rsum", "cd", "pd", "pf")] + [("ky", 40), ("kt", 32), ("wa", 48), ("tmp", 24 * 16)]
-      + [(_n, 8) for _n in ("kk", "cnt", "th", "rm", "rr", "aa", "a8", "am", "w3", "w4")])
-for _n, _w in (("icol", 16), ("ilist", 8)):
-    _b(_n, _w, "int32")
-for _n, _w in (("ulist", 8), ("pl", 24), ("of", 8), ("pu", 24), ("l1", 96), ("l2", 96), ("l3", 24)):
+_b("srt", C)
+_b("tb", EO + C + 8)
+_b("t2", 2 * C)
+_pack("cb", [(_n, C) for _n in ("r16", "r4", "nm16", "rst", "rz16")] + [("g64", 512), ("rz8", 192)], "bfloat16")
+_pack("consts", [(_n, C) for _n in ("em16", "em4", "e4", "hh", "ij", "c15")] + [("id4", XW), ("slt", XW)]
+      + [(_n, 24) for _n in ("k24", "ct", "cs", "j24", "st", "j16")]
+      + [("cols", 16), ("krow", 32), ("kr", 16), ("c2", 8), ("crow", 4), ("il", 8), ("pe", 6)])
+_pack("wide", [(_n, C) for _n in ("vm", "zz", "d1", "ex", "fj", "g1", "x4", "g2", "x2", "sl2")]
+      + [("ge", P), ("ze", P), ("ff", 192), ("fs", 192)])
+_pack("wb", [("vsa", C), ("vsb", C), ("dg", C), ("cm", 160), ("cn", 160), ("kb", 16)], "bfloat16")
+_pack("small", [(_n, 24) for _n in ("rsum", "ce", "rf", "sx", "lf", "lg")] + [("pk", 32), ("krd", 32), ("sl", 32), ("c23", 2), ("cc", 8)]
+      + [("k", 32)])
+_b("icol", 16, "int32")
+for _n, _w in (("ula", 8), ("ulc", 8), ("pl", 24), ("of", 8), ("pos", 24), ("pose", 6), ("l1", 96), ("l2", 96), ("l3", 24), ("o2", 2), ("loc", 24)):
     _b(_n, _w, "uint16")
 NDMA = 24
 SEMAPHORES += ["d%d" % _i for _i in range(NDMA)]
@@ -143,13 +152,15 @@ def rank_program(g, core, T, topo):
     def sc(x):
         return (x[0], [x[1]]) if isinstance(x, tuple) else (x, [])
 
-    def ts(o, i, s1, s2, op0, op1=None):
+    def ts(o, i, s1, s2, op0, op1=None, by=None):
         a, ra = sc(s1)
         b, rb = sc(s2)
+        x = i[0] if by is None else i[0].indirect(by[0])
+        ins = [i[1]] + ra + rb + ([] if by is None else [by[1]])
         if op1 is None:
-            op(V, lambda e: e.tensor_scalar(o[0], i[0], a, None, op0), [o[1]], [i[1]] + ra)
+            op(V, lambda e: e.tensor_scalar(o[0], x, a, None, op0), [o[1]], ins)
         else:
-            op(V, lambda e: e.tensor_scalar(o[0], i[0], a, b, op0, op1), [o[1]], [i[1]] + ra + rb)
+            op(V, lambda e: e.tensor_scalar(o[0], x, a, b, op0, op1), [o[1]], ins)
 
     def tt(o, i, j, o_):
         op(V, lambda e: e.tensor_tensor(o[0], i[0], j[0], o_), [o[1]], [i[1], j[1]])
@@ -167,18 +178,21 @@ def rank_program(g, core, T, topo):
         op(V, lambda e: e.memset(o[0], c), [o[1]], [])
 
     def act(o, i, f, scale=1.0, bias=None, acc=None):
+        kw, outs, ins = {"scale": scale}, [o[1]], [i[1]]
+        if bias is not None:
+            kw["bias"], rb = sc(bias)
+            ins = ins + rb
         if acc is not None:
-            op(S, lambda e: e.activation(o[0], i[0], f, accum_out=acc[0]), [o[1], acc[1]], [i[1]])
-        elif bias is None:
-            op(S, lambda e: e.activation(o[0], i[0], f, scale=scale), [o[1]], [i[1]])
-        else:
-            b, rb = sc(bias)
-            op(S, lambda e: e.activation(o[0], i[0], f, bias=b, scale=scale), [o[1]], [i[1]] + rb)
+            kw["accum_out"] = acc[0]
+            outs = outs + [acc[1]]
+        op(S, lambda e: e.activation(o[0], i[0], f, **kw), outs, ins)
 
     def pick(q, o, w, l, scale=1.0):
         x = w[0].indirect(l[0])
         if q == V:
             op(V, lambda e: e.tensor_copy(o[0], x), [o[1]], [w[1], l[1]])
+        elif scale == 1.0:
+            op(S, lambda e: e.activation(o[0], x, ACT.Copy), [o[1]], [w[1], l[1]])
         else:
             op(S, lambda e: e.activation(o[0], x, ACT.Copy, scale=scale), [o[1]], [w[1], l[1]])
 
@@ -213,9 +227,9 @@ def rank_program(g, core, T, topo):
         a = A(name, lo, hi)
         dma(q, a[0], src, [a[1]], [])
 
-    load(SY, "xw0", 0, 4 * C, T.x[:])
     load(S, "ut", 0, 512, T.u[:])
-    load(SY, "xw0", 2048, 2048 + 4 * C, T.x[:])
+    load(SY, "xw0", 0, 4 * C, T.x[:])
+    need(SY, [], [A("xw0", 0, 4 * C)[1]])
     wq = A("qw")
     dma(SY, wq[0].bitcast(dt.uint8), T.wc[:], [wq[1]], [])
     load(SY, "sw", 0, 512, T.ws[:])
@@ -223,68 +237,86 @@ def rank_program(g, core, T, topo):
 
     icol = lambda k: A("icol", k, k + 1)
     col = lambda k: A("cols", k, k + 1)
+    Q16, Q4, R4, PG, CA, KC, CL1, CL2 = 1, 2, 3, 4, 5, 6, 7, 8
     op(G, lambda e: e.iota(icol(0)[0], [[1, 1]], 0, 1), [icol(0)[1]], [])
+    iota(A("il"), [[16, 8]], 0, 0)
     iota(A("r16"), [[0, 24], [1, 16]], 0, 0)
-    op(G, lambda e: e.iota(A("ilist")[0], [[16, 8]], 4, 0), [A("ilist")[1]], [])
-    iota(A("ct"), [[-16, 24]], 368, 0)
-    iota(A("ki"), [[1, 4], [0, 6]], 0, 0)
-    iota(A("st"), [[0, 4], [16, 6]], -C, 0)
-    iota(A("koff"), [[DUMP, 4], [0, 6]], DUMP, 0)
-    iota(A("hm"), [[1, 2], [0, 16]], 0, 0)
+    iota(A("g64"), [[1, 8], [0, 64]], 0, 0)
     iota(A("ij"), [[1, C]], 0, 0)
-    ms(A("eone"), 1.0)
-    asel(A("gt1"), A("eone", 0, 512), [[-16, 8], [0, 64]], ALU.is_ge, 0, 1)
-    asel(A("gt"), A("gt1"), [[16, 8], [0, 64]], ALU.is_ge, 15, -1)
+    iota(A("ct"), [[-16, 24]], 368, 0)
+    iota(A("tb", EO, EO + C + 1), [[2, C + 1]], 0, 0)
+    iota(A("kr"), [[0, 4], [-1, 4]], 3, 0)
+    iota(A("c2", 0, 2), [[EO, 2]], CUTS[0][1] - 1, 0)
+    iota(A("c2", 2, 4), [[EO, 2]], CUTS[1][1] - 1, 0)
+    iota(A("c2", 4, 6), [[0, 2]], EO + CUTS[2][1] - 1, 0)
+    iota(A("st"), [[-8, 24]], -1, 0)
     iota(A("r4"), [[0, 96], [1, 4]], 0, 0)
+    iota(A("t2", 0, 2 * C, 2), [[0, C]], int(TOP) + 4 * C, 0)
+    iota(A("c15"), [[0, C]], 3, 0)
+    iota(A("bt", 4 * C, 4 * C + 128), [[0, 128]], 0, 0)
+    iota(A("xw0", 4 * C, 4 * NB0), [[0, 64]], 0, 0)
+    iota(A("eone"), [[0, 2048]], 1, 0)
     asel(A("ebt"), A("eone"), [[1000, 4], [-1, 128], [-1000, 4]], ALU.is_equal, 0, 1)
-    iota(A("xw0", 3584, 4096), [[0, 512]], 0, 0)
-    iota(A("xw1", 1536, 2048), [[0, 512]], 0, 0)
-    iota(A("xw1", 3584, 4096), [[0, 512]], 0, 0)
+    iota(A("pe"), [[-32, 6]], 2 * C - 1, 0)
     iota(A("zt0", 384, 512), [[0, 128]], 0, 0)
     iota(A("ht0", 384, 512), [[0, 128]], 0, 0)
+    iota(A("xw1", 4 * C, 4 * NB0), [[0, 64]], 0, 0)
+    iota(A("j16"), [[16, 24]], 0, 0)
+    iota(A("crow", 0, 1), [[0, 1]], NB0 + R3 - 1, 0)
+    iota(A("crow", 1, 4), [[P, 3]], NB0 - 1, 0)
+    iota(A("rz8"), [[0, 24], [1, 8]], 0, 0)
+    iota(A("id4"), [[4, XW]], 0, 0)
 
-    ts(icol(1), icol(0), 15, None, ALU.bitwise_and)
-    ts(icol(2), icol(0), 3, None, ALU.bitwise_and)
-    ts(icol(3), icol(0), 2, 3, ALU.logical_shift_right, ALU.bitwise_and)
-    ts(icol(4), icol(0), 4, 1, ALU.logical_shift_right, ALU.bitwise_and)
+    ts(icol(Q16), icol(0), 15, None, ALU.bitwise_and)
+    ts(icol(Q4), icol(0), 3, None, ALU.bitwise_and)
+    ts(icol(R4), icol(0), 2, 3, ALU.logical_shift_right, ALU.bitwise_and)
+    ts(icol(PG), icol(0), 4, None, ALU.logical_shift_right)
     cp(A("cols", 1, 5), A("icol", 1, 5))
-    ts(col(5), col(1), -1.0, None, ALU.mult)
-    ts(col(6), col(3), -1.0, None, ALU.mult)
-    act(A("nm1"), A("r16"), ACT.Abs, bias=col(5))
-    ts(A("rs1"), A("r16"), 0.5, -2 * BIG, ALU.is_gt, ALU.mult)
-    ts(A("rst16"), A("rs1"), BIG, None, ALU.add)
-    cp(A("ulist"), A("ilist"))
-    ts(A("nm2"), A("nm1"), 0.5, 2 * BIG, ALU.is_gt, ALU.mult)
-    ts(A("nm16"), A("nm2"), -BIG, None, ALU.add)
-    act(A("rz16"), A("r16"), ACT.Sign)
-    act(A("ioj"), A("ij"), ACT.Copy, scale=1.0 / 512)
-    act(A("srt0", C, POS), A("eone", 0, POS - C), ACT.Copy, scale=0.75)
-    quant("u", 0, 128, A("ut"))
-    ul = A("ulist")
-    qa, qb, sa, sb = A("qua"), A("qu"), A("sua"), A("su")
-    op(V, lambda e: e.tensor_copy(qa[0].bitcast(dt.uint32), qb[0].bitcast(dt.uint32).indirect(ul[0])), [qa[1]], [qb[1], ul[1]])
-    op(V, lambda e: e.tensor_copy(sa[0], sb[0].indirect(ul[0])), [sa[1]], [sb[1], ul[1]])
-    for i in range(6):
+    ts(A("ula"), A("il"), 4.0, None, ALU.add)
+    ts(A("ulc"), A("il"), col(Q4), None, ALU.add)
+    for i in (0, 2, 3, 4, 5, 1):
         ms(A("mt%d" % i, 4 * (336 - 64 * i), 4 * MTN[i]), 0.0)
     ms(A("rsum", 0, 1), 0.0)
-    ms(A("wsc", 0, 8), 0.0)
-    ms(A("xw0", 1536, 2048), 0.0)
-    ts(A("c24"), A("ct"), col(1), None, ALU.add)
-    ts(A("si"), A("st"), col(1), None, ALU.add)
-    ts(A("hm1"), A("hm"), col(4), 8.0 - 1.0e6, ALU.is_equal, ALU.mult)
-    ts(A("msk", 0, 32), A("hm1"), 1.0e6, None, ALU.add)
-    ms(A("msk", 32, 33), 8.0)
-    ts(A("rc", 1, 2), col(1), 3.5, 1.0e6, ALU.is_gt, ALU.mult)
-    ts(A("rc", 0, 1), A("rc", 1, 2), col(1), 8.0 * 54, ALU.add, ALU.add)
+    ms(A("tb", 0, 1), 0.0)
+    ms(A("krow", 0, 16), 1.0 / 6.0)
+    ts(col(CA), col(Q16), D16, A16 - 15 * D16, ALU.mult, ALU.add)
+    ts(col(KC), col(Q4), -0.125, 0.375, ALU.mult, ALU.add)
+    ts(A("nm16"), A("r16"), col(Q16), -BIG, ALU.not_equal, ALU.mult)
+    ts(A("rst"), A("r16"), 0.0, -2 * BIG, ALU.is_equal, ALU.mult)
+    quant("u", 0, 128, A("ut"))
+    for n in ("a", "c"):
+        ul, qa, qb = A("ul" + n), A("qu" + n), A("qu")
+        op(V, lambda e: e.tensor_copy(qa[0].bitcast(dt.uint32), qb[0].bitcast(dt.uint32).indirect(ul[0])), [qa[1]], [qb[1], ul[1]])
+        pick(S, A("su" + n), A("su"), ul)
+    act(A("rz16"), A("r16"), ACT.Sign)
+    act(A("em16"), A("nm16"), ACT.Identity, scale=(A16 + D16) / BIG, bias=A16)
+    act(A("d1"), A("nm16"), ACT.Identity, scale=(A16 + D16) / BIG, bias=A16)
+    ts(A("gt"), A("g64"), col(PG), None, ALU.is_equal)
+    quant("g", 0, 128, A("gt"))
 
-    def scalar_constants():
-        act(A("n41"), A("r4"), ACT.Abs, bias=col(6))
-        act(A("n42"), A("n41"), ACT.Sign, bias=-0.5)
-        act(A("nm4"), A("n42"), ACT.Copy, scale=BIG)
-        act(A("rs4"), A("r4"), ACT.Sign, bias=-0.5)
-        act(A("rst4"), A("rs4"), ACT.Copy, scale=-BIG)
-        act(A("ni"), A("ij"), ACT.Identity, scale=1.0 / 512, bias=NB0 / 512.0)
-        act(A("ebth"), A("ebt"), ACT.Copy, scale=0.5)
+    def late_constants(k):
+        if k == 0:
+            ts(A("k24"), A("ct"), col(Q16), -1.0, ALU.add, ALU.mult)
+            tt(A("k24"), A("k24"), A("em16", 15, C, 16), ALU.add)
+            ts(A("krow", 16, 32), A("kr"), 0.125, None, ALU.mult)
+            ts(col(9), col(R4), -2.0, None, ALU.mult)
+            ts(A("cs"), A("st"), col(9), None, ALU.add)
+            ts(col(10), col(R4), -D4, 3 * D4 - A4, ALU.mult, ALU.add)
+            ts(col(CL2), col(10), col(Q4), None, ALU.add)
+            ts(col(CL1), col(CL2), -TOP, None, ALU.add)
+            ts(A("e4"), A("r4"), col(R4), A4 + D4, ALU.is_equal, ALU.mult)
+        if k == 1:
+            act(A("c15"), A("c15"), ACT.Copy, scale=0.5)
+            act(A("em4"), A("e4"), ACT.Identity, bias=-D4)
+        if k == 2:
+            act(A("ebth"), A("ebt"), ACT.Copy, scale=0.5)
+            act(A("rz8"), A("rz8"), ACT.Sign)
+        if k == 3:
+            ts(col(11), col(Q16), -2.0, None, ALU.mult)
+            ts(A("pose"), A("pe"), col(11), None, ALU.add)
+            ts(A("j24"), A("j16"), col(Q16), None, ALU.add)
+
+    act(A("hh"), A("ij"), ACT.Identity, scale=2.0 ** -22, bias=0.5)
 
     cores = list(T.cores)
     n = len(cores)
@@ -292,18 +324,18 @@ def rank_program(g, core, T, topo):
     E = topo.engines(core, peers[0])
     quads = [E[0::4], E[2::4], E[1::4], E[3::4]]
     order = sorted(peers, key=lambda c: topo.die(c) == topo.die(core))
-    codes_of = {order[0]: 0, order[1]: 1, order[2]: 2}
-    plane_of = {order[0]: 3, order[1]: 2, order[2]: 0}
-    bits = lambda k: sum(1 << e for e in quads[k])
+    codes_of = {order[0]: (0,), order[1]: (1,), order[2]: (2, 3)}
+    plane_of = {order[0]: (2,), order[1]: (3,), order[2]: (0, 1)}
+    bits = lambda ks: sum(1 << e for k in ks for e in quads[k])
+    NARR = 32
 
-    def send(src, base, dst, back, rsem, lsem):
-        need(G, [], [A("q" + src)[1], A("s" + src)[1]])
+    def send(src, dst, back, rsem, lsem):
+        need(G, [], [A("q" + src, 0, R3)[1], A("s" + src, 0, R3)[1]])
         for kind, table in (("q", codes_of), ("s", plane_of)):
             tr = []
             for k in range(1, n):
                 c = cores[(rank - k) % n] if back else cores[(rank + k) % n]
-                lo = base + P * (k - 1)
-                a = T[kind + src][:, lo:lo + P]
+                a = T[kind + src][:, P * (k - 1):P * k]
                 b = T[kind + dst][:, P * (k - 1):P * k]
                 if kind == "q":
                     a, b = a.bitcast(dt.uint8), b.bitcast(dt.uint8)
@@ -312,7 +344,7 @@ def rank_program(g, core, T, topo):
             g.remote_dma_fused(tr, local_sem=T.sem[lsem])
 
     def arrived(dst, sem):
-        note([A("q" + dst)[1], A("s" + dst)[1]], [], (sem, 8 * (n - 1), "far"))
+        note([A("q" + dst)[1], A("s" + dst)[1]], [], (sem, NARR, "far"))
 
     ps = lambda b, m: A("ps%d" % b, 0, m)
     slots = {}
@@ -321,183 +353,230 @@ def rank_program(g, core, T, topo):
     jk = [0]
     for t in range(1, 24):
         jk.append(jk[-1] + 16 * t)
+    K = lambda i: A("kb", i, i + 1) if i in (9, 10) else A("k", i, i + 1)
+    ACC, TH, M1, M2, M3, OWN1, OWN2, OWN3, OWNB, B2, B3, EN1, EN2, S1, S2, S12, E12, DD, ZZ, EN3, STF, LW, ENF = range(23)
+    SB = (19, 18, 17)
+    VX = 52
+    VB = 38
 
     def one_round(r):
-        xw, srt, last = "xw%d" % r, "srt%d" % r, r == 1
-        quant("x%d" % r, 0, C, A(xw, 0, 4 * C))
-        mm(0, C, "ua", 0, "x%d" % r, 0)
-        mm(1, C, "u", 0, "x%d" % r, 0)
-        tt(A("vm"), ps(0, C), A("nm16"), ALU.max)
-        act(A("rl"), ps(1, C), ACT.Relu)
-        act(A("fb"), A("rl"), ACT.Sign)
-        scan(A("zz"), A("rst16"), A("vm"), ALU.max, ALU.min)
-        tt(A("mt0", 0, 4 * C, 4), ps(0, C), A("zz"), ALU.is_gt)
-        for t in range(23, 0, -1):
-            i, f = slots[t]
-            w = 16 * t
-            m = A("mt%d" % i, f, 4 * w, 4)
-            ts(m, ps(0, w), A("zz", w + 15, w + 16), None, ALU.is_ge)
-            act(A("jk", jk[t - 1], jk[t - 1] + w), m, ACT.Copy, acc=A("rsum", t, t + 1))
-            if f == 3:
-                if r == 0 and i == 0:
-                    quant("g", 0, 128, A("gt"))
-                quant("m%d" % i, 0, MTN[i], A("mt%d" % i))
-                mm(2, MTN[i], "g", 0, "m%d" % i, 0, i == 0, i == 5)
-            if t == 12:
-                tt(A("fj"), A("fb"), A("ioj"), ALU.add)
-                scan(A("dg"), A("rz16"), A("mt0", 0, 4 * C, 4), ALU.mult, ALU.add)
-                tt(A("cd"), A("c24"), A("dg", 15, C, 16), ALU.add)
+        xw, last = "xw%d" % r, r == 1
+        xq = "x%d" % r
         if r == 0:
-            scalar_constants()
-        tt(A("cx"), ps(2, C), A("nm16"), ALU.max)
-        scan(A("z2"), A("rst16"), A("cx"), ALU.max, ALU.min)
-        tt(A("pd"), A("cd"), A("z2", 15, C, 16), ALU.subtract)
-        tt(A("pf"), A("pd"), A("rsum"), ALU.add)
-        cp(A("pl"), A("pf"))
-        put(A(srt, 0, C), A("pl"), A("fj"))
-        ts(A("fs"), A(srt, 0, C), 1.0, 1.0, ALU.is_ge, ALU.add)
-        scan(A("wsc", 8, 8 + C), A("fs"), A("fs"), ALU.add, ALU.max)
-        tot = A("wsc", 7 + C, 8 + C)
-        thr, rem = tot, A("rc", 0, 1)
-        for m, (mult, lo, hi, nxt) in enumerate(((4.0, 54, 154, 119), (3.0, 119, 271, 207), (2.0, 207, 348, None))):
-            ts(A("cm", 0, hi - lo), A("wsc", 7 + lo, 7 + hi), mult, thr, ALU.mult, ALU.is_lt)
-            c, k = A("cnt", m, m + 1), A("kk", m, m + 1)
-            red(c, A("cm", 0, hi - lo), ALU.add)
-            ts(A("ky", 0, 33), A("msk", 0, 33), c, rem, ALU.mult, ALU.add)
-            kt, ky = A("kt"), A("ky", 0, 32)
-            op(V, lambda e: e.transpose(kt[0], ky[0]), [kt[1]], [ky[1]])
-            red(k, kt, ALU.min)
-            of = A("of", 2 * m, 2 * m + 1)
-            ts(of, k, 0.125, 7.0, ALU.mult, ALU.add)
-            if nxt is not None:
-                wa = A("wa", 16 * m, 16 * m + 16)
-                pick(V, wa, A("wsc", 0, 392), of)
-                ts(A("rm", m, m + 1), A("ky", 32, 33), k, 1.0e6, ALU.is_equal, ALU.mult)
-                ts(A("rr", m, m + 1), A("rm", m, m + 1), rem, 8.0 * (nxt - lo), ALU.add, ALU.add)
-                rem = A("rr", m, m + 1)
-                ts(A("th", m, m + 1), A("wa", 16 * m, 16 * m + 1), mult - 2.0, tot, ALU.mult, ALU.add)
-                thr = A("th", m, m + 1)
-        tmp = lambda k: A("tmp", 24 * k, 24 * k + 24)
-        c1 = lambda b, k: A(b, k, k + 1)
-        ts(A("aa", 0, 3), A("of", 0, 6, 2), -7.0, None, ALU.add)
-        ts(A("a8", 0, 3), A("aa", 0, 3), -8.0, None, ALU.mult)
-        ts(A("am", 0, 3), A("aa", 0, 3), -float(C), None, ALU.add)
-        tt(A("w3", 0, 3), A("a8", 0, 3), A("kk", 0, 3), ALU.add)
-        red(A("w4", 0, 1), A("w3", 0, 3), ALU.add)
-        ts(tmp(3), A("ki"), c1("w3", 1), c1("aa", 0), ALU.is_equal, ALU.mult)
-        ts(A("w4", 1, 2), A("w4", 0, 1), -1.0, 6.0, ALU.mult, ALU.add)
-        ts(tmp(4), A("ki"), c1("w3", 2), c1("aa", 1), ALU.is_equal, ALU.mult)
-        tt(tmp(7), A("si"), tmp(3), ALU.add)
-        ts(tmp(5), A("ki"), c1("w4", 1), c1("aa", 2), ALU.is_equal, ALU.mult)
-        ts(tmp(0), A("ki"), c1("w3", 0), c1("am", 0), ALU.is_equal, ALU.mult)
-        ts(tmp(1), A("ki"), c1("w3", 1), c1("am", 1), ALU.is_equal, ALU.mult)
-        tt(tmp(8), tmp(4), tmp(5), ALU.add)
-        ts(tmp(2), A("ki"), c1("w3", 2), c1("am", 2), ALU.is_equal, ALU.mult)
-        tt(tmp(6), tmp(0), tmp(1), ALU.add)
-        tt(tmp(10), tmp(7), tmp(8), ALU.add)
-        tt(tmp(9), tmp(6), tmp(2), ALU.add)
-        tt(tmp(11), tmp(10), tmp(9), ALU.is_ge)
-        tt(tmp(12), tmp(11), A("koff"), ALU.mult)
-        tt(tmp(13), tmp(10), tmp(12), ALU.add)
-        ts(A("pu"), tmp(13), float(C), None, ALU.add)
-        picktt(A("gm"), A(srt), A("pu"), A("nm4"), ALU.max)
-        scan(A("zs"), A("rst4"), A("gm"), ALU.max, ALU.min)
-        ts(A("l1"), A("zs", 3, C, 4), 2048.0, col(2), ALU.mult, ALU.add)
-        win = A(xw, 0, 3584)
-        pick(V, A("bt", 0, 768), win, A("l1", 0, 48))
-        pick(S, A("bt", 768, 1536), win, A("l1", 48, 96))
-        quant("b%d" % r, 0, C, A("bt"))
-        send("b%d" % r, P, "lb%d" % r, False, "ab%d" % r, "lb%d" % r)
+            quant(xq, 0, C, A(xw, 0, 4 * C))
+        mm(0, C, "ua", 0, xq, 0)
+        mm(2, C, "uc", 0, xq, 0)
+        mm(1, C, "ua", 0, xq, 0)
+        tt(A("vm"), ps(0, C), A("nm16"), ALU.add)
+        act(A("vsa"), ps(2, C), ACT.Sign)
+        act(A("vsb"), A("vsa"), ACT.Sign, bias=-0.5, acc=K(ACC))
+        scan(A("zz"), A("rst"), A("vm"), ALU.add, ALU.max)
+        own = lambda t: A("zz", 16 * t + 15, 16 * t + 16)
+        row = lambda t: A("mt%d" % slots[t][0], slots[t][1], 64 * t, 4)
+        tmp = lambda t: A("sgn", jk[t - 1], jk[t - 1] + 16 * t)
+        for t in SB:
+            act(tmp(t), ps(1, 16 * t), ACT.Sign, scale=-1.0, bias=own(t))
+        for t in SB:
+            act(row(t), tmp(t), ACT.Relu, acc=A("rsum", t, t + 1))
+        act(K(TH), K(ACC), ACT.Identity, scale=0.5, bias=1.5 * C + 1.0 / 6.0)
+        tt(A("mt0", 0, 4 * C, 4), ps(0, C), A("zz"), ALU.is_le)
+        for t in range(23, 0, -1):
+            if t in SB:
+                continue
+            i, f = slots[t]
+            ts(row(t), ps(0, 16 * t), own(t), None, ALU.is_lt)
+            act(A("jk", jk[t - 1], jk[t - 1] + 16 * t), row(t), ACT.Copy, acc=A("rsum", t, t + 1))
+            if f == 3:
+                quant("m%d" % i, 0, MTN[i], A("mt%d" % i))
+                mm(3, MTN[i], "g", 0, "m%d" % i, 0, i == 0, i == 5)
+                if i == 0 and r == 0:
+                    late_constants(0)
+                if i == 3:
+                    quant("m1", 0, MTN[1], A("mt1"))
+                    mm(3, MTN[1], "g", 0, "m1", 0, False, False)
+        scan(A("dg"), A("rz16"), A("mt0", 0, 4 * C, 4), ALU.mult, ALU.add)
+        scan(A("fj"), A("hh"), A("vsb"), ALU.max, ALU.mult)
+        tt(A("ce"), A("k24"), A("dg", 15, C, 16), ALU.subtract)
+        tt(A("d1", 15, C, 16), A("ce"), A("rsum"), ALU.subtract)
+        if r == 0:
+            late_constants(1)
+        scan(A("ex"), ps(3, C), A("d1"), ALU.max, ALU.add)
+        ts(A("pl"), A("ex", 15, C, 16), -1.0, col(CA), ALU.mult, ALU.add)
+        put(A("srt"), A("pl"), A("fj"))
+        top = CUTS[0][2]
+        scan(A("tb", 1, top), A("srt", 0, top - 1), A("c15", 0, top - 1), ALU.add, ALU.add)
+        act(A("t2", 1, 2 * C, 2), A("srt"), ACT.Abs, scale=2.0 ** 24)
+        if r == 0:
+            late_constants(2)
+        tb = A("tb", 0, EO + C + 1)
+
+        def eq(o, a, b, c):
+            ts(K(o), K(a), K(b), c, ALU.is_equal, ALU.mult)
+
+        for m, (mult, lo, hi) in enumerate(CUTS):
+            w = hi - lo
+            ts(A("cm", 0, w), A("tb", lo, hi), mult, K(TH), ALU.mult, ALU.is_le)
+            if m == 1:
+                eq(B2, OWN1, M1, GONE)
+                eq(EN1, OWN1, M1, K(M1))
+            if m == 2:
+                eq(B3, OWN2, M2, GONE)
+                ts(A("krd", 0, 16), A("krow", 16, 32), K(M2), None, ALU.subtract)
+            scan(A("cn", 0, w), A("cm", 0, w), A("cm", 0, w), ALU.add, ALU.max)
+            cnt, of = A("cn", w - 1, w), A("of", 2 * m, 2 * m + 2)
+            if m == 0:
+                ts(of, A("c2", 0, 2), cnt, None, ALU.add)
+                if r == 0:
+                    cp(A("krd", 16, 32), A("krow", 16, 32))
+            elif m == 1:
+                ts(of, A("c2", 2, 4), cnt, K(B2), ALU.add, ALU.add)
+                ts(A("c23"), A("c2", 4, 6), K(B2), None, ALU.add)
+            else:
+                ts(of, A("c23"), cnt, K(B3), ALU.add, ALU.add)
+                eq(EN2, OWN2, M2, K(M2))
+            picktt(A("pk"), tb, of, A("krow") if m < 2 else A("krd"), ALU.add)
+            if m < 2:
+                ts(K(OWN1 + m), A("of", 2 * m, 2 * m + 1), 2.0, col(KC), ALU.mult, ALU.add)
+                red(K(TH), A("pk", 0, 16), ALU.max)
+                red(K(M1 + m), A("pk", 16, 32), ALU.max)
+            if m == 1:
+                eq(S1, OWN1, M1, 2.0 * C)
+        ts(K(OWN3), A("of", 4, 5), -float(EO), 2.0, ALU.add, ALU.mult)
+        eq(S2, OWN2, M2, K(M1))
+        red(K(M3), A("pk", 16, 32), ALU.max)
+        ts(K(OWN3), K(OWN3), col(KC), None, ALU.add)
+        red(K(DD), A("pk", 0, 16), ALU.max)
+        ts(K(S12), K(S1), K(S2), K(M2), ALU.max, ALU.max)
+        ts(K(OWNB), K(OWN3), K(B2), K(B3), ALU.subtract, ALU.subtract)
+        ts(K(E12), K(EN1), K(EN2), None, ALU.max)
+        eq(EN3, OWN3, M3, K(M3))
+        ts(K(ZZ), K(OWNB), K(M3), K(DD), ALU.is_lt, ALU.mult)
+        ts(A("sx"), A("cs"), K(S12), K(E12), ALU.add, ALU.max)
+        ts(A("pos"), A("sx"), K(ZZ), K(EN3), ALU.add, ALU.max)
+        pick(V, A("g1", 0, 224), A("t2"), A("pos", 0, 14))
+        pick(S, A("g1", 224, C), A("t2"), A("pos", 14, 24))
+        for k in (1, 2, 3):
+            scan(A("x4", P * (k - 1), P * k), A("g1", k, C, 4), A("em4", 0, P), ALU.max, ALU.add)
+        ts(A("l1", 0, 72), A("x4", 3, R3, 4), col(CL1), None, ALU.add)
+        win = A(xw, 0, 4 * NB0)
+        pick(V, A("bt", 0, 16 * VB), win, A("l1", 0, VB))
+        pick(S, A("bt", 16 * VB, 4 * R3), win, A("l1", VB, 72))
+        bq = "b%d" % r
+        quant(bq, 0, R3, A("bt", 0, 4 * R3))
+        send(bq, "lb%d" % r, False, "ab%d" % r, "lb%d" % r)
         arrived("lb%d" % r, "ab%d" % r)
         if r == 0:
-            quant("eh", 0, 512, A("ebth"))
-        for b in range(4):
-            mm(4 + b, 128, "eh", 128 * b, "b%d" % r, 0)
-        tt(A("ge"), A(srt, 0, P), A("nm4", 0, P), ALU.max)
-        scan(A("ze"), A("rst4", 0, P), A("ge"), ALU.max, ALU.min)
-        ts(A("l3"), A("ze", 3, P, 4), 2048.0, col(2), ALU.mult, ALU.add)
+            late_constants(3)
+        pick(S, A("ge"), A("t2"), A("pose"))
+        scan(A("x4", R3, C), A("g1", 0, C, 4), A("em4", 0, P), ALU.max, ALU.add)
+        ts(A("l1", 72, 96), A("x4", R3 + 3, C, 4), col(CL1), None, ALU.add)
+        scan(A("ze"), A("ge"), A("em4", 0, P), ALU.max, ALU.add)
+        ts(A("l3"), A("ze", 3, P, 4), col(CL1), None, ALU.add)
+        pick(V, A("bt", 4 * R3, 4 * C), win, A("l1", 72, 96))
         pick(S, A("e3", 0, 384), win, A("l3"), scale=0.5)
         act(A("e3", 384, 768), A("e3", 0, 384), ACT.Copy)
         act(A("e3", 768, 1152), A("e3", 0, 384), ACT.Copy)
+        quant(bq, R3, R3 + 128, A("bt", 4 * R3, 4 * R3 + 512))
         if r == 0:
-            quant("e1", 0, 512, A("ebt"))
+            quant("eh", 0, 512, A("ebth"))
         for b in range(4):
-            tt(A("zt0", b, 384, 4), ps(4 + b, P), A("e3", b, 384, 4), ALU.add)
+            mm(b, 128, "eh", 128 * b, bq, R3)
+        ts(K(STF), K(S12), K(ZZ), None, ALU.add)
+        ts(K(ENF), K(E12), K(EN3), None, ALU.max)
+        ts(A("rf"), A("ex", 15, C, 16), -1.0, col(CA), ALU.mult, ALU.add)
+        ts(K(LW), K(STF), -2.0 * P, K(ENF), ALU.add, ALU.max)
+        ts(A("o2"), A("k", STF, STF + 2), 0.5, float(EO), ALU.mult, ALU.add)
+        for b in range(4):
+            tt(A("zt0", b, 384, 4), ps(b, P), A("e3", b, 384, 4), ALU.add)
         quant("z0", 0, 128, A("zt0"))
         for b in range(4):
             mm(b, 128, "w", 128 * b, "z0", 0)
         for b in range(4):
             act(A("ht0", b, 384, 4), ps(b, P), ACT.Copy, scale=0.03125)
-        put(A(srt), A("pu"), A("ni"))
+        ts(A("sl"), tb, 0.5, None, ALU.mult, by=A("o2"))
+        tt(A("cc", 0, 4), A("sl", 0, 4), A("crow"), ALU.add)
+        ts(A("cc", 4, 8), A("cc", 0, 4), -1.0, None, ALU.mult)
+        for k in range(4):
+            ts(A("ff", k, 192, 8), A("rf"), A("sl", 16 + k, 17 + k), A("cc", k, k + 1), ALU.is_ge, ALU.mult)
+        for k in range(4):
+            ts(A("ff", 4 + k, 192, 8), A("rf"), A("sl", k, k + 1), A("cc", 4 + k, 5 + k), ALU.is_ge, ALU.mult)
+        scan(A("fs"), A("rz8"), A("ff"), ALU.mult, ALU.add)
+        tt(A("lf"), A("fs", 7, 192, 8), A("rf"), ALU.subtract)
+        tt(A("lg"), A("lf"), A("j24"), ALU.max)
+        cp(A("loc"), A("lg"))
+        lb, hq = "lb%d" % r, "h%d" % r
         for c in range(2):
             for b in range(4):
-                mm(b + 4 - 4 * c, HALF, "eh", 128 * b, "lb%d" % r, HALF * c)
+                mm(b + 4 - 4 * c, HALF, "eh", 128 * b, lb, HALF * c)
         for c in range(2):
             lo, hi = 4 * HALF * c, 4 * HALF * (c + 1)
             for b in range(4):
                 tt(A("zt", lo + b, hi, 4), ps(b + 4 - 4 * c, HALF), A("e3", lo + b, hi, 4), ALU.add)
             quant("z", HALF * c, HALF * (c + 1), A("zt", lo, hi))
-            for b in (0, 2, 1, 3):
+            for b in range(4):
                 mm(b + 4 - 4 * c, HALF, "w", 128 * b, "z", HALF * c)
-        for c in range(2):
-            lo, hi = 4 * HALF * c, 4 * HALF * (c + 1)
-            for b in range(2):
-                ts(A("ht", lo + b, hi, 4), ps(b + 4 - 4 * c, HALF), 0.03125, None, ALU.mult)
-            for b in range(2, 4):
-                act(A("ht", lo + b, hi, 4), ps(b + 4 - 4 * c, HALF), ACT.Copy, scale=0.03125)
-        quant("h%d" % r, 0, R3, A("ht"))
-        send("h%d" % r, 0, "lh%d" % r, True, "ah%d" % r, "lh%d" % r)
-        arrived("lh%d" % r, "ah%d" % r)
-        quant("h0k", 0, 128, A("ht0"))
         for b in range(4):
-            mm(4 + b, 128, "e1", 128 * b, "h0k", 0)
-        picktt(A("gm2"), A(srt, 0, C), A("pl"), A("nm4"), ALU.max)
-        scan(A("zs2"), A("rst4"), A("gm2"), ALU.max, ALU.min)
-        ts(A("l2"), A("zs2", 3, C, 4), 2048.0, col(2), ALU.mult, ALU.add)
+            act(A("ht", b, 4 * HALF, 4), ps(b + 4, HALF), ACT.Copy, scale=0.03125)
+        quant(hq, 0, HALF, A("ht", 0, 4 * HALF))
+        for b in range(4):
+            o = A("ht", 4 * HALF + b, 4 * R3, 4)
+            if b % 2:
+                ts(o, ps(b, HALF), 0.03125, None, ALU.mult)
+            else:
+                act(o, ps(b, HALF), ACT.Copy, scale=0.03125)
+        quant(hq, HALF, R3, A("ht", 4 * HALF, 4 * R3))
+        send(hq, "lh%d" % r, True, "ah%d" % r, "lh%d" % r)
+        arrived("lh%d" % r, "ah%d" % r)
+        pick(S, A("g2"), A("id4"), A("loc"))
+        quant("h0k", 0, 128, A("ht0"))
+        if r == 0:
+            quant("e1", 0, 512, A("ebt"))
+        for b in range(4):
+            mm(b, 128, "e1", 128 * b, "h0k", 0)
+        scan(A("x2"), A("g2"), A("em4"), ALU.max, ALU.add)
+        ts(A("l2"), A("x2", 3, C, 4), col(CL2), None, ALU.add)
         base = 4 * NB0
         for b in range(4):
-            tt(A(xw, base + b, base + 384, 4), ps(4 + b, P), A("bt", b, 384, 4), ALU.add)
+            tt(A(xw, base + 4 * R3 + b, base + 4 * C, 4), ps(b, P), A("bt", 4 * R3 + b, 4 * C, 4), ALU.add)
         if last:
-            pick(S, A("slg"), A(srt, 0, C), A("pl"))
-            act(A("sl1"), A("slg"), ACT.Relu, scale=512.0, bias=1.0 - NB0)
-            act(A("sl2"), A("sl1"), ACT.Identity, bias=-1.0)
+            pick(S, A("sl2"), A("slt"), A("loc"))
             buf, at = HOME["sl2"]
             dma(SY, T.sl[:], T[buf][0:128:16, at:at + C], [], [A("sl2")[1]])
         else:
-            act(A("srt1", C, POS), A("eone", 0, POS - C), ACT.Copy, scale=0.75)
             quant("v", 0, 128, A("vt"))
+            iota(A("slt", 0, NB0), [[0, NB0]], -1, 0)
+            iota(A("slt", NB0, NB0 + R3), [[1, R3]], P, 0)
+            iota(A("slt", NB0 + R3, XW), [[1, P]], 0, 0)
         for b in range(4):
             mm(4 + b, R3, "e1", 128 * b, "lh%d" % r, 0)
         for b in range(4):
-            tt(A(xw, base + 384 + b, base + 1536, 4), ps(4 + b, R3), A("bt", 384 + b, 1536, 4), ALU.add)
-        xn = "xf" if last else "xw1"
+            tt(A(xw, base + b, base + 4 * R3, 4), ps(4 + b, R3), A("bt", b, 4 * R3, 4), ALU.add)
+        xn, xq = ("xf", "xf") if last else ("xw1", "x1")
         full = A(xw, 0, 4 * XW)
-        pick(V, A(xn, 0, 768), full, A("l2", 0, 48))
-        pick(S, A(xn, 768, 1536), full, A("l2", 48, 96))
-        if not last:
-            a, b = A(xn, 2048, 2048 + 4 * C), A(xn, 0, 4 * C)
-            dma(SY, a[0], b[0], [a[1]], [b[1]])
+        pick(V, A(xn, 0, 16 * VX), full, A("l2", 0, VX))
+        pick(S, A(xn, 16 * VX, 4 * C), full, A("l2", VX, 96))
+        quant(xq, 0, 4 * VX, A(xn, 0, 16 * VX))
+        quant(xq, 4 * VX, C, A(xn, 16 * VX, 4 * C))
 
     one_round(0)
     one_round(1)
 
-    h = C // 2
-    quant("xf", 0, C, A("xf"))
+    h = 4 * VX
     mm(3, h, "v", 0, "xf", 0)
-    mm(2, h, "v", 0, "xf", h)
+    mm(2, C - h, "v", 0, "xf", h)
     qf = A("qxf")
     dma(SY, T.oc[:], qf[0].bitcast(dt.uint8), [], [qf[1]])
-    for k in range(4):
-        dma(SY, T.osc[4 * k:4 * k + 4, :], T["sxf"][32 * k:32 * k + 4, :], [], [A("sxf")[1]])
     y0, y1 = A("yt", 0, h), A("yt", h, C)
-    cp(y0, ps(3, h))
-    act(y1, ps(2, h), ACT.Copy)
-    dma(SY, T.y[:, 0:h], y0[0], [], [y0[1]])
-    dma(S, T.y[:, h:C], y1[0], [], [y1[1]])
+    act(y0, ps(3, h), ACT.Copy)
+    cp(y1, ps(2, C - h))
+    dma(S, T.y[:, 0:h], y0[0], [], [y0[1]])
+    for k in range(4):
+        dma(SY if k < 2 else S, T.osc[4 * k:4 * k + 4, :], T["sxf"][32 * k:32 * k + 4, :], [], [A("sxf")[1]])
+    dma(SY, T.y[:, h:C], y1[0], [], [y1[1]])
     for q in (V, S, PE, G):
         g.sync.wait_ge(T.sem["s" + q], count[q])
     for s in used:
         g.sync.wait_ge(T.sem[s], 16)
     for r in range(2):
-        g.wait_ge(T.sem["lb%d" % r], 8 * (n - 1))
-        g.wait_ge(T.sem["lh%d" % r], 8 * (n - 1))
+        g.wait_ge(T.sem["lb%d" % r], NARR)
+        g.wait_ge(T.sem["lh%d" % r], NARR)

@@ -13,6 +13,15 @@ D16, A16 = 1024.0, 14848.0
 D4, A4 = 8192.0, 20480.0
 CUTS = ((4.0 / 3.0, 230, 330), (1.5, 114, 264), (2.0, 38, 176))
 GONE = -4096.0
+STAGES = ((1, 2), (3,))
+STAGE = []
+_to = _lo = 0
+for _ks in STAGES:
+    _w = P * len(_ks)
+    STAGE.append((_ks, _w, max(_w, 128), _to, _lo, 32 if _w < 128 and _lo else 0))
+    _to += max(_w, 128)
+    _lo += _w + (0 if _lo else 128)
+TW, LWD = _to, _lo
 
 SCRATCH = {}
 SEMAPHORES = ["sv", "ss", "st", "sp"]
@@ -44,15 +53,15 @@ for _i in range(8):
     _b("ps%d" % _i, 512, "float32", "psum")
 for _r in range(2):
     _b("xw%d" % _r, 4 * XW, "bfloat16")
-    for _n, _w in (("x", C), ("b", C + 32), ("lb", R3), ("h", R3), ("lh", R3)):
+    for _n, _w in (("x", C), ("b", TW + 128), ("lb", LWD), ("h", TW), ("lh", LWD)):
         _q("%s%d" % (_n, _r), _w)
-    SEMAPHORES += ["ab%d" % _r, "ah%d" % _r, "lb%d" % _r, "lh%d" % _r]
+    SEMAPHORES += ["lb%d" % _r, "lh%d" % _r] + ["a%s%d_%d" % (_n, _r, _s) for _n in "bh" for _s in range(len(STAGES))]
 _b("xf", 4 * C, "bfloat16")
 for _n, _w in (("xf", C), ("u", 128), ("ua", 128), ("uc", 128), ("v", 128), ("w", 512), ("e1", 512), ("eh", 512), ("g", 128),
-               ("z0", 128), ("z", R3), ("h0k", 128)):
+               ("z0", 128), ("z", TW), ("h0k", 128)):
     _q(_n, _w)
-for _n, _w in (("ut", 512), ("vt", 512), ("eone", 2048), ("ebt", 2048), ("ebth", 2048), ("gt", 512), ("bt", 4 * C + 128),
-               ("e3", 4 * R3), ("zt0", 512), ("zt", 4 * R3), ("ht0", 512), ("ht", 4 * R3), ("jk", 4416), ("sgn", 4416)):
+for _n, _w in (("ut", 512), ("vt", 512), ("eone", 516), ("ebt", 516), ("ebth", 516), ("gt", 512), ("bt", 4 * TW + 512),
+               ("e3", 8 * P), ("zt0", 512), ("zt", 4 * TW), ("ht0", 512), ("ht", 4 * TW), ("jk", 4416), ("sgn", 4416), ("nil", 512)):
     _b(_n, _w, "bfloat16")
 MTN = (384, 320, 256, 192, 128, 128)
 for _i in range(6):
@@ -62,8 +71,8 @@ _b("yt", C)
 _b("srt", C)
 _b("tb", EO + C + 8)
 _b("t2", 2 * C)
-_pack("cb", [(_n, C) for _n in ("r16", "r4", "nm16", "rst", "rz16")] + [("g64", 512), ("rz8", 192)], "bfloat16")
-_pack("consts", [(_n, C) for _n in ("em16", "em4", "e4", "hh", "ij", "c15")] + [("id4", XW), ("slt", XW)]
+_pack("cb", [(_n, C) for _n in ("r16", "r4", "nm16", "rst", "rz16", "e4")] + [("g64", 512), ("rz8", 192)], "bfloat16")
+_pack("consts", [(_n, C) for _n in ("em16", "em4", "hh", "ij", "c15")] + [("id4", XW), ("slt", XW)]
       + [(_n, 24) for _n in ("k24", "ct", "cs", "j24", "st", "j16")]
       + [("cols", 16), ("krow", 32), ("kr", 16), ("c2", 8), ("crow", 4), ("il", 8), ("pe", 6)])
 _pack("wide", [(_n, C) for _n in ("vm", "zz", "d1", "ex", "fj", "g1", "x4", "g2", "x2", "sl2")]
@@ -238,33 +247,35 @@ def rank_program(g, core, T, topo):
     icol = lambda k: A("icol", k, k + 1)
     col = lambda k: A("cols", k, k + 1)
     Q16, Q4, R4, PG, CA, KC, CL1, CL2 = 1, 2, 3, 4, 5, 6, 7, 8
+    ms(A("eone"), 0.5)
     op(G, lambda e: e.iota(icol(0)[0], [[1, 1]], 0, 1), [icol(0)[1]], [])
     iota(A("il"), [[16, 8]], 0, 0)
     iota(A("r16"), [[0, 24], [1, 16]], 0, 0)
-    iota(A("g64"), [[1, 8], [0, 64]], 0, 0)
-    iota(A("ij"), [[1, C]], 0, 0)
-    iota(A("ct"), [[-16, 24]], 368, 0)
-    iota(A("tb", EO, EO + C + 1), [[2, C + 1]], 0, 0)
+    iota(A("j16"), [[16, 24]], 0, 0)
     iota(A("kr"), [[0, 4], [-1, 4]], 3, 0)
+    iota(A("g64"), [[1, 8], [0, 64]], 0, 0)
+    iota(A("r4"), [[0, 96], [1, 4]], 0, 0)
+    iota(A("ij"), [[1, C]], 0, 0)
+    iota(A("tb", EO, EO + C + 1), [[2, C + 1]], 0, 0)
     iota(A("c2", 0, 2), [[EO, 2]], CUTS[0][1] - 1, 0)
     iota(A("c2", 2, 4), [[EO, 2]], CUTS[1][1] - 1, 0)
     iota(A("c2", 4, 6), [[0, 2]], EO + CUTS[2][1] - 1, 0)
-    iota(A("st"), [[-8, 24]], -1, 0)
-    iota(A("r4"), [[0, 96], [1, 4]], 0, 0)
-    iota(A("t2", 0, 2 * C, 2), [[0, C]], int(TOP) + 4 * C, 0)
     iota(A("c15"), [[0, C]], 3, 0)
-    iota(A("bt", 4 * C, 4 * C + 128), [[0, 128]], 0, 0)
+    iota(A("rz8"), [[0, 24], [1, 8]], 0, 0)
+    iota(A("t2", 0, 2 * C, 2), [[0, C]], int(TOP) + 4 * C, 0)
     iota(A("xw0", 4 * C, 4 * NB0), [[0, 64]], 0, 0)
-    iota(A("eone"), [[0, 2048]], 1, 0)
-    asel(A("ebt"), A("eone"), [[1000, 4], [-1, 128], [-1000, 4]], ALU.is_equal, 0, 1)
-    iota(A("pe"), [[-32, 6]], 2 * C - 1, 0)
+    asel(A("ebth"), A("eone"), [[1, 516]], ALU.is_equal, -3, -4)
+    for ks, w, ww, to, lo, io in STAGE:
+        if w < ww:
+            for t_ in ("bt", "zt", "ht"):
+                iota(A(t_, 4 * (to + w), 4 * (to + ww)), [[0, 4 * (ww - w)]], 0, 0)
+    iota(A("bt", 4 * (TW + P), 4 * (TW + 128)), [[0, 128]], 0, 0)
+    iota(A("nil"), [[0, 512]], 0, 0)
     iota(A("zt0", 384, 512), [[0, 128]], 0, 0)
     iota(A("ht0", 384, 512), [[0, 128]], 0, 0)
     iota(A("xw1", 4 * C, 4 * NB0), [[0, 64]], 0, 0)
-    iota(A("j16"), [[16, 24]], 0, 0)
     iota(A("crow", 0, 1), [[0, 1]], NB0 + R3 - 1, 0)
     iota(A("crow", 1, 4), [[P, 3]], NB0 - 1, 0)
-    iota(A("rz8"), [[0, 24], [1, 8]], 0, 0)
     iota(A("id4"), [[4, XW]], 0, 0)
 
     ts(icol(Q16), icol(0), 15, None, ALU.bitwise_and)
@@ -292,29 +303,27 @@ def rank_program(g, core, T, topo):
     act(A("em16"), A("nm16"), ACT.Identity, scale=(A16 + D16) / BIG, bias=A16)
     act(A("d1"), A("nm16"), ACT.Identity, scale=(A16 + D16) / BIG, bias=A16)
     ts(A("gt"), A("g64"), col(PG), None, ALU.is_equal)
+    ts(col(9), col(R4), -2.0, -1.0, ALU.mult, ALU.add)
+    ts(col(10), col(R4), -D4, 3 * D4 - A4, ALU.mult, ALU.add)
+    ts(col(11), col(Q16), -1.0, -368.0, ALU.mult, ALU.add)
+    ts(A("j24"), A("j16"), col(Q16), None, ALU.add)
     quant("g", 0, 128, A("gt"))
+    ts(A("ct"), A("j16"), col(11), None, ALU.add)
+    ts(A("cs"), A("j16"), -0.5, col(9), ALU.mult, ALU.add)
+    ts(col(CL2), col(10), col(Q4), None, ALU.add)
+    ts(A("pose"), A("j24", 0, 6), -2.0, 2.0 * C - 1.0, ALU.mult, ALU.add)
+    ts(A("krow", 16, 32), A("kr"), 0.125, None, ALU.mult)
+    ts(col(CL1), col(CL2), -TOP, None, ALU.add)
 
     def late_constants(k):
         if k == 0:
-            ts(A("k24"), A("ct"), col(Q16), -1.0, ALU.add, ALU.mult)
-            tt(A("k24"), A("k24"), A("em16", 15, C, 16), ALU.add)
-            ts(A("krow", 16, 32), A("kr"), 0.125, None, ALU.mult)
-            ts(col(9), col(R4), -2.0, None, ALU.mult)
-            ts(A("cs"), A("st"), col(9), None, ALU.add)
-            ts(col(10), col(R4), -D4, 3 * D4 - A4, ALU.mult, ALU.add)
-            ts(col(CL2), col(10), col(Q4), None, ALU.add)
-            ts(col(CL1), col(CL2), -TOP, None, ALU.add)
-            ts(A("e4"), A("r4"), col(R4), A4 + D4, ALU.is_equal, ALU.mult)
+            ts(A("e4"), A("r4"), col(R4), None, ALU.is_equal)
+            tt(A("k24"), A("ct"), A("em16", 15, C, 16), ALU.add)
+            cp(A("krd", 16, 32), A("krow", 16, 32))
         if k == 1:
             act(A("c15"), A("c15"), ACT.Copy, scale=0.5)
-            act(A("em4"), A("e4"), ACT.Identity, bias=-D4)
-        if k == 2:
-            act(A("ebth"), A("ebt"), ACT.Copy, scale=0.5)
+            act(A("em4"), A("e4"), ACT.Identity, scale=A4 + D4, bias=-D4)
             act(A("rz8"), A("rz8"), ACT.Sign)
-        if k == 3:
-            ts(col(11), col(Q16), -2.0, None, ALU.mult)
-            ts(A("pose"), A("pe"), col(11), None, ALU.add)
-            ts(A("j24"), A("j16"), col(Q16), None, ALU.add)
 
     act(A("hh"), A("ij"), ACT.Identity, scale=2.0 ** -22, bias=0.5)
 
@@ -322,29 +331,24 @@ def rank_program(g, core, T, topo):
     n = len(cores)
     peers = [cores[(rank + k) % n] for k in range(1, n)]
     E = topo.engines(core, peers[0])
-    quads = [E[0::4], E[2::4], E[1::4], E[3::4]]
-    order = sorted(peers, key=lambda c: topo.die(c) == topo.die(core))
-    codes_of = {order[0]: (0,), order[1]: (1,), order[2]: (2, 3)}
-    plane_of = {order[0]: (2,), order[1]: (3,), order[2]: (0, 1)}
-    bits = lambda ks: sum(1 << e for k in ks for e in quads[k])
-    NARR = 32
+    NARR = 2 * len(E)
 
-    def send(src, dst, back, rsem, lsem):
-        need(G, [], [A("q" + src, 0, R3)[1], A("s" + src, 0, R3)[1]])
-        for kind, table in (("q", codes_of), ("s", plane_of)):
+    def send(src, dst, s, back, sem):
+        ks, w, ww, to, lo, io = STAGE[s]
+        need(G, [], [A("q" + src, to, to + w)[1], A("s" + src, to, to + w)[1]])
+        for kind in "qs":
             tr = []
-            for k in range(1, n):
+            for i, k in enumerate(ks):
                 c = cores[(rank - k) % n] if back else cores[(rank + k) % n]
-                a = T[kind + src][:, P * (k - 1):P * k]
-                b = T[kind + dst][:, P * (k - 1):P * k]
+                a = T[kind + src][:, to + P * i:to + P * (i + 1)]
+                b = T[kind + dst][:, lo + P * i:lo + P * (i + 1)]
                 if kind == "q":
                     a, b = a.bitcast(dt.uint8), b.bitcast(dt.uint8)
                 rid, pid, _ = topo.addr(c)
-                tr.append(RemoteDMATransfer(dst_ids=[DstId(rid=rid, pnc=pid)], dma_engine_mask=bits(table[c]), remote_sem=T.sem[rsem], src=a, dst=b))
-            g.remote_dma_fused(tr, local_sem=T.sem[lsem])
-
-    def arrived(dst, sem):
-        note([A("q" + dst)[1], A("s" + dst)[1]], [], (sem, NARR, "far"))
+                mask = sum(1 << e for e in E[i::len(ks)])
+                tr.append(RemoteDMATransfer(dst_ids=[DstId(rid=rid, pnc=pid)], dma_engine_mask=mask, remote_sem=T.sem["a%s_%d" % (sem, s)], src=a, dst=b))
+            g.remote_dma_fused(tr, local_sem=T.sem["l" + sem])
+        note([A("q" + dst, lo, lo + w)[1], A("s" + dst, lo, lo + w)[1]], [], ("a%s_%d" % (sem, s), NARR, "far"))
 
     ps = lambda b, m: A("ps%d" % b, 0, m)
     slots = {}
@@ -356,8 +360,11 @@ def rank_program(g, core, T, topo):
     K = lambda i: A("kb", i, i + 1) if i in (9, 10) else A("k", i, i + 1)
     ACC, TH, M1, M2, M3, OWN1, OWN2, OWN3, OWNB, B2, B3, EN1, EN2, S1, S2, S12, E12, DD, ZZ, EN3, STF, LW, ENF = range(23)
     SB = (19, 18, 17)
+    RV = 7
     VX = 52
-    VB = 38
+    VB = (26, 14)
+    H0V, H1V = (3,), (1, 3)
+    OWNQ = S
 
     def one_round(r):
         xw, last = "xw%d" % r, r == 1
@@ -367,6 +374,8 @@ def rank_program(g, core, T, topo):
         mm(0, C, "ua", 0, xq, 0)
         mm(2, C, "uc", 0, xq, 0)
         mm(1, C, "ua", 0, xq, 0)
+        if r == 0:
+            late_constants(0)
         tt(A("vm"), ps(0, C), A("nm16"), ALU.add)
         act(A("vsa"), ps(2, C), ACT.Sign)
         act(A("vsb"), A("vsa"), ACT.Sign, bias=-0.5, acc=K(ACC))
@@ -379,22 +388,31 @@ def rank_program(g, core, T, topo):
         for t in SB:
             act(row(t), tmp(t), ACT.Relu, acc=A("rsum", t, t + 1))
         act(K(TH), K(ACC), ACT.Identity, scale=0.5, bias=1.5 * C + 1.0 / 6.0)
-        tt(A("mt0", 0, 4 * C, 4), ps(0, C), A("zz"), ALU.is_le)
+        def sums(i):
+            quant("m%d" % i, 0, MTN[i], A("mt%d" % i))
+            mm(3, MTN[i], "g", 0, "m%d" % i, 0, i == 0, i == 5)
+
+        done = None
         for t in range(23, 0, -1):
             if t in SB:
                 continue
             i, f = slots[t]
             ts(row(t), ps(0, 16 * t), own(t), None, ALU.is_lt)
-            act(A("jk", jk[t - 1], jk[t - 1] + 16 * t), row(t), ACT.Copy, acc=A("rsum", t, t + 1))
+            if t > RV:
+                act(A("jk", jk[t - 1], jk[t - 1] + 16 * t), row(t), ACT.Copy, acc=A("rsum", t, t + 1))
+            if t == 22:
+                tt(A("mt0", 0, 4 * C, 4), ps(0, C), A("zz"), ALU.is_le)
+            if done is not None:
+                sums(done)
+                done = None
             if f == 3:
-                quant("m%d" % i, 0, MTN[i], A("mt%d" % i))
-                mm(3, MTN[i], "g", 0, "m%d" % i, 0, i == 0, i == 5)
-                if i == 0 and r == 0:
-                    late_constants(0)
-                if i == 3:
-                    quant("m1", 0, MTN[1], A("mt1"))
-                    mm(3, MTN[1], "g", 0, "m1", 0, False, False)
+                done = i
+            if t == 9:
+                sums(1)
         scan(A("dg"), A("rz16"), A("mt0", 0, 4 * C, 4), ALU.mult, ALU.add)
+        sums(5)
+        for t in range(RV, 0, -1):
+            red(A("rsum", t, t + 1), row(t), ALU.add)
         scan(A("fj"), A("hh"), A("vsb"), ALU.max, ALU.mult)
         tt(A("ce"), A("k24"), A("dg", 15, C, 16), ALU.subtract)
         tt(A("d1", 15, C, 16), A("ce"), A("rsum"), ALU.subtract)
@@ -406,9 +424,9 @@ def rank_program(g, core, T, topo):
         top = CUTS[0][2]
         scan(A("tb", 1, top), A("srt", 0, top - 1), A("c15", 0, top - 1), ALU.add, ALU.add)
         act(A("t2", 1, 2 * C, 2), A("srt"), ACT.Abs, scale=2.0 ** 24)
-        if r == 0:
-            late_constants(2)
+        pick(S, A("ge"), A("t2"), A("pose"))
         tb = A("tb", 0, EO + C + 1)
+        win = A(xw, 0, 4 * NB0)
 
         def eq(o, a, b, c):
             ts(K(o), K(a), K(b), c, ALU.is_equal, ALU.mult)
@@ -426,8 +444,6 @@ def rank_program(g, core, T, topo):
             cnt, of = A("cn", w - 1, w), A("of", 2 * m, 2 * m + 2)
             if m == 0:
                 ts(of, A("c2", 0, 2), cnt, None, ALU.add)
-                if r == 0:
-                    cp(A("krd", 16, 32), A("krow", 16, 32))
             elif m == 1:
                 ts(of, A("c2", 2, 4), cnt, K(B2), ALU.add, ALU.add)
                 ts(A("c23"), A("c2", 4, 6), K(B2), None, ALU.add)
@@ -439,8 +455,13 @@ def rank_program(g, core, T, topo):
                 ts(K(OWN1 + m), A("of", 2 * m, 2 * m + 1), 2.0, col(KC), ALU.mult, ALU.add)
                 red(K(TH), A("pk", 0, 16), ALU.max)
                 red(K(M1 + m), A("pk", 16, 32), ALU.max)
+            if m == 0:
+                scan(A("ze"), A("ge"), A("em4", 0, P), ALU.max, ALU.add)
             if m == 1:
                 eq(S1, OWN1, M1, 2.0 * C)
+                ts(A("l3"), A("ze", 3, P, 4), col(CL1), None, ALU.add)
+                pick(S, A("e3", 0, 384), win, A("l3"), scale=0.5)
+                act(A("e3", 384, 768), A("e3", 0, 384), ACT.Copy)
         ts(K(OWN3), A("of", 4, 5), -float(EO), 2.0, ALU.add, ALU.mult)
         eq(S2, OWN2, M2, K(M1))
         red(K(M3), A("pk", 16, 32), ALU.max)
@@ -455,89 +476,126 @@ def rank_program(g, core, T, topo):
         ts(A("pos"), A("sx"), K(ZZ), K(EN3), ALU.add, ALU.max)
         pick(V, A("g1", 0, 224), A("t2"), A("pos", 0, 14))
         pick(S, A("g1", 224, C), A("t2"), A("pos", 14, 24))
-        for k in (1, 2, 3):
-            scan(A("x4", P * (k - 1), P * k), A("g1", k, C, 4), A("em4", 0, P), ALU.max, ALU.add)
-        ts(A("l1", 0, 72), A("x4", 3, R3, 4), col(CL1), None, ALU.add)
-        win = A(xw, 0, 4 * NB0)
-        pick(V, A("bt", 0, 16 * VB), win, A("l1", 0, VB))
-        pick(S, A("bt", 16 * VB, 4 * R3), win, A("l1", VB, 72))
-        bq = "b%d" % r
-        quant(bq, 0, R3, A("bt", 0, 4 * R3))
-        send(bq, "lb%d" % r, False, "ab%d" % r, "lb%d" % r)
-        arrived("lb%d" % r, "ab%d" % r)
-        if r == 0:
-            late_constants(3)
-        pick(S, A("ge"), A("t2"), A("pose"))
+        bq, lb, hq, lh = "b%d" % r, "lb%d" % r, "h%d" % r, "lh%d" % r
+        NS = len(STAGE)
+        for s, (ks, w, ww, to, lo, io) in enumerate(STAGE):
+            at = P * (ks[0] - 1)
+            for k in ks:
+                scan(A("x4", P * (k - 1), P * k), A("g1", k, C, 4), A("em4", 0, P), ALU.max, ALU.add)
+            ts(A("l1", at // 4, (at + w) // 4), A("x4", at + 3, at + w, 4), col(CL1), None, ALU.add)
+            if VB[s] < w // 4:
+                pick(S, A("bt", 4 * to + 16 * VB[s], 4 * (to + w)), win, A("l1", at // 4 + VB[s], (at + w) // 4))
+        for s, (ks, w, ww, to, lo, io) in enumerate(STAGE):
+            at = P * (ks[0] - 1)
+            if VB[s]:
+                pick(V, A("bt", 4 * to, 4 * to + 16 * VB[s]), win, A("l1", at // 4, at // 4 + VB[s]))
+            quant(bq, to, to + ww, A("bt", 4 * to, 4 * (to + ww)))
+            send(bq, lb, s, False, "b%d" % r)
         scan(A("x4", R3, C), A("g1", 0, C, 4), A("em4", 0, P), ALU.max, ALU.add)
         ts(A("l1", 72, 96), A("x4", R3 + 3, C, 4), col(CL1), None, ALU.add)
-        scan(A("ze"), A("ge"), A("em4", 0, P), ALU.max, ALU.add)
-        ts(A("l3"), A("ze", 3, P, 4), col(CL1), None, ALU.add)
-        pick(V, A("bt", 4 * R3, 4 * C), win, A("l1", 72, 96))
-        pick(S, A("e3", 0, 384), win, A("l3"), scale=0.5)
-        act(A("e3", 384, 768), A("e3", 0, 384), ACT.Copy)
-        act(A("e3", 768, 1152), A("e3", 0, 384), ACT.Copy)
-        quant(bq, R3, R3 + 128, A("bt", 4 * R3, 4 * R3 + 512))
+        pick(OWNQ, A("bt", 4 * TW, 4 * (TW + P)), win, A("l1", 72, 96))
         if r == 0:
-            quant("eh", 0, 512, A("ebth"))
-        for b in range(4):
-            mm(b, 128, "eh", 128 * b, bq, R3)
+            act(A("ebt"), A("ebth"), ACT.Copy, scale=2.0)
+            for b in range(4):
+                quant("eh", 128 * b, 128 * b + 128, A("ebth", 3 - b, 515 - b))
+            quant(lb, STAGE[0][1], STAGE[0][1] + 128, A("nil"))
         ts(K(STF), K(S12), K(ZZ), None, ALU.add)
         ts(K(ENF), K(E12), K(EN3), None, ALU.max)
         ts(A("rf"), A("ex", 15, C, 16), -1.0, col(CA), ALU.mult, ALU.add)
         ts(K(LW), K(STF), -2.0 * P, K(ENF), ALU.add, ALU.max)
         ts(A("o2"), A("k", STF, STF + 2), 0.5, float(EO), ALU.mult, ALU.add)
+        quant(bq, TW, TW + 128, A("bt", 4 * TW, 4 * TW + 512))
         for b in range(4):
-            tt(A("zt0", b, 384, 4), ps(b, P), A("e3", b, 384, 4), ALU.add)
-        quant("z0", 0, 128, A("zt0"))
-        for b in range(4):
-            mm(b, 128, "w", 128 * b, "z0", 0)
-        for b in range(4):
-            act(A("ht0", b, 384, 4), ps(b, P), ACT.Copy, scale=0.03125)
+            mm(b, 128, "eh", 128 * b, bq, TW)
         ts(A("sl"), tb, 0.5, None, ALU.mult, by=A("o2"))
         tt(A("cc", 0, 4), A("sl", 0, 4), A("crow"), ALU.add)
         ts(A("cc", 4, 8), A("cc", 0, 4), -1.0, None, ALU.mult)
-        for k in range(4):
-            ts(A("ff", k, 192, 8), A("rf"), A("sl", 16 + k, 17 + k), A("cc", k, k + 1), ALU.is_ge, ALU.mult)
-        for k in range(4):
-            ts(A("ff", 4 + k, 192, 8), A("rf"), A("sl", k, k + 1), A("cc", 4 + k, 5 + k), ALU.is_ge, ALU.mult)
-        scan(A("fs"), A("rz8"), A("ff"), ALU.mult, ALU.add)
-        tt(A("lf"), A("fs", 7, 192, 8), A("rf"), ALU.subtract)
-        tt(A("lg"), A("lf"), A("j24"), ALU.max)
-        cp(A("loc"), A("lg"))
-        lb, hq = "lb%d" % r, "h%d" % r
-        for c in range(2):
-            for b in range(4):
-                mm(b + 4 - 4 * c, HALF, "eh", 128 * b, lb, HALF * c)
-        for c in range(2):
-            lo, hi = 4 * HALF * c, 4 * HALF * (c + 1)
-            for b in range(4):
-                tt(A("zt", lo + b, hi, 4), ps(b + 4 - 4 * c, HALF), A("e3", lo + b, hi, 4), ALU.add)
-            quant("z", HALF * c, HALF * (c + 1), A("zt", lo, hi))
-            for b in range(4):
-                mm(b + 4 - 4 * c, HALF, "w", 128 * b, "z", HALF * c)
         for b in range(4):
-            act(A("ht", b, 4 * HALF, 4), ps(b + 4, HALF), ACT.Copy, scale=0.03125)
-        quant(hq, 0, HALF, A("ht", 0, 4 * HALF))
+            tt(A("zt0", b, 384, 4), ps(b, P), A("e3", b, 384, 4), ALU.add)
+        quant("z0", 0, 128, A("zt0"))
+
+        def state_list(part):
+            if part == 0:
+                for k in range(4):
+                    ts(A("ff", k, 192, 8), A("rf"), A("sl", 16 + k, 17 + k), A("cc", k, k + 1), ALU.is_ge, ALU.mult)
+                for k in range(4):
+                    ts(A("ff", 4 + k, 192, 8), A("rf"), A("sl", k, k + 1), A("cc", 4 + k, 5 + k), ALU.is_ge, ALU.mult)
+                scan(A("fs"), A("rz8"), A("ff"), ALU.mult, ALU.add)
+                return
+            tt(A("lf"), A("fs", 7, 192, 8), A("rf"), ALU.subtract)
+            tt(A("lg"), A("lf"), A("j24"), ALU.max)
+            cp(A("loc"), A("lg"))
+
+        bank = lambda s: 4 * ((s + 1) % 2)
+        pw = lambda b, io, w: A("ps%d" % b, io, io + w)
+
+        def unpack(s, const, src, at):
+            ks, w, ww, to, lo, io = STAGE[s]
+            for b in range(4):
+                mm(at + b, ww, const, 128 * b, src, lo - io)
+
+        def make_z(s):
+            ks, w, ww, to, lo, io = STAGE[s]
+            for b in range(4):
+                tt(A("zt", 4 * to + b, 4 * (to + w), 4), pw(bank(s) + b, io, w), A("e3", b, 4 * w, 4), ALU.add)
+
+        def layer(s):
+            ks, w, ww, to, lo, io = STAGE[s]
+            quant("z", to, to + ww, A("zt", 4 * to, 4 * (to + ww)))
+            for b in range(4):
+                mm(bank(s) + b, ww, "w", 128 * b, "z", to)
+
+        def make_h(s, on_v):
+            ks, w, ww, to, lo, io = STAGE[s]
+            for b in range(4):
+                o = A("ht", 4 * to + b, 4 * (to + w), 4)
+                if b in on_v:
+                    ts(o, ps(bank(s) + b, w), 0.03125, None, ALU.mult)
+                else:
+                    act(o, ps(bank(s) + b, w), ACT.Copy, scale=0.03125)
+
+        def back(s):
+            ks, w, ww, to, lo, io = STAGE[s]
+            quant(hq, to, to + ww, A("ht", 4 * to, 4 * (to + ww)))
+            send(hq, lh, s, True, "h%d" % r)
+
+        unpack(0, "eh", lb, bank(0))
+        unpack(1, "eh", lb, bank(1))
+        make_z(0)
+        layer(0)
+        make_z(1)
+        layer(1)
+        state_list(0)
+        make_h(0, H0V)
+        back(0)
+        ob = bank(0)
         for b in range(4):
-            o = A("ht", 4 * HALF + b, 4 * R3, 4)
-            if b % 2:
-                ts(o, ps(b, HALF), 0.03125, None, ALU.mult)
-            else:
-                act(o, ps(b, HALF), ACT.Copy, scale=0.03125)
-        quant(hq, HALF, R3, A("ht", 4 * HALF, 4 * R3))
-        send(hq, "lh%d" % r, True, "ah%d" % r, "lh%d" % r)
-        arrived("lh%d" % r, "ah%d" % r)
+            mm(ob + b, 128, "w", 128 * b, "z0", 0)
+        make_h(1, H1V)
+        back(1)
+        for b in range(4):
+            act(A("ht0", b, 384, 4), ps(ob + b, P), ACT.Copy, scale=0.03125)
+        state_list(1)
         pick(S, A("g2"), A("id4"), A("loc"))
-        quant("h0k", 0, 128, A("ht0"))
         if r == 0:
-            quant("e1", 0, 512, A("ebt"))
+            for b in range(4):
+                quant("e1", 128 * b, 128 * b + 128, A("ebt", 3 - b, 515 - b))
+            quant(lh, STAGE[0][1], STAGE[0][1] + 128, A("nil"))
+        quant("h0k", 0, 128, A("ht0"))
         for b in range(4):
-            mm(b, 128, "e1", 128 * b, "h0k", 0)
-        scan(A("x2"), A("g2"), A("em4"), ALU.max, ALU.add)
-        ts(A("l2"), A("x2", 3, C, 4), col(CL2), None, ALU.add)
+            mm(ob + b, 128, "e1", 128 * b, "h0k", 0)
         base = 4 * NB0
+
+        def renew(s):
+            ks, w, ww, to, lo, io = STAGE[s]
+            at = base + 4 * P * (ks[0] - 1)
+            for b in range(4):
+                tt(A(xw, at + b, at + 4 * w, 4), pw(bank(s + 1) + b, io, w), A("bt", 4 * to + b, 4 * (to + w), 4), ALU.add)
+
+        scan(A("x2"), A("g2"), A("em4"), ALU.max, ALU.add)
         for b in range(4):
-            tt(A(xw, base + 4 * R3 + b, base + 4 * C, 4), ps(b, P), A("bt", 4 * R3 + b, 4 * C, 4), ALU.add)
+            tt(A(xw, base + 4 * R3 + b, base + 4 * C, 4), ps(ob + b, P), A("bt", 4 * TW + b, 4 * (TW + P), 4), ALU.add)
+        ts(A("l2"), A("x2", 3, C, 4), col(CL2), None, ALU.add)
         if last:
             pick(S, A("sl2"), A("slt"), A("loc"))
             buf, at = HOME["sl2"]
@@ -547,10 +605,12 @@ def rank_program(g, core, T, topo):
             iota(A("slt", 0, NB0), [[0, NB0]], -1, 0)
             iota(A("slt", NB0, NB0 + R3), [[1, R3]], P, 0)
             iota(A("slt", NB0 + R3, XW), [[1, P]], 0, 0)
-        for b in range(4):
-            mm(4 + b, R3, "e1", 128 * b, "lh%d" % r, 0)
-        for b in range(4):
-            tt(A(xw, base + b, base + 4 * R3, 4), ps(4 + b, R3), A("bt", b, 4 * R3, 4), ALU.add)
+        for s in range(NS):
+            unpack(s, "e1", lh, bank(s + 1))
+            renew(s)
+            if s == 0 and not last:
+                quant("lb1", STAGE[0][1], STAGE[0][1] + 128, A("nil"))
+                quant("lh1", STAGE[0][1], STAGE[0][1] + 128, A("nil"))
         xn, xq = ("xf", "xf") if last else ("xw1", "x1")
         full = A(xw, 0, 4 * XW)
         pick(V, A(xn, 0, 16 * VX), full, A("l2", 0, VX))
@@ -578,5 +638,5 @@ def rank_program(g, core, T, topo):
     for s in used:
         g.sync.wait_ge(T.sem[s], 16)
     for r in range(2):
-        g.wait_ge(T.sem["lb%d" % r], NARR)
-        g.wait_ge(T.sem["lh%d" % r], NARR)
+        g.wait_ge(T.sem["lb%d" % r], NARR * len(STAGES))
+        g.wait_ge(T.sem["lh%d" % r], NARR * len(STAGES))

@@ -237,7 +237,8 @@ def rank_program(g, core, T, topo):
         dma(q, a[0], src, [a[1]], [])
 
     load(S, "ut", 0, 512, T.u[:])
-    load(SY, "xw0", 0, 4 * C, T.x[:])
+    load(SY, "xw0", 0, 2 * C, T.x[:, 0:2 * C])
+    load(SY, "xw0", 2 * C, 4 * C, T.x[:, 2 * C:4 * C])
     need(SY, [], [A("xw0", 0, 4 * C)[1]])
     wq = A("qw")
     dma(SY, wq[0].bitcast(dt.uint8), T.wc[:], [wq[1]], [])
@@ -292,8 +293,19 @@ def rank_program(g, core, T, topo):
     ms(A("krow", 0, 16), 1.0 / 6.0)
     ts(col(CA), col(Q16), D16, A16 - 15 * D16, ALU.mult, ALU.add)
     ts(col(KC), col(Q4), -0.125, 0.375, ALU.mult, ALU.add)
+    ts(col(9), col(R4), -2.0, -1.0, ALU.mult, ALU.add)
+    ts(col(10), col(R4), -D4, 3 * D4 - A4, ALU.mult, ALU.add)
+    ts(col(11), col(Q16), -1.0, -368.0, ALU.mult, ALU.add)
+    ts(col(12), col(KC), 2.0 * (CUTS[2][1] - 1), None, ALU.add)
     ts(A("nm16"), A("r16"), col(Q16), -BIG, ALU.not_equal, ALU.mult)
     ts(A("rst"), A("r16"), 0.0, -2 * BIG, ALU.is_equal, ALU.mult)
+    ts(A("j24"), A("j16"), col(Q16), None, ALU.add)
+    ts(A("ct"), A("j16"), col(11), None, ALU.add)
+    ts(A("cs"), A("j16"), -0.5, col(9), ALU.mult, ALU.add)
+    ts(col(CL2), col(10), col(Q4), None, ALU.add)
+    ts(A("pose"), A("j24", 0, 6), -2.0, 2.0 * C - 1.0, ALU.mult, ALU.add)
+    ts(A("krow", 16, 32), A("kr"), 0.125, None, ALU.mult)
+    ts(col(CL1), col(CL2), -TOP, None, ALU.add)
     quant("u", 0, 128, A("ut"))
     for n in ("a", "c"):
         ul, qa, qb = A("ul" + n), A("qu" + n), A("qu")
@@ -302,27 +314,17 @@ def rank_program(g, core, T, topo):
     act(A("rz16"), A("r16"), ACT.Sign)
     act(A("em16"), A("nm16"), ACT.Identity, scale=(A16 + D16) / BIG, bias=A16)
     act(A("d1"), A("nm16"), ACT.Identity, scale=(A16 + D16) / BIG, bias=A16)
-    ts(A("gt"), A("g64"), col(PG), None, ALU.is_equal)
-    ts(col(9), col(R4), -2.0, -1.0, ALU.mult, ALU.add)
-    ts(col(10), col(R4), -D4, 3 * D4 - A4, ALU.mult, ALU.add)
-    ts(col(11), col(Q16), -1.0, -368.0, ALU.mult, ALU.add)
-    ts(A("j24"), A("j16"), col(Q16), None, ALU.add)
-    quant("g", 0, 128, A("gt"))
-    ts(A("ct"), A("j16"), col(11), None, ALU.add)
-    ts(A("cs"), A("j16"), -0.5, col(9), ALU.mult, ALU.add)
-    ts(col(CL2), col(10), col(Q4), None, ALU.add)
-    ts(A("pose"), A("j24", 0, 6), -2.0, 2.0 * C - 1.0, ALU.mult, ALU.add)
-    ts(A("krow", 16, 32), A("kr"), 0.125, None, ALU.mult)
-    ts(col(CL1), col(CL2), -TOP, None, ALU.add)
 
     def late_constants(k):
         if k == 0:
+            ts(A("gt"), A("g64"), col(PG), None, ALU.is_equal)
             ts(A("e4"), A("r4"), col(R4), None, ALU.is_equal)
+            quant("g", 0, 128, A("gt"))
             tt(A("k24"), A("ct"), A("em16", 15, C, 16), ALU.add)
-            cp(A("krd", 16, 32), A("krow", 16, 32))
         if k == 1:
             act(A("c15"), A("c15"), ACT.Copy, scale=0.5)
             act(A("em4"), A("e4"), ACT.Identity, scale=A4 + D4, bias=-D4)
+            act(A("krd", 16, 32), A("kr"), ACT.Copy, scale=-0.125)
             act(A("rz8"), A("rz8"), ACT.Sign)
 
     act(A("hh"), A("ij"), ACT.Identity, scale=2.0 ** -22, bias=0.5)
@@ -358,10 +360,13 @@ def rank_program(g, core, T, topo):
     for t in range(1, 24):
         jk.append(jk[-1] + 16 * t)
     K = lambda i: A("kb", i, i + 1) if i in (9, 10) else A("k", i, i + 1)
-    ACC, TH, M1, M2, M3, OWN1, OWN2, OWN3, OWNB, B2, B3, EN1, EN2, S1, S2, S12, E12, DD, ZZ, EN3, STF, LW, ENF = range(23)
+    ACC, TH, M1, M2, M3, OWN1, OWN2, OWN3, OWNB, B2, B3, EN1, EN2, S1, S2, S12, E12, DD, ZZ, EN3, STF, LW, ENF, AC2, X2, X3 = range(26)
     SB = (19, 18, 17)
-    RV = 7
-    VX = 52
+    RV = (1, 2, 3, 4, 5, 6)
+    LO = C // 2
+    LOW = ((11, 10, 9, 8, 7), (6, 5), (4, 3, 2, 1))
+    VG = 18
+    VX = (30, 22)
     VB = (26, 14)
     H0V, H1V = (3,), (1, 3)
     OWNQ = S
@@ -370,52 +375,70 @@ def rank_program(g, core, T, topo):
         xw, last = "xw%d" % r, r == 1
         xq = "x%d" % r
         if r == 0:
-            quant(xq, 0, C, A(xw, 0, 4 * C))
-        mm(0, C, "ua", 0, xq, 0)
-        mm(2, C, "uc", 0, xq, 0)
-        mm(1, C, "ua", 0, xq, 0)
-        if r == 0:
+            quant(xq, 0, LO, A(xw, 0, 4 * LO))
+            mm(0, LO, "ua", 0, xq, 0)
             late_constants(0)
-        tt(A("vm"), ps(0, C), A("nm16"), ALU.add)
-        act(A("vsa"), ps(2, C), ACT.Sign)
-        act(A("vsb"), A("vsa"), ACT.Sign, bias=-0.5, acc=K(ACC))
-        scan(A("zz"), A("rst"), A("vm"), ALU.add, ALU.max)
+        mm(5, LO, "uc", 0, xq, 0)
+        act(A("vsa", 0, LO), ps(5, LO), ACT.Sign)
+        act(A("vsb", 0, LO), A("vsa", 0, LO), ACT.Sign, bias=-0.5, acc=K(ACC))
+        act(K(AC2), K(ACC), ACT.Identity, scale=0.5, bias=1.5 * C + 1.0 / 6.0)
         own = lambda t: A("zz", 16 * t + 15, 16 * t + 16)
         row = lambda t: A("mt%d" % slots[t][0], slots[t][1], 64 * t, 4)
         tmp = lambda t: A("sgn", jk[t - 1], jk[t - 1] + 16 * t)
+
+        def compare(ts_, bank):
+            for t in ts_:
+                ts(row(t), ps(bank, 16 * t), own(t), None, ALU.is_lt)
+                if t not in RV:
+                    act(A("jk", jk[t - 1], jk[t - 1] + 16 * t), row(t), ACT.Copy, acc=A("rsum", t, t + 1))
+
+        def pack(i):
+            quant("m%d" % i, 0, MTN[i], A("mt%d" % i))
+
+        def sums(i):
+            mm(3, MTN[i], "g", 0, "m%d" % i, 0, i == 0, i == 3)
+
+        tt(A("vm", 0, LO), ps(0, LO), A("nm16", 0, LO), ALU.add)
+        if r == 0:
+            quant(xq, LO, C, A(xw, 4 * LO, 4 * C))
+        mm(4, C, "ua", 0, xq, 0)
+        mm(1, C, "ua", 0, xq, 0)
+        mm(2, LO, "uc", 0, xq, LO)
+        scan(A("zz", 0, LO), A("rst", 0, LO), A("vm", 0, LO), ALU.add, ALU.max)
+        compare(LOW[0], 0)
+        tt(A("vm", LO, C), A("ps4", LO, C), A("nm16", LO, C), ALU.add)
+        compare(LOW[1], 0)
+        scan(A("zz", LO, C), A("rst", LO, C), A("vm", LO, C), ALU.add, ALU.max)
+        compare(LOW[2], 0)
+        pack(4)
+        pack(5)
         for t in SB:
             act(tmp(t), ps(1, 16 * t), ACT.Sign, scale=-1.0, bias=own(t))
+        act(A("vsa", LO, C), ps(2, LO), ACT.Sign)
         for t in SB:
             act(row(t), tmp(t), ACT.Relu, acc=A("rsum", t, t + 1))
-        act(K(TH), K(ACC), ACT.Identity, scale=0.5, bias=1.5 * C + 1.0 / 6.0)
-        def sums(i):
-            quant("m%d" % i, 0, MTN[i], A("mt%d" % i))
-            mm(3, MTN[i], "g", 0, "m%d" % i, 0, i == 0, i == 5)
-
-        done = None
-        for t in range(23, 0, -1):
-            if t in SB:
-                continue
-            i, f = slots[t]
-            ts(row(t), ps(0, 16 * t), own(t), None, ALU.is_lt)
-            if t > RV:
-                act(A("jk", jk[t - 1], jk[t - 1] + 16 * t), row(t), ACT.Copy, acc=A("rsum", t, t + 1))
-            if t == 22:
-                tt(A("mt0", 0, 4 * C, 4), ps(0, C), A("zz"), ALU.is_le)
-            if done is not None:
-                sums(done)
-                done = None
-            if f == 3:
-                done = i
-            if t == 9:
-                sums(1)
+        act(A("vsb", LO, C), A("vsa", LO, C), ACT.Sign, bias=-0.5, acc=K(ACC))
+        compare((23, 22), 4)
+        tt(A("mt0", 0, 4 * C, 4), ps(4, C), A("zz"), ALU.is_le)
+        compare((21,), 4)
+        compare([t for t in (20, 19, 18, 17) if t not in SB] + [16], 4)
+        pack(0)
+        for i in (0, 4, 5):
+            sums(i)
+        compare((15, 14, 13, 12), 4)
+        pack(2)
+        sums(2)
+        pack(1)
+        sums(1)
+        pack(3)
+        sums(3)
         scan(A("dg"), A("rz16"), A("mt0", 0, 4 * C, 4), ALU.mult, ALU.add)
-        sums(5)
-        for t in range(RV, 0, -1):
+        for t in RV:
             red(A("rsum", t, t + 1), row(t), ALU.add)
         scan(A("fj"), A("hh"), A("vsb"), ALU.max, ALU.mult)
         tt(A("ce"), A("k24"), A("dg", 15, C, 16), ALU.subtract)
         tt(A("d1", 15, C, 16), A("ce"), A("rsum"), ALU.subtract)
+        act(K(TH), K(ACC), ACT.Identity, scale=0.5, bias=K(AC2))
         if r == 0:
             late_constants(1)
         scan(A("ex"), ps(3, C), A("d1"), ALU.max, ALU.add)
@@ -436,21 +459,26 @@ def rank_program(g, core, T, topo):
             ts(A("cm", 0, w), A("tb", lo, hi), mult, K(TH), ALU.mult, ALU.is_le)
             if m == 1:
                 eq(B2, OWN1, M1, GONE)
-                eq(EN1, OWN1, M1, K(M1))
+                act(A("c23"), A("c2", 4, 6), ACT.Identity, bias=K(B2))
+                act(K(X2), K(B2), ACT.Identity, scale=-1.0, bias=col(12))
+                act(K(S1), K(B2), ACT.Copy, scale=2.0 * C / GONE)
             if m == 2:
                 eq(B3, OWN2, M2, GONE)
-                ts(A("krd", 0, 16), A("krow", 16, 32), K(M2), None, ALU.subtract)
             scan(A("cn", 0, w), A("cm", 0, w), A("cm", 0, w), ALU.add, ALU.max)
             cnt, of = A("cn", w - 1, w), A("of", 2 * m, 2 * m + 2)
             if m == 0:
                 ts(of, A("c2", 0, 2), cnt, None, ALU.add)
             elif m == 1:
+                eq(EN1, OWN1, M1, K(M1))
                 ts(of, A("c2", 2, 4), cnt, K(B2), ALU.add, ALU.add)
-                ts(A("c23"), A("c2", 4, 6), K(B2), None, ALU.add)
+                ts(A("l3"), A("ze", 3, P, 4), col(CL1), None, ALU.add)
             else:
+                ts(K(X3), K(B3), -1.0, K(X2), ALU.mult, ALU.add)
+                eq(S2, OWN2, M2, K(M1))
                 ts(of, A("c23"), cnt, K(B3), ALU.add, ALU.add)
                 eq(EN2, OWN2, M2, K(M2))
-            picktt(A("pk"), tb, of, A("krow") if m < 2 else A("krd"), ALU.add)
+                ts(K(S12), K(S1), K(S2), K(M2), ALU.max, ALU.max)
+            picktt(A("pk"), tb, of, A("krow") if m < 2 else A("krd"), ALU.add if m < 2 else ALU.subtract)
             if m < 2:
                 ts(K(OWN1 + m), A("of", 2 * m, 2 * m + 1), 2.0, col(KC), ALU.mult, ALU.add)
                 red(K(TH), A("pk", 0, 16), ALU.max)
@@ -458,31 +486,28 @@ def rank_program(g, core, T, topo):
             if m == 0:
                 scan(A("ze"), A("ge"), A("em4", 0, P), ALU.max, ALU.add)
             if m == 1:
-                eq(S1, OWN1, M1, 2.0 * C)
-                ts(A("l3"), A("ze", 3, P, 4), col(CL1), None, ALU.add)
+                act(A("krd", 0, 16), A("krow", 16, 32), ACT.Identity, scale=-1.0, bias=K(M2))
                 pick(S, A("e3", 0, 384), win, A("l3"), scale=0.5)
                 act(A("e3", 384, 768), A("e3", 0, 384), ACT.Copy)
-        ts(K(OWN3), A("of", 4, 5), -float(EO), 2.0, ALU.add, ALU.mult)
-        eq(S2, OWN2, M2, K(M1))
-        red(K(M3), A("pk", 16, 32), ALU.max)
-        ts(K(OWN3), K(OWN3), col(KC), None, ALU.add)
-        red(K(DD), A("pk", 0, 16), ALU.max)
-        ts(K(S12), K(S1), K(S2), K(M2), ALU.max, ALU.max)
-        ts(K(OWNB), K(OWN3), K(B2), K(B3), ALU.subtract, ALU.subtract)
+        ts(K(OWNB), cnt, 2.0, K(X3), ALU.mult, ALU.add)
         ts(K(E12), K(EN1), K(EN2), None, ALU.max)
-        eq(EN3, OWN3, M3, K(M3))
-        ts(K(ZZ), K(OWNB), K(M3), K(DD), ALU.is_lt, ALU.mult)
+        red(K(M3), A("pk", 16, 32), ALU.max)
+        red(K(DD), A("pk", 0, 16), ALU.max)
         ts(A("sx"), A("cs"), K(S12), K(E12), ALU.add, ALU.max)
+        eq(EN3, OWNB, M3, K(M3))
+        ts(K(ZZ), K(OWNB), K(M3), K(DD), ALU.is_lt, ALU.mult)
         ts(A("pos"), A("sx"), K(ZZ), K(EN3), ALU.add, ALU.max)
-        pick(V, A("g1", 0, 224), A("t2"), A("pos", 0, 14))
-        pick(S, A("g1", 224, C), A("t2"), A("pos", 14, 24))
+        pick(V, A("g1", 0, 16 * VG), A("t2"), A("pos", 0, VG))
+        pick(S, A("g1", 16 * VG, C), A("t2"), A("pos", VG, 24))
         bq, lb, hq, lh = "b%d" % r, "lb%d" % r, "h%d" % r, "lh%d" % r
         NS = len(STAGE)
+        for k in (1, 2, 3):
+            scan(A("x4", P * (k - 1), P * k), A("g1", k, C, 4), A("em4", 0, P), ALU.max, ALU.add)
+        scan(A("x4", R3, C), A("g1", 0, C, 4), A("em4", 0, P), ALU.max, ALU.add)
+        ts(A("l1", 0, 72), A("x4", 3, R3, 4), col(CL1), None, ALU.add)
+        ts(A("l1", 72, 96), A("x4", R3 + 3, C, 4), col(CL1), None, ALU.add)
         for s, (ks, w, ww, to, lo, io) in enumerate(STAGE):
             at = P * (ks[0] - 1)
-            for k in ks:
-                scan(A("x4", P * (k - 1), P * k), A("g1", k, C, 4), A("em4", 0, P), ALU.max, ALU.add)
-            ts(A("l1", at // 4, (at + w) // 4), A("x4", at + 3, at + w, 4), col(CL1), None, ALU.add)
             if VB[s] < w // 4:
                 pick(S, A("bt", 4 * to + 16 * VB[s], 4 * (to + w)), win, A("l1", at // 4 + VB[s], (at + w) // 4))
         for s, (ks, w, ww, to, lo, io) in enumerate(STAGE):
@@ -491,8 +516,6 @@ def rank_program(g, core, T, topo):
                 pick(V, A("bt", 4 * to, 4 * to + 16 * VB[s]), win, A("l1", at // 4, at // 4 + VB[s]))
             quant(bq, to, to + ww, A("bt", 4 * to, 4 * (to + ww)))
             send(bq, lb, s, False, "b%d" % r)
-        scan(A("x4", R3, C), A("g1", 0, C, 4), A("em4", 0, P), ALU.max, ALU.add)
-        ts(A("l1", 72, 96), A("x4", R3 + 3, C, 4), col(CL1), None, ALU.add)
         pick(OWNQ, A("bt", 4 * TW, 4 * (TW + P)), win, A("l1", 72, 96))
         if r == 0:
             act(A("ebt"), A("ebth"), ACT.Copy, scale=2.0)
@@ -565,14 +588,24 @@ def rank_program(g, core, T, topo):
         layer(0)
         make_z(1)
         layer(1)
-        state_list(0)
+        if NS == 2:
+            state_list(0)
         make_h(0, H0V)
-        back(0)
-        ob = bank(0)
+        if NS == 3:
+            unpack(2, "eh", lb, bank(2))
+            back(0)
+            make_z(2)
+            layer(2)
+            make_h(1, H0V)
+            back(1)
+            state_list(0)
+        else:
+            back(0)
+        ob = bank(NS)
         for b in range(4):
             mm(ob + b, 128, "w", 128 * b, "z0", 0)
-        make_h(1, H1V)
-        back(1)
+        make_h(NS - 1, H1V)
+        back(NS - 1)
         for b in range(4):
             act(A("ht0", b, 384, 4), ps(ob + b, P), ACT.Copy, scale=0.03125)
         state_list(1)
@@ -590,7 +623,7 @@ def rank_program(g, core, T, topo):
             ks, w, ww, to, lo, io = STAGE[s]
             at = base + 4 * P * (ks[0] - 1)
             for b in range(4):
-                tt(A(xw, at + b, at + 4 * w, 4), pw(bank(s + 1) + b, io, w), A("bt", 4 * to + b, 4 * (to + w), 4), ALU.add)
+                tt(A(xw, at + b, at + 4 * w, 4), pw(bank(NS + s + 1) + b, io, w), A("bt", 4 * to + b, 4 * (to + w), 4), ALU.add)
 
         scan(A("x2"), A("g2"), A("em4"), ALU.max, ALU.add)
         for b in range(4):
@@ -606,33 +639,35 @@ def rank_program(g, core, T, topo):
             iota(A("slt", NB0, NB0 + R3), [[1, R3]], P, 0)
             iota(A("slt", NB0 + R3, XW), [[1, P]], 0, 0)
         for s in range(NS):
-            unpack(s, "e1", lh, bank(s + 1))
+            unpack(s, "e1", lh, bank(NS + s + 1))
             renew(s)
             if s == 0 and not last:
                 quant("lb1", STAGE[0][1], STAGE[0][1] + 128, A("nil"))
                 quant("lh1", STAGE[0][1], STAGE[0][1] + 128, A("nil"))
         xn, xq = ("xf", "xf") if last else ("xw1", "x1")
         full = A(xw, 0, 4 * XW)
-        pick(V, A(xn, 0, 16 * VX), full, A("l2", 0, VX))
-        pick(S, A(xn, 16 * VX, 4 * C), full, A("l2", VX, 96))
-        quant(xq, 0, 4 * VX, A(xn, 0, 16 * VX))
-        quant(xq, 4 * VX, C, A(xn, 16 * VX, 4 * C))
+        for h in range(2):
+            pick(S, A(xn, 4 * LO * h + 16 * VX[h], 4 * LO * (h + 1)), full, A("l2", 48 * h + VX[h], 48 * (h + 1)))
+        for h in range(2):
+            pick(V, A(xn, 4 * LO * h, 4 * LO * h + 16 * VX[h]), full, A("l2", 48 * h, 48 * h + VX[h]))
+            quant(xq, LO * h, LO * (h + 1), A(xn, 4 * LO * h, 4 * LO * (h + 1)))
+            if last:
+                mm(3 - h, LO, "v", 0, xq, LO * h)
+                qf = A("qxf", LO * h, LO * (h + 1))
+                dma(SY, T.oc[:, 4 * LO * h:4 * LO * (h + 1)], qf[0].bitcast(dt.uint8), [], [qf[1]])
+            elif h == 0:
+                mm(0, LO, "ua", 0, xq, 0)
 
     one_round(0)
     one_round(1)
 
-    h = 4 * VX
-    mm(3, h, "v", 0, "xf", 0)
-    mm(2, C - h, "v", 0, "xf", h)
-    qf = A("qxf")
-    dma(SY, T.oc[:], qf[0].bitcast(dt.uint8), [], [qf[1]])
-    y0, y1 = A("yt", 0, h), A("yt", h, C)
-    act(y0, ps(3, h), ACT.Copy)
-    cp(y1, ps(2, C - h))
-    dma(S, T.y[:, 0:h], y0[0], [], [y0[1]])
+    y0, y1 = A("yt", 0, LO), A("yt", LO, C)
+    act(y0, ps(3, LO), ACT.Copy)
+    cp(y1, ps(2, LO))
+    dma(S, T.y[:, 0:LO], y0[0], [], [y0[1]])
     for k in range(4):
         dma(SY if k < 2 else S, T.osc[4 * k:4 * k + 4, :], T["sxf"][32 * k:32 * k + 4, :], [], [A("sxf")[1]])
-    dma(SY, T.y[:, h:C], y1[0], [], [y1[1]])
+    dma(SY, T.y[:, LO:C], y1[0], [], [y1[1]])
     for q in (V, S, PE, G):
         g.sync.wait_ge(T.sem["s" + q], count[q])
     for s in used:

@@ -5,23 +5,21 @@ C, P = 384, 96
 R3 = 3 * P
 HALF = R3 // 2
 BIG = 2.0 ** 93
-NB0 = 400
+XZ = C + 16
+NB0 = C
 XW = NB0 + C
-EO = 336
+EO = 400
 TOP = 2.0 ** 23
 D16, A16 = 1024.0, 14848.0
 D4, A4 = 8192.0, 20480.0
-CUTS = ((4.0 / 3.0, 230, 330), (1.5, 114, 264), (2.0, 38, 176))
+CUTS = ((4.0 / 3.0 - 0.00038, 230, 330), (1.5, 114, 264), (2.0, 38, 176))
 GONE = -4096.0
+TINY = 2.0 ** -120
 STAGES = ((1, 2), (3,))
-STAGE = []
-_to = _lo = 0
-for _ks in STAGES:
-    _w = P * len(_ks)
-    STAGE.append((_ks, _w, max(_w, 128), _to, _lo, 32 if _w < 128 and _lo else 0))
-    _to += max(_w, 128)
-    _lo += _w + (0 if _lo else 128)
-TW, LWD = _to, _lo
+W2 = 2 * P
+OWN = 3 * P + 32
+B_FROM, B_TO = {1: 0, 2: P, 3: 2 * P, 0: OWN}, {3: OWN + P, 1: OWN + 2 * P, 2: OWN + 3 * P}
+H_FROM, H_TO = {1: 0, 2: P, 0: 5 * P, 3: 6 * P}, {1: 2 * P, 2: 3 * P, 3: 4 * P}
 
 SCRATCH = {}
 SEMAPHORES = ["sv", "ss", "st", "sp"]
@@ -52,16 +50,17 @@ def _pack(buf, pieces, dtype="float32"):
 for _i in range(8):
     _b("ps%d" % _i, 512, "float32", "psum")
 for _r in range(2):
-    _b("xw%d" % _r, 4 * XW, "bfloat16")
-    for _n, _w in (("x", C), ("b", TW + 128), ("lb", LWD), ("h", TW), ("lh", LWD)):
+    _b("xw%d" % _r, 4 * XZ, "bfloat16")
+    _b("xp%d" % _r, 4 * XW, "bfloat16")
+    for _n, _w in (("x", C), ("b", OWN + 4 * P), ("h", 7 * P)):
         _q("%s%d" % (_n, _r), _w)
     SEMAPHORES += ["lb%d" % _r, "lh%d" % _r] + ["a%s%d_%d" % (_n, _r, _s) for _n in "bh" for _s in range(len(STAGES))]
 _b("xf", 4 * C, "bfloat16")
 for _n, _w in (("xf", C), ("u", 128), ("ua", 128), ("uc", 128), ("v", 128), ("w", 512), ("e1", 512), ("eh", 512), ("g", 128),
-               ("z0", 128), ("z", TW), ("h0k", 128)):
+               ("z", C)):
     _q(_n, _w)
-for _n, _w in (("ut", 512), ("vt", 512), ("eone", 516), ("ebt", 516), ("ebth", 516), ("gt", 512), ("bt", 4 * TW + 512),
-               ("e3", 8 * P), ("zt0", 512), ("zt", 4 * TW), ("ht0", 512), ("ht", 4 * TW), ("jk", 4416), ("sgn", 4416), ("nil", 512)):
+for _n, _w in (("ut", 512), ("vt", 512), ("eone", 516), ("ebt", 516), ("ebth", 516), ("gt", 512), ("bt", 4 * (OWN + P)),
+               ("e3", 4 * P), ("zt", 4 * C), ("ht", 4 * C), ("jk", 4416), ("sgn", 4416)):
     _b(_n, _w, "bfloat16")
 MTN = (384, 320, 256, 192, 128, 128)
 for _i in range(6):
@@ -69,19 +68,19 @@ for _i in range(6):
     _q("m%d" % _i, MTN[_i])
 _b("yt", C)
 _b("srt", C)
-_b("tb", EO + C + 8)
+_b("tb", EO + 2 * C + 8)
 _b("t2", 2 * C)
-_pack("cb", [(_n, C) for _n in ("r16", "r4", "nm16", "rst", "rz16", "e4")] + [("g64", 512), ("rz8", 192)], "bfloat16")
-_pack("consts", [(_n, C) for _n in ("em16", "em4", "hh", "ij", "c15")] + [("id4", XW), ("slt", XW)]
+_pack("cb", [(_n, C) for _n in ("r16", "nm16", "rst", "rz16")] + [("g64", 512), ("rz5", 120), ("r4", P), ("e4", P)], "bfloat16")
+_pack("consts", [(_n, C) for _n in ("hh", "ij", "c15")] + [("slt", XW), ("em4", P)]
       + [(_n, 24) for _n in ("k24", "ct", "cs", "j24", "st", "j16")]
-      + [("cols", 16), ("krow", 32), ("kr", 16), ("c2", 8), ("crow", 4), ("il", 8), ("pe", 6)])
+      + [("cols", 24), ("krow", 32), ("kr", 16), ("c2", 8), ("crow", 4), ("il", 8), ("pe", 6)])
 _pack("wide", [(_n, C) for _n in ("vm", "zz", "d1", "ex", "fj", "g1", "x4", "g2", "x2", "sl2")]
-      + [("ge", P), ("ze", P), ("ff", 192), ("fs", 192)])
-_pack("wb", [("vsa", C), ("vsb", C), ("dg", C), ("cm", 160), ("cn", 160), ("kb", 16)], "bfloat16")
-_pack("small", [(_n, 24) for _n in ("rsum", "ce", "rf", "sx", "lf", "lg")] + [("pk", 32), ("krd", 32), ("sl", 32), ("c23", 2), ("cc", 8)]
-      + [("k", 32)])
+      + [("ge", P), ("ze", P), ("ff", 120), ("fs", 120), ("fa", P), ("fb", P)])
+_pack("wb", [("vsa", C), ("vsb", C), ("dg", C), ("cm", 160), ("cn", 480), ("kb", 16)], "bfloat16")
+_pack("small", [(_n, 24) for _n in ("rsum", "ce", "rf", "sx", "lf", "lg")] + [("pk", 32), ("krd", 32), ("sl", 48), ("c23", 2), ("cc", 8)]
+      + [("k", 40)])
 _b("icol", 16, "int32")
-for _n, _w in (("ula", 8), ("ulc", 8), ("pl", 24), ("of", 8), ("pos", 24), ("pose", 6), ("l1", 96), ("l2", 96), ("l3", 24), ("o2", 2), ("loc", 24)):
+for _n, _w in (("ula", 8), ("ulc", 8), ("pl", 24), ("of", 8), ("pos", 24), ("pose", 6), ("l1", 96), ("l2", 96), ("l3", 24), ("o2", 4), ("loc", 24)):
     _b(_n, _w, "uint16")
 NDMA = 24
 SEMAPHORES += ["d%d" % _i for _i in range(NDMA)]
@@ -187,7 +186,8 @@ def rank_program(g, core, T, topo):
         op(V, lambda e: e.memset(o[0], c), [o[1]], [])
 
     def act(o, i, f, scale=1.0, bias=None, acc=None):
-        kw, outs, ins = {"scale": scale}, [o[1]], [i[1]]
+        scale, rs = sc(scale)
+        kw, outs, ins = {"scale": scale}, [o[1]], [i[1]] + rs
         if bias is not None:
             kw["bias"], rb = sc(bias)
             ins = ins + rb
@@ -237,8 +237,9 @@ def rank_program(g, core, T, topo):
         dma(q, a[0], src, [a[1]], [])
 
     load(S, "ut", 0, 512, T.u[:])
-    load(SY, "xw0", 0, 2 * C, T.x[:, 0:2 * C])
-    load(SY, "xw0", 2 * C, 4 * C, T.x[:, 2 * C:4 * C])
+    LO = 192
+    load(SY, "xw0", 0, 4 * LO, T.x[:, 0:4 * LO])
+    load(SY, "xw0", 4 * LO, 4 * C, T.x[:, 4 * LO:4 * C])
     need(SY, [], [A("xw0", 0, 4 * C)[1]])
     wq = A("qw")
     dma(SY, wq[0].bitcast(dt.uint8), T.wc[:], [wq[1]], [])
@@ -248,36 +249,32 @@ def rank_program(g, core, T, topo):
     icol = lambda k: A("icol", k, k + 1)
     col = lambda k: A("cols", k, k + 1)
     Q16, Q4, R4, PG, CA, KC, CL1, CL2 = 1, 2, 3, 4, 5, 6, 7, 8
-    ms(A("eone"), 0.5)
     op(G, lambda e: e.iota(icol(0)[0], [[1, 1]], 0, 1), [icol(0)[1]], [])
     iota(A("il"), [[16, 8]], 0, 0)
     iota(A("r16"), [[0, 24], [1, 16]], 0, 0)
-    iota(A("j16"), [[16, 24]], 0, 0)
-    iota(A("kr"), [[0, 4], [-1, 4]], 3, 0)
-    iota(A("g64"), [[1, 8], [0, 64]], 0, 0)
-    iota(A("r4"), [[0, 96], [1, 4]], 0, 0)
     iota(A("ij"), [[1, C]], 0, 0)
+    iota(A("j16"), [[16, 24]], 0, 0)
+    iota(A("g64"), [[1, 8], [0, 64]], 0, 0)
+    iota(A("r4"), [[0, 24], [1, 4]], 0, 0)
+    tail = lambda i: A("mt%d" % i, 4 * (336 - 64 * i), 4 * MTN[i])
+    for i in (1, 0, 2):
+        iota(tail(i), [[0, 192]], 0, 0)
+    iota(A("kr"), [[0, 4], [-1, 4]], 3, 0)
+    iota(A("c15"), [[0, C]], 3, 0)
+    iota(A("rz5"), [[0, 24], [1, 5]], 0, 0)
     iota(A("tb", EO, EO + C + 1), [[2, C + 1]], 0, 0)
     iota(A("c2", 0, 2), [[EO, 2]], CUTS[0][1] - 1, 0)
     iota(A("c2", 2, 4), [[EO, 2]], CUTS[1][1] - 1, 0)
     iota(A("c2", 4, 6), [[0, 2]], EO + CUTS[2][1] - 1, 0)
-    iota(A("c15"), [[0, C]], 3, 0)
-    iota(A("rz8"), [[0, 24], [1, 8]], 0, 0)
     iota(A("t2", 0, 2 * C, 2), [[0, C]], int(TOP) + 4 * C, 0)
-    iota(A("xw0", 4 * C, 4 * NB0), [[0, 64]], 0, 0)
-    asel(A("ebth"), A("eone"), [[1, 516]], ALU.is_equal, -3, -4)
-    for ks, w, ww, to, lo, io in STAGE:
-        if w < ww:
-            for t_ in ("bt", "zt", "ht"):
-                iota(A(t_, 4 * (to + w), 4 * (to + ww)), [[0, 4 * (ww - w)]], 0, 0)
-    iota(A("bt", 4 * (TW + P), 4 * (TW + 128)), [[0, 128]], 0, 0)
-    iota(A("nil"), [[0, 512]], 0, 0)
-    iota(A("zt0", 384, 512), [[0, 128]], 0, 0)
-    iota(A("ht0", 384, 512), [[0, 128]], 0, 0)
-    iota(A("xw1", 4 * C, 4 * NB0), [[0, 64]], 0, 0)
+    iota(A("xw0", 4 * C, 4 * XZ), [[0, 64]], 0, 0)
+    iota(A("eone"), [[0, 516]], 1, 0)
+    asel(A("ebt"), A("eone"), [[1, 516]], ALU.is_equal, -3, -4)
+    iota(A("tb", EO + C + 1, EO + 2 * C + 2), [[2, C + 1]], 2 * C + 2, 0)
+    iota(A("bt", 4 * R3, 4 * OWN), [[0, 128]], 0, 0)
+    iota(A("xw1", 4 * C, 4 * XZ), [[0, 64]], 0, 0)
     iota(A("crow", 0, 1), [[0, 1]], NB0 + R3 - 1, 0)
     iota(A("crow", 1, 4), [[P, 3]], NB0 - 1, 0)
-    iota(A("id4"), [[4, XW]], 0, 0)
 
     ts(icol(Q16), icol(0), 15, None, ALU.bitwise_and)
     ts(icol(Q4), icol(0), 3, None, ALU.bitwise_and)
@@ -286,48 +283,52 @@ def rank_program(g, core, T, topo):
     cp(A("cols", 1, 5), A("icol", 1, 5))
     ts(A("ula"), A("il"), 4.0, None, ALU.add)
     ts(A("ulc"), A("il"), col(Q4), None, ALU.add)
-    for i in (0, 2, 3, 4, 5, 1):
-        ms(A("mt%d" % i, 4 * (336 - 64 * i), 4 * MTN[i]), 0.0)
+    for i in (3, 4, 5):
+        ms(tail(i), 0.0)
     ms(A("rsum", 0, 1), 0.0)
     ms(A("tb", 0, 1), 0.0)
     ms(A("krow", 0, 16), 1.0 / 6.0)
     ts(col(CA), col(Q16), D16, A16 - 15 * D16, ALU.mult, ALU.add)
     ts(col(KC), col(Q4), -0.125, 0.375, ALU.mult, ALU.add)
     ts(col(9), col(R4), -2.0, -1.0, ALU.mult, ALU.add)
-    ts(col(10), col(R4), -D4, 3 * D4 - A4, ALU.mult, ALU.add)
-    ts(col(11), col(Q16), -1.0, -368.0, ALU.mult, ALU.add)
+    ts(col(10), col(R4), -D4, 3 * D4 - A4 - TOP, ALU.mult, ALU.add)
+    ts(col(11), col(Q16), -1.0, -368.0 - D16, ALU.mult, ALU.add)
     ts(col(12), col(KC), 2.0 * (CUTS[2][1] - 1), None, ALU.add)
+    ts(col(15), col(Q16), 14.5, A16 + D16, ALU.is_gt, ALU.mult)
     ts(A("nm16"), A("r16"), col(Q16), -BIG, ALU.not_equal, ALU.mult)
     ts(A("rst"), A("r16"), 0.0, -2 * BIG, ALU.is_equal, ALU.mult)
-    ts(A("j24"), A("j16"), col(Q16), None, ALU.add)
-    ts(A("ct"), A("j16"), col(11), None, ALU.add)
-    ts(A("cs"), A("j16"), -0.5, col(9), ALU.mult, ALU.add)
-    ts(col(CL2), col(10), col(Q4), None, ALU.add)
-    ts(A("pose"), A("j24", 0, 6), -2.0, 2.0 * C - 1.0, ALU.mult, ALU.add)
-    ts(A("krow", 16, 32), A("kr"), 0.125, None, ALU.mult)
-    ts(col(CL1), col(CL2), -TOP, None, ALU.add)
     quant("u", 0, 128, A("ut"))
-    for n in ("a", "c"):
+
+    def u_columns(n):
         ul, qa, qb = A("ul" + n), A("qu" + n), A("qu")
         op(V, lambda e: e.tensor_copy(qa[0].bitcast(dt.uint32), qb[0].bitcast(dt.uint32).indirect(ul[0])), [qa[1]], [qb[1], ul[1]])
         pick(S, A("su" + n), A("su"), ul)
+
     act(A("rz16"), A("r16"), ACT.Sign)
-    act(A("em16"), A("nm16"), ACT.Identity, scale=(A16 + D16) / BIG, bias=A16)
     act(A("d1"), A("nm16"), ACT.Identity, scale=(A16 + D16) / BIG, bias=A16)
+    act(A("hh"), A("ij"), ACT.Identity, scale=2.0 ** -22, bias=0.5)
+    u_columns("a")
 
     def late_constants(k):
         if k == 0:
-            ts(A("gt"), A("g64"), col(PG), None, ALU.is_equal)
-            ts(A("e4"), A("r4"), col(R4), None, ALU.is_equal)
-            quant("g", 0, 128, A("gt"))
-            tt(A("k24"), A("ct"), A("em16", 15, C, 16), ALU.add)
+            u_columns("c")
+            act(A("g64"), A("g64"), ACT.Abs, scale=-1.0, bias=col(PG))
+            act(A("gt"), A("g64"), ACT.Relu, scale=-1.0, bias=1.0)
+            ts(A("j24"), A("j16"), col(Q16), None, ALU.add)
+            ts(A("k24"), A("j16"), col(11), col(15), ALU.add, ALU.add)
+            ts(A("pose"), A("j24", 0, 6), -2.0, 2.0 * C - 1.0, ALU.mult, ALU.add)
         if k == 1:
             act(A("c15"), A("c15"), ACT.Copy, scale=0.5)
             act(A("em4"), A("e4"), ACT.Identity, scale=A4 + D4, bias=-D4)
             act(A("krd", 16, 32), A("kr"), ACT.Copy, scale=-0.125)
-            act(A("rz8"), A("rz8"), ACT.Sign)
-
-    act(A("hh"), A("ij"), ACT.Identity, scale=2.0 ** -22, bias=0.5)
+            act(A("cs"), A("j16"), ACT.Identity, scale=-0.5, bias=col(9))
+            act(col(CL1), col(10), ACT.Identity, bias=col(Q4))
+            act(A("krow", 16, 32), A("kr"), ACT.Copy, scale=0.125)
+            act(A("rz5"), A("rz5"), ACT.Sign)
+            act(col(13), col(CA), ACT.Identity, scale=2.0, bias=1.0)
+            act(col(14), col(CA), ACT.Copy, scale=-1.0)
+            for m in range(2):
+                act(col(16 + m), col(KC), ACT.Identity, bias=2.0 * (CUTS[m][1] - 1))
 
     cores = list(T.cores)
     n = len(cores)
@@ -335,8 +336,9 @@ def rank_program(g, core, T, topo):
     E = topo.engines(core, peers[0])
     NARR = 2 * len(E)
 
-    def send(src, dst, s, back, sem):
-        ks, w, ww, to, lo, io = STAGE[s]
+    def send(s, back, sem):
+        ks, src, dst = STAGES[s], sem, sem
+        to, lo, w = (H_FROM if back else B_FROM)[ks[0]], (H_TO if back else B_TO)[ks[0]], P * len(ks)
         need(G, [], [A("q" + src, to, to + w)[1], A("s" + src, to, to + w)[1]])
         for kind in "qs":
             tr = []
@@ -360,16 +362,17 @@ def rank_program(g, core, T, topo):
     for t in range(1, 24):
         jk.append(jk[-1] + 16 * t)
     K = lambda i: A("kb", i, i + 1) if i in (9, 10) else A("k", i, i + 1)
-    ACC, TH, M1, M2, M3, OWN1, OWN2, OWN3, OWNB, B2, B3, EN1, EN2, S1, S2, S12, E12, DD, ZZ, EN3, STF, LW, ENF, AC2, X2, X3 = range(26)
+    ACC, TH, M1, M2, M3, OWN1, OWN2, OWN3, OWNB, B2, B3, EN1, EN2, S1, S2, S12, E12, DD, ZZ, EN3, SUM, DIF, STF, LW, ENF, X1, X2, X3, Y1, Y2, M2N = range(31)
     SB = (19, 18, 17)
-    RV = (1, 2, 3, 4, 5, 6)
-    LO = C // 2
-    LOW = ((11, 10, 9, 8, 7), (6, 5), (4, 3, 2, 1))
-    VG = 18
-    VX = (30, 22)
-    VB = (26, 14)
-    H0V, H1V = (3,), (1, 3)
-    OWNQ = S
+    FJ = 256
+    RV0 = ()
+    RV = (1, 2, 3, 4, 5)
+    LOW = ((11, 10, 9, 8, 7), (6, 5), (4, 3, 2, 1), ())
+    VG = 14
+    VX = ((0, LO, (0, 0, 96, 192)), (LO, C, (0, 0, 96, 192)))
+    EFIRST = True
+    VB = (26, 0, 24)
+    H0V, H1V = (2, 3), (2, 3)
 
     def one_round(r):
         xw, last = "xw%d" % r, r == 1
@@ -379,15 +382,15 @@ def rank_program(g, core, T, topo):
             mm(0, LO, "ua", 0, xq, 0)
             late_constants(0)
         mm(5, LO, "uc", 0, xq, 0)
-        act(A("vsa", 0, LO), ps(5, LO), ACT.Sign)
-        act(A("vsb", 0, LO), A("vsa", 0, LO), ACT.Sign, bias=-0.5, acc=K(ACC))
-        act(K(AC2), K(ACC), ACT.Identity, scale=0.5, bias=1.5 * C + 1.0 / 6.0)
+        act(A("vsb", 0, LO), ps(5, LO), ACT.Sign, bias=-TINY)
         own = lambda t: A("zz", 16 * t + 15, 16 * t + 16)
         row = lambda t: A("mt%d" % slots[t][0], slots[t][1], 64 * t, 4)
         tmp = lambda t: A("sgn", jk[t - 1], jk[t - 1] + 16 * t)
 
         def compare(ts_, bank):
             for t in ts_:
+                if t in SB:
+                    continue
                 ts(row(t), ps(bank, 16 * t), own(t), None, ALU.is_lt)
                 if t not in RV:
                     act(A("jk", jk[t - 1], jk[t - 1] + 16 * t), row(t), ACT.Copy, acc=A("rsum", t, t + 1))
@@ -399,25 +402,30 @@ def rank_program(g, core, T, topo):
             mm(3, MTN[i], "g", 0, "m%d" % i, 0, i == 0, i == 3)
 
         tt(A("vm", 0, LO), ps(0, LO), A("nm16", 0, LO), ALU.add)
+        scan(A("zz", 0, LO), A("rst", 0, LO), A("vm", 0, LO), ALU.add, ALU.max)
         if r == 0:
             quant(xq, LO, C, A(xw, 4 * LO, 4 * C))
         mm(4, C, "ua", 0, xq, 0)
         mm(1, C, "ua", 0, xq, 0)
-        mm(2, LO, "uc", 0, xq, LO)
-        scan(A("zz", 0, LO), A("rst", 0, LO), A("vm", 0, LO), ALU.add, ALU.max)
+        mm(2, C - LO, "uc", 0, xq, LO)
         compare(LOW[0], 0)
+        for t in RV0:
+            red(A("rsum", t, t + 1), row(t), ALU.add)
         tt(A("vm", LO, C), A("ps4", LO, C), A("nm16", LO, C), ALU.add)
         compare(LOW[1], 0)
         scan(A("zz", LO, C), A("rst", LO, C), A("vm", LO, C), ALU.add, ALU.max)
         compare(LOW[2], 0)
+        compare(LOW[3], 4)
         pack(4)
         pack(5)
+        if r == 0:
+            quant("g", 0, 128, A("gt"))
+            ts(A("e4"), A("r4"), col(R4), None, ALU.is_equal)
         for t in SB:
             act(tmp(t), ps(1, 16 * t), ACT.Sign, scale=-1.0, bias=own(t))
-        act(A("vsa", LO, C), ps(2, LO), ACT.Sign)
+        act(A("vsb", LO, C), ps(2, C - LO), ACT.Sign, bias=-TINY)
         for t in SB:
             act(row(t), tmp(t), ACT.Relu, acc=A("rsum", t, t + 1))
-        act(A("vsb", LO, C), A("vsa", LO, C), ACT.Sign, bias=-0.5, acc=K(ACC))
         compare((23, 22), 4)
         tt(A("mt0", 0, 4 * C, 4), ps(4, C), A("zz"), ALU.is_le)
         compare((21,), 4)
@@ -434,63 +442,71 @@ def rank_program(g, core, T, topo):
         sums(3)
         scan(A("dg"), A("rz16"), A("mt0", 0, 4 * C, 4), ALU.mult, ALU.add)
         for t in RV:
-            red(A("rsum", t, t + 1), row(t), ALU.add)
-        scan(A("fj"), A("hh"), A("vsb"), ALU.max, ALU.mult)
+            if t not in RV0:
+                red(A("rsum", t, t + 1), row(t), ALU.add)
         tt(A("ce"), A("k24"), A("dg", 15, C, 16), ALU.subtract)
+        scan(A("fj", 0, FJ), A("hh", 0, FJ), A("vsb", 0, FJ), ALU.max, ALU.mult)
         tt(A("d1", 15, C, 16), A("ce"), A("rsum"), ALU.subtract)
-        act(K(TH), K(ACC), ACT.Identity, scale=0.5, bias=K(AC2))
+        scan(A("fj", FJ, C), A("hh", FJ, C), A("vsb", FJ, C), ALU.max, ALU.mult)
         if r == 0:
             late_constants(1)
+        xp = "xp%d" % r
+        for b in range(4):
+            if r or b < 2:
+                act(A(xp, XW * b, XW * b + C), A(xw, b, 4 * C, 4), ACT.Copy)
         scan(A("ex"), ps(3, C), A("d1"), ALU.max, ALU.add)
         ts(A("pl"), A("ex", 15, C, 16), -1.0, col(CA), ALU.mult, ALU.add)
+        act(A("rf"), A("ex", 15, C, 16), ACT.Identity, scale=-2.0, bias=col(13))
+        act(A("ff", 4, 120, 5), A("ex", 15, C, 16), ACT.Identity, bias=col(14))
         put(A("srt"), A("pl"), A("fj"))
-        top = CUTS[0][2]
-        scan(A("tb", 1, top), A("srt", 0, top - 1), A("c15", 0, top - 1), ALU.add, ALU.add)
+        scan(A("tb", 1, C + 1), A("srt"), A("c15"), ALU.add, ALU.add)
         act(A("t2", 1, 2 * C, 2), A("srt"), ACT.Abs, scale=2.0 ** 24)
-        pick(S, A("ge"), A("t2"), A("pose"))
         tb = A("tb", 0, EO + C + 1)
-        win = A(xw, 0, 4 * NB0)
+        win = A(xw, 0, 4 * XZ)
 
         def eq(o, a, b, c):
             ts(K(o), K(a), K(b), c, ALU.is_equal, ALU.mult)
 
         for m, (mult, lo, hi) in enumerate(CUTS):
             w = hi - lo
-            ts(A("cm", 0, w), A("tb", lo, hi), mult, K(TH), ALU.mult, ALU.is_le)
+            ts(A("cm", 0, w), A("tb", lo, hi), mult, K(TH) if m else A("tb", C, C + 1), ALU.mult, ALU.is_le)
             if m == 1:
                 eq(B2, OWN1, M1, GONE)
+                act(K(X1), K(B2), ACT.Identity, scale=-1.0, bias=col(17))
+            if m == 2:
+                eq(B3, OWN2, M2, GONE)
+                act(K(X3), K(B3), ACT.Identity, scale=-1.0, bias=K(X2))
+            scan(A("cn", 160 * m, 160 * m + w), A("cm", 0, w), A("cm", 0, w), ALU.add, ALU.max)
+            cnt, of = A("cn", 160 * m + w - 1, 160 * m + w), A("of", 2 * m, 2 * m + 2)
+            if m == 0:
+                act(K(OWN1), cnt, ACT.Identity, scale=2.0, bias=col(16))
+                pick(S, A("ge"), A("t2"), A("pose"))
+            if m == 1:
+                act(K(OWN2), cnt, ACT.Identity, scale=2.0, bias=K(X1))
                 act(A("c23"), A("c2", 4, 6), ACT.Identity, bias=K(B2))
                 act(K(X2), K(B2), ACT.Identity, scale=-1.0, bias=col(12))
                 act(K(S1), K(B2), ACT.Copy, scale=2.0 * C / GONE)
-            if m == 2:
-                eq(B3, OWN2, M2, GONE)
-            scan(A("cn", 0, w), A("cm", 0, w), A("cm", 0, w), ALU.add, ALU.max)
-            cnt, of = A("cn", w - 1, w), A("of", 2 * m, 2 * m + 2)
+                act(K(EN2), K(B2), ACT.Identity, scale=K(M1))
+                act(K(EN1), K(EN2), ACT.Copy, scale=1.0 / GONE)
             if m == 0:
                 ts(of, A("c2", 0, 2), cnt, None, ALU.add)
             elif m == 1:
-                eq(EN1, OWN1, M1, K(M1))
+                scan(A("ze"), A("ge"), A("em4", 0, P), ALU.max, ALU.add)
                 ts(of, A("c2", 2, 4), cnt, K(B2), ALU.add, ALU.add)
                 ts(A("l3"), A("ze", 3, P, 4), col(CL1), None, ALU.add)
             else:
-                ts(K(X3), K(B3), -1.0, K(X2), ALU.mult, ALU.add)
+                act(K(OWNB), cnt, ACT.Identity, scale=2.0, bias=K(X3))
+                act(K(E12), K(B3), ACT.Identity, scale=K(M2N), bias=K(EN1))
                 eq(S2, OWN2, M2, K(M1))
                 ts(of, A("c23"), cnt, K(B3), ALU.add, ALU.add)
-                eq(EN2, OWN2, M2, K(M2))
                 ts(K(S12), K(S1), K(S2), K(M2), ALU.max, ALU.max)
             picktt(A("pk"), tb, of, A("krow") if m < 2 else A("krd"), ALU.add if m < 2 else ALU.subtract)
             if m < 2:
-                ts(K(OWN1 + m), A("of", 2 * m, 2 * m + 1), 2.0, col(KC), ALU.mult, ALU.add)
                 red(K(TH), A("pk", 0, 16), ALU.max)
                 red(K(M1 + m), A("pk", 16, 32), ALU.max)
-            if m == 0:
-                scan(A("ze"), A("ge"), A("em4", 0, P), ALU.max, ALU.add)
             if m == 1:
-                act(A("krd", 0, 16), A("krow", 16, 32), ACT.Identity, scale=-1.0, bias=K(M2))
-                pick(S, A("e3", 0, 384), win, A("l3"), scale=0.5)
-                act(A("e3", 384, 768), A("e3", 0, 384), ACT.Copy)
-        ts(K(OWNB), cnt, 2.0, K(X3), ALU.mult, ALU.add)
-        ts(K(E12), K(EN1), K(EN2), None, ALU.max)
+                act(A("krd", 0, 16), A("krd", 16, 32), ACT.Identity, bias=K(M2))
+                act(K(M2N), K(M2), ACT.Copy, scale=1.0 / GONE)
         red(K(M3), A("pk", 16, 32), ALU.max)
         red(K(DD), A("pk", 0, 16), ALU.max)
         ts(A("sx"), A("cs"), K(S12), K(E12), ALU.add, ALU.max)
@@ -498,137 +514,125 @@ def rank_program(g, core, T, topo):
         ts(K(ZZ), K(OWNB), K(M3), K(DD), ALU.is_lt, ALU.mult)
         ts(A("pos"), A("sx"), K(ZZ), K(EN3), ALU.add, ALU.max)
         pick(V, A("g1", 0, 16 * VG), A("t2"), A("pos", 0, VG))
-        pick(S, A("g1", 16 * VG, C), A("t2"), A("pos", VG, 24))
-        bq, lb, hq, lh = "b%d" % r, "lb%d" % r, "h%d" % r, "lh%d" % r
-        NS = len(STAGE)
-        for k in (1, 2, 3):
-            scan(A("x4", P * (k - 1), P * k), A("g1", k, C, 4), A("em4", 0, P), ALU.max, ALU.add)
-        scan(A("x4", R3, C), A("g1", 0, C, 4), A("em4", 0, P), ALU.max, ALU.add)
-        ts(A("l1", 0, 72), A("x4", 3, R3, 4), col(CL1), None, ALU.add)
-        ts(A("l1", 72, 96), A("x4", R3 + 3, C, 4), col(CL1), None, ALU.add)
-        for s, (ks, w, ww, to, lo, io) in enumerate(STAGE):
-            at = P * (ks[0] - 1)
-            if VB[s] < w // 4:
-                pick(S, A("bt", 4 * to + 16 * VB[s], 4 * (to + w)), win, A("l1", at // 4 + VB[s], (at + w) // 4))
-        for s, (ks, w, ww, to, lo, io) in enumerate(STAGE):
-            at = P * (ks[0] - 1)
-            if VB[s]:
-                pick(V, A("bt", 4 * to, 4 * to + 16 * VB[s]), win, A("l1", at // 4, at // 4 + VB[s]))
-            quant(bq, to, to + ww, A("bt", 4 * to, 4 * (to + ww)))
-            send(bq, lb, s, False, "b%d" % r)
-        pick(OWNQ, A("bt", 4 * TW, 4 * (TW + P)), win, A("l1", 72, 96))
+        if VG < 24:
+            pick(S, A("g1", 16 * VG, C), A("t2"), A("pos", VG, 24))
+        bq, hq = "b%d" % r, "h%d" % r
+
+        def offsets(k):
+            at = P * ((k + 3) % 4)
+            scan(A("x4", at, at + P), A("g1", k, C, 4), A("em4", 0, P), ALU.max, ALU.add)
+
+        def listed(s):
+            ts(A("l1", 48 * s, 48 * s + 48), A("x4", W2 * s + 3, W2 * (s + 1), 4), col(CL1), None, ALU.add)
+
+        def slots_by(q, a, b):
+            at = 128 if a >= 72 else 0
+            if a < b:
+                pick(q, A("bt", at + 16 * a, at + 16 * b), win, A("l1", a, b))
+
+        act(K(STF), K(S12), ACT.Identity, bias=K(ZZ))
+        act(K(ENF), K(E12), ACT.Identity, bias=K(EN3))
+        act(K(Y1), K(ENF), ACT.Identity, bias=2.0 * P)
+        act(K(Y2), K(STF), ACT.Relu, scale=-1.0, bias=K(Y1))
+        offsets(1)
+        offsets(2)
+        listed(0)
+        slots_by(S, VB[0], 48)
         if r == 0:
-            act(A("ebt"), A("ebth"), ACT.Copy, scale=2.0)
+            act(A("ebth"), A("ebt"), ACT.Copy, scale=0.5)
+        act(K(LW), K(Y2), ACT.Identity, bias=-2.0 * P)
+        act(K(DIF), K(Y2), ACT.Identity, scale=-1.0, bias=2.0 * P + 0.375)
+        act(K(SUM), K(STF), ACT.Identity, scale=2.0, bias=K(LW))
+        slots_by(V, 0, VB[0])
+        offsets(3)
+        quant(bq, 0, W2, A("bt", 0, 4 * W2))
+        send(0, False, bq)
+        offsets(0)
+        if EFIRST:
+            pick(S, A("e3"), win, A("l3"), scale=0.5)
+        listed(1)
+        slots_by(S, 48 + VB[2], 72)
+        if not EFIRST:
+            pick(S, A("e3"), win, A("l3"), scale=0.5)
+        slots_by(S, 72 + VB[1], 96)
+        slots_by(V, 48, 48 + VB[2])
+        quant(bq, W2, OWN, A("bt", 4 * W2, 4 * OWN))
+        send(1, False, bq)
+        if r == 0:
             for b in range(4):
                 quant("eh", 128 * b, 128 * b + 128, A("ebth", 3 - b, 515 - b))
-            quant(lb, STAGE[0][1], STAGE[0][1] + 128, A("nil"))
-        ts(K(STF), K(S12), K(ZZ), None, ALU.add)
-        ts(K(ENF), K(E12), K(EN3), None, ALU.max)
-        ts(A("rf"), A("ex", 15, C, 16), -1.0, col(CA), ALU.mult, ALU.add)
-        ts(K(LW), K(STF), -2.0 * P, K(ENF), ALU.add, ALU.max)
-        ts(A("o2"), A("k", STF, STF + 2), 0.5, float(EO), ALU.mult, ALU.add)
-        quant(bq, TW, TW + 128, A("bt", 4 * TW, 4 * TW + 512))
+        slots_by(V, 72, 72 + VB[1])
+        quant(bq, R3, OWN + P, A("bt", 4 * R3, 4 * (OWN + P)))
         for b in range(4):
-            mm(b, 128, "eh", 128 * b, bq, TW)
-        ts(A("sl"), tb, 0.5, None, ALU.mult, by=A("o2"))
-        tt(A("cc", 0, 4), A("sl", 0, 4), A("crow"), ALU.add)
-        ts(A("cc", 4, 8), A("cc", 0, 4), -1.0, None, ALU.mult)
-        for b in range(4):
-            tt(A("zt0", b, 384, 4), ps(b, P), A("e3", b, 384, 4), ALU.add)
-        quant("z0", 0, 128, A("zt0"))
+            mm(b, 128, "eh", 128 * b, bq, R3)
+        ts(A("o2", 0, 3), A("k", SUM, SUM + 3), 0.5, None, ALU.mult)
+        ts(A("sl"), A("tb", EO, EO + 2 * C + 2), 0.5, None, ALU.mult, by=A("o2", 0, 3))
+        tt(A("cc", 0, 4), A("sl", 32, 36), A("crow"), ALU.add)
+        for k in range(4):
+            act(A("fa", 24 * k, 24 * k + 24), A("rf"), ACT.Abs, scale=-1.0, bias=A("sl", k, k + 1))
+        for k in range(4):
+            act(A("fb", 24 * k, 24 * k + 24), A("fa", 24 * k, 24 * k + 24), ACT.Sign, scale=-1.0, bias=A("sl", 16 + k, 17 + k))
+        for k in range(4):
+            act(A("ff", k, 120, 5), A("fb", 24 * k, 24 * k + 24), ACT.Relu, scale=A("cc", k, k + 1))
+        if r == 0:
+            for b in (2, 3):
+                act(A(xp, XW * b, XW * b + C), A(xw, b, 4 * C, 4), ACT.Copy)
 
-        def state_list(part):
-            if part == 0:
-                for k in range(4):
-                    ts(A("ff", k, 192, 8), A("rf"), A("sl", 16 + k, 17 + k), A("cc", k, k + 1), ALU.is_ge, ALU.mult)
-                for k in range(4):
-                    ts(A("ff", 4 + k, 192, 8), A("rf"), A("sl", k, k + 1), A("cc", 4 + k, 5 + k), ALU.is_ge, ALU.mult)
-                scan(A("fs"), A("rz8"), A("ff"), ALU.mult, ALU.add)
-                return
-            tt(A("lf"), A("fs", 7, 192, 8), A("rf"), ALU.subtract)
-            tt(A("lg"), A("lf"), A("j24"), ALU.max)
-            cp(A("loc"), A("lg"))
-
-        bank = lambda s: 4 * ((s + 1) % 2)
+        bank = (4, 0)
         pw = lambda b, io, w: A("ps%d" % b, io, io + w)
 
-        def unpack(s, const, src, at):
-            ks, w, ww, to, lo, io = STAGE[s]
+        def make_z(s, parts, io):
             for b in range(4):
-                mm(at + b, ww, const, 128 * b, src, lo - io)
-
-        def make_z(s):
-            ks, w, ww, to, lo, io = STAGE[s]
-            for b in range(4):
-                tt(A("zt", 4 * to + b, 4 * (to + w), 4), pw(bank(s) + b, io, w), A("e3", b, 4 * w, 4), ALU.add)
+                for i in parts:
+                    at = 4 * (W2 * s + P * i)
+                    tt(A("zt", at + b, at + 4 * P, 4), pw(bank[s] + b, io + P * i * (1 - s), P), A("e3", b, 4 * P, 4), ALU.add)
 
         def layer(s):
-            ks, w, ww, to, lo, io = STAGE[s]
-            quant("z", to, to + ww, A("zt", 4 * to, 4 * (to + ww)))
+            quant("z", W2 * s, W2 * (s + 1), A("zt", 4 * W2 * s, 4 * W2 * (s + 1)))
             for b in range(4):
-                mm(bank(s) + b, ww, "w", 128 * b, "z", to)
+                mm(bank[s] + b, W2, "w", 128 * b, "z", W2 * s)
 
         def make_h(s, on_v):
-            ks, w, ww, to, lo, io = STAGE[s]
             for b in range(4):
-                o = A("ht", 4 * to + b, 4 * (to + w), 4)
+                o = A("ht", 4 * W2 * s + b, 4 * W2 * (s + 1), 4)
                 if b in on_v:
-                    ts(o, ps(bank(s) + b, w), 0.03125, None, ALU.mult)
+                    ts(o, ps(bank[s] + b, W2), 0.03125, None, ALU.mult)
                 else:
-                    act(o, ps(bank(s) + b, w), ACT.Copy, scale=0.03125)
+                    act(o, ps(bank[s] + b, W2), ACT.Copy, scale=0.03125)
 
         def back(s):
-            ks, w, ww, to, lo, io = STAGE[s]
-            quant(hq, to, to + ww, A("ht", 4 * to, 4 * (to + ww)))
-            send(hq, lh, s, True, "h%d" % r)
+            at = H_FROM[(1, 0)[s]]
+            quant(hq, at, at + W2, A("ht", 4 * W2 * s, 4 * W2 * (s + 1)))
+            send(s, True, hq)
 
-        unpack(0, "eh", lb, bank(0))
-        unpack(1, "eh", lb, bank(1))
-        make_z(0)
+        make_z(1, (0,), 32)
+        for b in range(4):
+            mm(4 + b, W2, "eh", 128 * b, bq, B_TO[1])
+        for b in range(4):
+            mm(b, 128, "eh", 128 * b, bq, B_TO[3] - 32)
+        make_z(0, (0, 1), 0)
         layer(0)
-        make_z(1)
+        make_z(1, (1,), 32)
         layer(1)
-        if NS == 2:
-            state_list(0)
+        scan(A("fs"), A("rz5"), A("ff"), ALU.mult, ALU.add)
         make_h(0, H0V)
-        if NS == 3:
-            unpack(2, "eh", lb, bank(2))
-            back(0)
-            make_z(2)
-            layer(2)
-            make_h(1, H0V)
-            back(1)
-            state_list(0)
-        else:
-            back(0)
-        ob = bank(NS)
-        for b in range(4):
-            mm(ob + b, 128, "w", 128 * b, "z0", 0)
-        make_h(NS - 1, H1V)
-        back(NS - 1)
-        for b in range(4):
-            act(A("ht0", b, 384, 4), ps(ob + b, P), ACT.Copy, scale=0.03125)
-        state_list(1)
-        pick(S, A("g2"), A("id4"), A("loc"))
+        tt(A("lg"), A("fs", 4, 120, 5), A("j24"), ALU.max)
+        back(0)
+        cp(A("loc"), A("lg"))
+        make_h(1, H1V)
+        back(1)
         if r == 0:
             for b in range(4):
                 quant("e1", 128 * b, 128 * b + 128, A("ebt", 3 - b, 515 - b))
-            quant(lh, STAGE[0][1], STAGE[0][1] + 128, A("nil"))
-        quant("h0k", 0, 128, A("ht0"))
-        for b in range(4):
-            mm(ob + b, 128, "e1", 128 * b, "h0k", 0)
-        base = 4 * NB0
 
-        def renew(s):
-            ks, w, ww, to, lo, io = STAGE[s]
-            at = base + 4 * P * (ks[0] - 1)
-            for b in range(4):
-                tt(A(xw, at + b, at + 4 * w, 4), pw(bank(NS + s + 1) + b, io, w), A("bt", 4 * to + b, 4 * (to + w), 4), ALU.add)
+        def renew(s, b):
+            bk, n_, src, at = ((b, W2, H_TO[1], 0), (4 + b, 128, H_TO[3], W2), (4 + b, 128, H_FROM[0], R3))[s]
+            w, old = W2 if s == 0 else P, OWN if s == 2 else at
+            mm(bk, n_, "e1", 128 * b, hq, src)
+            tt(A(xp, XW * b + NB0 + at, XW * b + NB0 + at + w), ps(bk, w), A("bt", 4 * old + b, 4 * (old + w), 4), ALU.add)
 
-        scan(A("x2"), A("g2"), A("em4"), ALU.max, ALU.add)
         for b in range(4):
-            tt(A(xw, base + 4 * R3 + b, base + 4 * C, 4), ps(ob + b, P), A("bt", 4 * TW + b, 4 * (TW + P), 4), ALU.add)
-        ts(A("l2"), A("x2", 3, C, 4), col(CL2), None, ALU.add)
+            renew(2, b)
         if last:
             pick(S, A("sl2"), A("slt"), A("loc"))
             buf, at = HOME["sl2"]
@@ -638,36 +642,45 @@ def rank_program(g, core, T, topo):
             iota(A("slt", 0, NB0), [[0, NB0]], -1, 0)
             iota(A("slt", NB0, NB0 + R3), [[1, R3]], P, 0)
             iota(A("slt", NB0 + R3, XW), [[1, P]], 0, 0)
-        for s in range(NS):
-            unpack(s, "e1", lh, bank(NS + s + 1))
-            renew(s)
-            if s == 0 and not last:
-                quant("lb1", STAGE[0][1], STAGE[0][1] + 128, A("nil"))
-                quant("lh1", STAGE[0][1], STAGE[0][1] + 128, A("nil"))
         xn, xq = ("xf", "xf") if last else ("xw1", "x1")
-        full = A(xw, 0, 4 * XW)
-        for h in range(2):
-            pick(S, A(xn, 4 * LO * h + 16 * VX[h], 4 * LO * (h + 1)), full, A("l2", 48 * h + VX[h], 48 * (h + 1)))
-        for h in range(2):
-            pick(V, A(xn, 4 * LO * h, 4 * LO * h + 16 * VX[h]), full, A("l2", 48 * h, 48 * h + VX[h]))
-            quant(xq, LO * h, LO * (h + 1), A(xn, 4 * LO * h, 4 * LO * (h + 1)))
+        parts = END if last else VX
+
+        def gather(q, b, lo, hi):
+            pick(q, A(xn, 4 * lo + b, 4 * hi, 4), A(xp, XW * b, XW * (b + 1)), A("loc", lo // 16, hi // 16))
+
+        for s, b in RETURN:
+            renew(s, b)
+        for h, (lo, hi, v) in enumerate(parts):
+            for b in range(4):
+                if lo + v[b] < hi:
+                    gather(S, b, lo + v[b], hi)
+        for h, (lo, hi, v) in enumerate(parts):
+            for b in range(4):
+                if v[b]:
+                    gather(V, b, lo, lo + v[b])
+            quant(xq, lo, hi, A(xn, 4 * lo, 4 * hi))
             if last:
-                mm(3 - h, LO, "v", 0, xq, LO * h)
-                qf = A("qxf", LO * h, LO * (h + 1))
-                dma(SY, T.oc[:, 4 * LO * h:4 * LO * (h + 1)], qf[0].bitcast(dt.uint8), [], [qf[1]])
+                mm(3 - h, hi - lo, "v", 0, xq, lo)
+                qf = A("qxf", lo, hi)
+                dma(SY, T.oc[:, 4 * lo:4 * hi], qf[0].bitcast(dt.uint8), [], [qf[1]])
             elif h == 0:
                 mm(0, LO, "ua", 0, xq, 0)
 
+    RETURN = ((0, 0), (0, 1), (1, 0), (1, 1), (0, 2), (1, 2), (0, 3), (1, 3))
+    END = ((0, 192, (0, 0, 96, 192)), (192, C, (0, 0, 96, 192)))
     one_round(0)
     one_round(1)
 
-    y0, y1 = A("yt", 0, LO), A("yt", LO, C)
-    act(y0, ps(3, LO), ACT.Copy)
-    cp(y1, ps(2, LO))
-    dma(S, T.y[:, 0:LO], y0[0], [], [y0[1]])
-    for k in range(4):
-        dma(SY if k < 2 else S, T.osc[4 * k:4 * k + 4, :], T["sxf"][32 * k:32 * k + 4, :], [], [A("sxf")[1]])
-    dma(SY, T.y[:, LO:C], y1[0], [], [y1[1]])
+    for h, (lo, hi, v) in enumerate(END):
+        y = A("yt", lo, hi)
+        if h == len(END) - 1:
+            for k in range(4):
+                dma(SY if k < 2 else S, T.osc[4 * k:4 * k + 4, :], T["sxf"][32 * k:32 * k + 4, :], [], [A("sxf")[1]])
+            cp(y, ps(3 - h, hi - lo))
+            dma(SY, T.y[:, lo:hi], y[0], [], [y[1]])
+        else:
+            act(y, ps(3 - h, hi - lo), ACT.Copy)
+            dma(S, T.y[:, lo:hi], y[0], [], [y[1]])
     for q in (V, S, PE, G):
         g.sync.wait_ge(T.sem["s" + q], count[q])
     for s in used:

from concourse.bass import DstId, RemoteDMATransfer
from concourse.mybir import dt, AluOpType as ALU, AxisListType, ActivationFunctionType as ACT

C, P = 384, 96
R3 = 3 * P
HALF = R3 // 2
BIG = 2.0 ** 93
XZ = C + 16
NB0 = C
XW = NB0 + C
EO = 400
TOP = 2.0 ** 23
D16, A16 = 1024.0, 14848.0
D4, A4 = 8192.0, 20480.0
CUTS = ((4.0 / 3.0 - 0.00038, 230, 330), (1.5, 114, 264), (2.0, 38, 176))
GONE = -4096.0
TINY = 2.0 ** -120
STAGES = ((1, 2), (3,))
W2 = 2 * P
OWN = 3 * P + 32
B_FROM, B_TO = {1: 0, 2: P, 3: 2 * P, 0: OWN}, {3: OWN + P, 1: OWN + 2 * P, 2: OWN + 3 * P}
H_FROM, H_TO = {1: 0, 2: P, 0: 5 * P, 3: 6 * P}, {1: 2 * P, 2: 3 * P, 3: 4 * P}

SCRATCH = {}
SEMAPHORES = ["sv", "ss", "st", "sp"]
WIDTH = {}
HOME = {}


def _b(name, n, dtype="float32", where="sbuf"):
    SCRATCH[name] = (where, [128, n], dtype)
    WIDTH[name] = n
    HOME[name] = (name, 0)


def _q(name, n):
    _b("q" + name, n, "float8_e4m3fn_x4")
    _b("s" + name, n, "uint8")


def _pack(buf, pieces, dtype="float32"):
    at = 0
    for name, n in pieces:
        WIDTH[name] = n
        HOME[name] = (buf, at)
        at += -(-n // 16) * 16
    SCRATCH[buf] = ("sbuf", [128, at], dtype)


for _i in range(8):
    _b("ps%d" % _i, 512, "float32", "psum")
for _r in range(2):
    _b("xw%d" % _r, 4 * XZ, "bfloat16")
    _b("xp%d" % _r, 4 * XW, "bfloat16")
    for _n, _w in (("x", C), ("b", OWN + 4 * P), ("h", 7 * P)):
        _q("%s%d" % (_n, _r), _w)
    SEMAPHORES += ["lb%d" % _r, "lh%d" % _r] + ["a%s%d_%d" % (_n, _r, _s) for _n in "bh" for _s in range(len(STAGES))]
_b("xf", 4 * C, "bfloat16")
for _n, _w in (("xf", C), ("u", 128), ("ua", 128), ("uc", 128), ("v", 128), ("w", 512), ("e1", 512), ("eh", 512), ("g", 128),
               ("z", C)):
    _q(_n, _w)
for _n, _w in (("ut", 512), ("vt", 512), ("eone", 516), ("ebt", 516), ("ebth", 516), ("gt", 512), ("bt", 4 * (OWN + P)),
               ("e3", 4 * P), ("zt", 4 * C), ("ht", 4 * C), ("jk", 4416), ("sgn", 4416)):
    _b(_n, _w, "bfloat16")
MTN = (384, 320, 256, 192, 128, 128)
for _i in range(6):
    _b("mt%d" % _i, 4 * MTN[_i], "bfloat16")
    _q("m%d" % _i, MTN[_i])
_b("yt", C)
_b("srt", C)
_b("tb", EO + 2 * C + 8)
_b("t2", 2 * C)
_pack("cb", [(_n, C) for _n in ("r16", "nm16", "rst", "rz16")] + [("g64", 512), ("rz5", 120), ("r4", P), ("e4", P)], "bfloat16")
_pack("consts", [(_n, C) for _n in ("hh", "ij", "c15")] + [("slt", XW), ("em4", P)]
      + [(_n, 24) for _n in ("k24", "ct", "cs", "j24", "st", "j16")]
      + [("cols", 24), ("krow", 32), ("kr", 16), ("c2", 8), ("crow", 4), ("il", 8), ("pe", 6)])
_pack("wide", [(_n, C) for _n in ("vm", "zz", "d1", "ex", "fj", "g1", "x4", "g2", "x2", "sl2")]
      + [("ge", P), ("ze", P), ("ff", 120), ("fs", 120), ("fa", P), ("fb", P)])
_pack("wb", [("vsa", C), ("vsb", C), ("dg", C), ("cm", 160), ("cn", 480), ("kb", 16)], "bfloat16")
_pack("small", [(_n, 24) for _n in ("rsum", "ce", "rf", "sx", "lf", "lg")] + [("pk", 32), ("krd", 32), ("sl", 48), ("c23", 2), ("cc", 8)]
      + [("k", 40)])
_b("icol", 16, "int32")
for _n, _w in (("ula", 8), ("ulc", 8), ("pl", 24), ("of", 8), ("pos", 24), ("pose", 6), ("l1", 96), ("l2", 96), ("l3", 24), ("o2", 4), ("loc", 24)):
    _b(_n, _w, "uint16")
NDMA = 24
SEMAPHORES += ["d%d" % _i for _i in range(NDMA)]


def rank_program(g, core, T, topo):
    rank = T.rank_of(core)
    if rank is None:
        return
    V, S, PE, G, SY = "v", "s", "t", "p", "y"
    eng = {V: g.vector, S: g.scalar, PE: g.tensor, G: g, SY: g.sync}
    count = {V: 0, S: 0, PE: 0, G: 0}
    clock = {q: {} for q in eng}
    evclock = {}
    hist = {}
    used = []

    def A(n, lo=None, hi=None, st=1):
        if lo is None:
            lo, hi = 0, WIDTH[n]
        buf, at = HOME[n]
        lo, hi = lo + at, hi + at
        return (T[buf][:, lo:hi] if st == 1 else T[buf][:, lo:hi:st], (buf, lo, hi, st))

    def meet(a, b):
        if a[0].startswith("ps"):
            return True
        if a[2] <= b[1] or b[2] <= a[1]:
            return False
        if a[3] == b[3] and a[3] > 1 and (a[1] - b[1]) % a[3]:
            return False
        return True

    def need(q, outs, ins):
        want = {}
        for kind, regs in (("w", outs), ("r", ins)):
            for r in regs:
                for (r2, k2, ev) in hist.get(r[0], ()):
                    bank = r[0].startswith("ps") and ev[2] != q
                    if (kind == "w" or k2 == "w" or bank) and meet(r, r2):
                        want[ev[0]] = max(want.get(ev[0], 0), ev[1])
        ck = clock[q]
        for s in sorted(want):
            n = want[s]
            if ck.get(s, 0) >= n:
                continue
            eng[q].wait_ge(T.sem[s], n)
            ck[s] = n
            for s2, n2 in evclock.get((s, n), {}).items():
                ck[s2] = max(ck.get(s2, 0), n2)

    def note(outs, ins, ev):
        for r in outs:
            h = hist.setdefault(r[0], [])
            if r[3] == 1:
                h[:] = [e for e in h if not (e[0][1] >= r[1] and e[0][2] <= r[2])]
            h.append((r, "w", ev))
        for r in ins:
            hist.setdefault(r[0], []).append((r, "r", ev))

    def op(q, fn, outs, ins):
        need(q, outs, ins)
        count[q] += 1
        s = "s" + q
        fn(eng[q]).then_inc(T.sem[s], 1)
        evclock[(s, count[q])] = dict(clock[q])
        note(outs, ins, (s, count[q], q))

    def dma(q, out, in_, outs, ins):
        need(q, outs, ins)
        s = "d%d" % len(used)
        used.append(s)
        eng[q].dma_start(out, in_).then_inc(T.sem[s], 16)
        evclock[(s, 16)] = dict(clock[q])
        note(outs, ins, (s, 16, s))

    def sc(x):
        return (x[0], [x[1]]) if isinstance(x, tuple) else (x, [])

    def ts(o, i, s1, s2, op0, op1=None, by=None):
        a, ra = sc(s1)
        b, rb = sc(s2)
        x = i[0] if by is None else i[0].indirect(by[0])
        ins = [i[1]] + ra + rb + ([] if by is None else [by[1]])
        if op1 is None:
            op(V, lambda e: e.tensor_scalar(o[0], x, a, None, op0), [o[1]], ins)
        else:
            op(V, lambda e: e.tensor_scalar(o[0], x, a, b, op0, op1), [o[1]], ins)

    def tt(o, i, j, o_):
        op(V, lambda e: e.tensor_tensor(o[0], i[0], j[0], o_), [o[1]], [i[1], j[1]])

    def scan(o, i, j, a, b):
        op(V, lambda e: e.tensor_tensor_scan(o[0], i[0], j[0], 0.0, a, b), [o[1]], [i[1], j[1]])

    def red(o, i, o_):
        op(V, lambda e: e.tensor_reduce(o[0], i[0], AxisListType.X, o_), [o[1]], [i[1]])

    def cp(o, i):
        op(V, lambda e: e.tensor_copy(o[0], i[0]), [o[1]], [i[1]])

    def ms(o, c):
        op(V, lambda e: e.memset(o[0], c), [o[1]], [])

    def act(o, i, f, scale=1.0, bias=None, acc=None):
        scale, rs = sc(scale)
        kw, outs, ins = {"scale": scale}, [o[1]], [i[1]] + rs
        if bias is not None:
            kw["bias"], rb = sc(bias)
            ins = ins + rb
        if acc is not None:
            kw["accum_out"] = acc[0]
            outs = outs + [acc[1]]
        op(S, lambda e: e.activation(o[0], i[0], f, **kw), outs, ins)

    def pick(q, o, w, l, scale=1.0):
        x = w[0].indirect(l[0])
        if q == V:
            op(V, lambda e: e.tensor_copy(o[0], x), [o[1]], [w[1], l[1]])
        elif scale == 1.0:
            op(S, lambda e: e.activation(o[0], x, ACT.Copy), [o[1]], [w[1], l[1]])
        else:
            op(S, lambda e: e.activation(o[0], x, ACT.Copy, scale=scale), [o[1]], [w[1], l[1]])

    def picktt(o, w, l, j, o_):
        x = w[0].indirect(l[0])
        op(V, lambda e: e.tensor_tensor(o[0], x, j[0], o_), [o[1]], [w[1], l[1], j[1]])

    def put(w, l, i):
        x = w[0].indirect(l[0])
        op(V, lambda e: e.tensor_copy(x, i[0]), [w[1]], [l[1], i[1]])

    def quant(n, lo, hi, i):
        o, s = A("q" + n, lo, hi), A("s" + n, lo, hi)
        op(V, lambda e: e.quantize_mx(o[0], s[0], i[0]), [o[1], s[1]], [i[1]])

    def mm(bank, n, ln, llo, rn, rlo, start=True, stop=True):
        o = A("ps%d" % bank, 0, n)
        l, ls = A("q" + ln, llo, llo + 128), A("s" + ln, llo, llo + 128)
        r, rs = A("q" + rn, rlo, rlo + n), A("s" + rn, rlo, rlo + n)
        ins = [l[1], ls[1], r[1], rs[1]]
        op(PE, lambda e: e.matmul_mx(o[0], l[0], ls[0], r[0], rs[0], start, stop), [o[1]] if start else [], ins)
        if not start:
            note([o[1]], [], ("st", count[PE], PE))

    def iota(o, pattern, base, cm):
        op(G, lambda e: e.iota(o[0], pattern, base, cm, allow_small_or_imprecise_dtypes=True), [o[1]], [])

    def asel(o, i, pattern, cmp, base, cm):
        op(G, lambda e: e.affine_select(o[0], i[0], pattern, cmp, 0.0, base, cm), [o[1]], [i[1]])

    def load(q, name, lo, hi, src):
        a = A(name, lo, hi)
        dma(q, a[0], src, [a[1]], [])

    load(S, "ut", 0, 512, T.u[:])
    LO = 192
    load(SY, "xw0", 0, 4 * LO, T.x[:, 0:4 * LO])
    load(SY, "xw0", 4 * LO, 4 * C, T.x[:, 4 * LO:4 * C])
    need(SY, [], [A("xw0", 0, 4 * C)[1]])
    wq = A("qw")
    dma(SY, wq[0].bitcast(dt.uint8), T.wc[:], [wq[1]], [])
    load(SY, "sw", 0, 512, T.ws[:])
    load(SY, "vt", 0, 512, T.v[:])

    icol = lambda k: A("icol", k, k + 1)
    col = lambda k: A("cols", k, k + 1)
    Q16, Q4, R4, PG, CA, KC, CL1, CL2 = 1, 2, 3, 4, 5, 6, 7, 8
    op(G, lambda e: e.iota(icol(0)[0], [[1, 1]], 0, 1), [icol(0)[1]], [])
    iota(A("il"), [[16, 8]], 0, 0)
    iota(A("r16"), [[0, 24], [1, 16]], 0, 0)
    iota(A("ij"), [[1, C]], 0, 0)
    iota(A("j16"), [[16, 24]], 0, 0)
    iota(A("g64"), [[1, 8], [0, 64]], 0, 0)
    iota(A("r4"), [[0, 24], [1, 4]], 0, 0)
    tail = lambda i: A("mt%d" % i, 4 * (336 - 64 * i), 4 * MTN[i])
    for i in (1, 0, 2):
        iota(tail(i), [[0, 192]], 0, 0)
    iota(A("kr"), [[0, 4], [-1, 4]], 3, 0)
    iota(A("c15"), [[0, C]], 3, 0)
    iota(A("rz5"), [[0, 24], [1, 5]], 0, 0)
    iota(A("tb", EO, EO + C + 1), [[2, C + 1]], 0, 0)
    iota(A("c2", 0, 2), [[EO, 2]], CUTS[0][1] - 1, 0)
    iota(A("c2", 2, 4), [[EO, 2]], CUTS[1][1] - 1, 0)
    iota(A("c2", 4, 6), [[0, 2]], EO + CUTS[2][1] - 1, 0)
    iota(A("t2", 0, 2 * C, 2), [[0, C]], int(TOP) + 4 * C, 0)
    iota(A("xw0", 4 * C, 4 * XZ), [[0, 64]], 0, 0)
    iota(A("eone"), [[0, 516]], 1, 0)
    asel(A("ebt"), A("eone"), [[1, 516]], ALU.is_equal, -3, -4)
    iota(A("tb", EO + C + 1, EO + 2 * C + 2), [[2, C + 1]], 2 * C + 2, 0)
    iota(A("bt", 4 * R3, 4 * OWN), [[0, 128]], 0, 0)
    iota(A("xw1", 4 * C, 4 * XZ), [[0, 64]], 0, 0)
    iota(A("crow", 0, 1), [[0, 1]], NB0 + R3 - 1, 0)
    iota(A("crow", 1, 4), [[P, 3]], NB0 - 1, 0)

    ts(icol(Q16), icol(0), 15, None, ALU.bitwise_and)
    ts(icol(Q4), icol(0), 3, None, ALU.bitwise_and)
    ts(icol(R4), icol(0), 2, 3, ALU.logical_shift_right, ALU.bitwise_and)
    ts(icol(PG), icol(0), 4, None, ALU.logical_shift_right)
    cp(A("cols", 1, 5), A("icol", 1, 5))
    ts(A("ula"), A("il"), 4.0, None, ALU.add)
    ts(A("ulc"), A("il"), col(Q4), None, ALU.add)
    for i in (3, 4, 5):
        ms(tail(i), 0.0)
    ms(A("rsum", 0, 1), 0.0)
    ms(A("tb", 0, 1), 0.0)
    ms(A("krow", 0, 16), 1.0 / 6.0)
    ts(col(CA), col(Q16), D16, A16 - 15 * D16, ALU.mult, ALU.add)
    ts(col(KC), col(Q4), -0.125, 0.375, ALU.mult, ALU.add)
    ts(col(9), col(R4), -2.0, -1.0, ALU.mult, ALU.add)
    ts(col(10), col(R4), -D4, 3 * D4 - A4 - TOP, ALU.mult, ALU.add)
    ts(col(11), col(Q16), -1.0, -368.0 - D16, ALU.mult, ALU.add)
    ts(col(12), col(KC), 2.0 * (CUTS[2][1] - 1), None, ALU.add)
    ts(col(15), col(Q16), 14.5, A16 + D16, ALU.is_gt, ALU.mult)
    ts(A("nm16"), A("r16"), col(Q16), -BIG, ALU.not_equal, ALU.mult)
    ts(A("rst"), A("r16"), 0.0, -2 * BIG, ALU.is_equal, ALU.mult)
    quant("u", 0, 128, A("ut"))

    def u_columns(n):
        ul, qa, qb = A("ul" + n), A("qu" + n), A("qu")
        op(V, lambda e: e.tensor_copy(qa[0].bitcast(dt.uint32), qb[0].bitcast(dt.uint32).indirect(ul[0])), [qa[1]], [qb[1], ul[1]])
        pick(S, A("su" + n), A("su"), ul)

    act(A("rz16"), A("r16"), ACT.Sign)
    act(A("d1"), A("nm16"), ACT.Identity, scale=(A16 + D16) / BIG, bias=A16)
    act(A("hh"), A("ij"), ACT.Identity, scale=2.0 ** -22, bias=0.5)
    u_columns("a")

    def late_constants(k):
        if k == 0:
            u_columns("c")
            act(A("g64"), A("g64"), ACT.Abs, scale=-1.0, bias=col(PG))
            act(A("gt"), A("g64"), ACT.Relu, scale=-1.0, bias=1.0)
            ts(A("j24"), A("j16"), col(Q16), None, ALU.add)
            ts(A("k24"), A("j16"), col(11), col(15), ALU.add, ALU.add)
            ts(A("pose"), A("j24", 0, 6), -2.0, 2.0 * C - 1.0, ALU.mult, ALU.add)
        if k == 1:
            act(A("c15"), A("c15"), ACT.Copy, scale=0.5)
            act(A("em4"), A("e4"), ACT.Identity, scale=A4 + D4, bias=-D4)
            act(A("krd", 16, 32), A("kr"), ACT.Copy, scale=-0.125)
            act(A("cs"), A("j16"), ACT.Identity, scale=-0.5, bias=col(9))
            act(col(CL1), col(10), ACT.Identity, bias=col(Q4))
            act(A("krow", 16, 32), A("kr"), ACT.Copy, scale=0.125)
            act(A("rz5"), A("rz5"), ACT.Sign)
            act(col(13), col(CA), ACT.Identity, scale=2.0, bias=1.0)
            act(col(14), col(CA), ACT.Copy, scale=-1.0)
            for m in range(2):
                act(col(16 + m), col(KC), ACT.Identity, bias=2.0 * (CUTS[m][1] - 1))

    cores = list(T.cores)
    n = len(cores)
    peers = [cores[(rank + k) % n] for k in range(1, n)]
    E = topo.engines(core, peers[0])
    NARR = 2 * len(E)

    def send(s, back, sem):
        ks, src, dst = STAGES[s], sem, sem
        to, lo, w = (H_FROM if back else B_FROM)[ks[0]], (H_TO if back else B_TO)[ks[0]], P * len(ks)
        need(G, [], [A("q" + src, to, to + w)[1], A("s" + src, to, to + w)[1]])
        for kind in "qs":
            tr = []
            for i, k in enumerate(ks):
                c = cores[(rank - k) % n] if back else cores[(rank + k) % n]
                a = T[kind + src][:, to + P * i:to + P * (i + 1)]
                b = T[kind + dst][:, lo + P * i:lo + P * (i + 1)]
                if kind == "q":
                    a, b = a.bitcast(dt.uint8), b.bitcast(dt.uint8)
                rid, pid, _ = topo.addr(c)
                mask = sum(1 << e for e in E[i::len(ks)])
                tr.append(RemoteDMATransfer(dst_ids=[DstId(rid=rid, pnc=pid)], dma_engine_mask=mask, remote_sem=T.sem["a%s_%d" % (sem, s)], src=a, dst=b))
            g.remote_dma_fused(tr, local_sem=T.sem["l" + sem])
        note([A("q" + dst, lo, lo + w)[1], A("s" + dst, lo, lo + w)[1]], [], ("a%s_%d" % (sem, s), NARR, "far"))

    ps = lambda b, m: A("ps%d" % b, 0, m)
    slots = {}
    for i, t in enumerate([None] + list(range(23, 0, -1))):
        slots[t] = (i // 4, i % 4)
    jk = [0]
    for t in range(1, 24):
        jk.append(jk[-1] + 16 * t)
    K = lambda i: A("kb", i, i + 1) if i in (9, 10) else A("k", i, i + 1)
    ACC, TH, M1, M2, M3, OWN1, OWN2, OWN3, OWNB, B2, B3, EN1, EN2, S1, S2, S12, E12, DD, ZZ, EN3, SUM, DIF, STF, LW, ENF, X1, X2, X3, Y1, Y2, M2N = range(31)
    SB = (19, 18, 17)
    FJ = 256
    RV0 = ()
    RV = (1, 2, 3, 4, 5)
    LOW = ((11, 10, 9, 8, 7), (6, 5), (4, 3, 2, 1), ())
    VG = 14
    VX = ((0, LO, (0, 0, 96, 192)), (LO, C, (0, 0, 96, 192)))
    EFIRST = True
    VB = (26, 0, 24)
    H0V, H1V = (2, 3), (2, 3)

    def one_round(r):
        xw, last = "xw%d" % r, r == 1
        xq = "x%d" % r
        if r == 0:
            quant(xq, 0, LO, A(xw, 0, 4 * LO))
            mm(0, LO, "ua", 0, xq, 0)
            late_constants(0)
        mm(5, LO, "uc", 0, xq, 0)
        act(A("vsb", 0, LO), ps(5, LO), ACT.Sign, bias=-TINY)
        own = lambda t: A("zz", 16 * t + 15, 16 * t + 16)
        row = lambda t: A("mt%d" % slots[t][0], slots[t][1], 64 * t, 4)
        tmp = lambda t: A("sgn", jk[t - 1], jk[t - 1] + 16 * t)

        def compare(ts_, bank):
            for t in ts_:
                if t in SB:
                    continue
                ts(row(t), ps(bank, 16 * t), own(t), None, ALU.is_lt)
                if t not in RV:
                    act(A("jk", jk[t - 1], jk[t - 1] + 16 * t), row(t), ACT.Copy, acc=A("rsum", t, t + 1))

        def pack(i):
            quant("m%d" % i, 0, MTN[i], A("mt%d" % i))

        def sums(i):
            mm(3, MTN[i], "g", 0, "m%d" % i, 0, i == 0, i == 3)

        tt(A("vm", 0, LO), ps(0, LO), A("nm16", 0, LO), ALU.add)
        scan(A("zz", 0, LO), A("rst", 0, LO), A("vm", 0, LO), ALU.add, ALU.max)
        if r == 0:
            quant(xq, LO, C, A(xw, 4 * LO, 4 * C))
        mm(4, C, "ua", 0, xq, 0)
        mm(1, C, "ua", 0, xq, 0)
        mm(2, C - LO, "uc", 0, xq, LO)
        compare(LOW[0], 0)
        for t in RV0:
            red(A("rsum", t, t + 1), row(t), ALU.add)
        tt(A("vm", LO, C), A("ps4", LO, C), A("nm16", LO, C), ALU.add)
        compare(LOW[1], 0)
        scan(A("zz", LO, C), A("rst", LO, C), A("vm", LO, C), ALU.add, ALU.max)
        compare(LOW[2], 0)
        compare(LOW[3], 4)
        pack(4)
        pack(5)
        if r == 0:
            quant("g", 0, 128, A("gt"))
            ts(A("e4"), A("r4"), col(R4), None, ALU.is_equal)
        for t in SB:
            act(tmp(t), ps(1, 16 * t), ACT.Sign, scale=-1.0, bias=own(t))
        act(A("vsb", LO, C), ps(2, C - LO), ACT.Sign, bias=-TINY)
        for t in SB:
            act(row(t), tmp(t), ACT.Relu, acc=A("rsum", t, t + 1))
        compare((23, 22), 4)
        tt(A("mt0", 0, 4 * C, 4), ps(4, C), A("zz"), ALU.is_le)
        compare((21,), 4)
        compare([t for t in (20, 19, 18, 17) if t not in SB] + [16], 4)
        pack(0)
        for i in (0, 4, 5):
            sums(i)
        compare((15, 14, 13, 12), 4)
        pack(2)
        sums(2)
        pack(1)
        sums(1)
        pack(3)
        sums(3)
        scan(A("dg"), A("rz16"), A("mt0", 0, 4 * C, 4), ALU.mult, ALU.add)
        for t in RV:
            if t not in RV0:
                red(A("rsum", t, t + 1), row(t), ALU.add)
        tt(A("ce"), A("k24"), A("dg", 15, C, 16), ALU.subtract)
        scan(A("fj", 0, FJ), A("hh", 0, FJ), A("vsb", 0, FJ), ALU.max, ALU.mult)
        tt(A("d1", 15, C, 16), A("ce"), A("rsum"), ALU.subtract)
        scan(A("fj", FJ, C), A("hh", FJ, C), A("vsb", FJ, C), ALU.max, ALU.mult)
        if r == 0:
            late_constants(1)
        xp = "xp%d" % r
        for b in range(4):
            if r or b < 2:
                act(A(xp, XW * b, XW * b + C), A(xw, b, 4 * C, 4), ACT.Copy)
        scan(A("ex"), ps(3, C), A("d1"), ALU.max, ALU.add)
        ts(A("pl"), A("ex", 15, C, 16), -1.0, col(CA), ALU.mult, ALU.add)
        act(A("rf"), A("ex", 15, C, 16), ACT.Identity, scale=-2.0, bias=col(13))
        act(A("ff", 4, 120, 5), A("ex", 15, C, 16), ACT.Identity, bias=col(14))
        put(A("srt"), A("pl"), A("fj"))
        scan(A("tb", 1, C + 1), A("srt"), A("c15"), ALU.add, ALU.add)
        act(A("t2", 1, 2 * C, 2), A("srt"), ACT.Abs, scale=2.0 ** 24)
        tb = A("tb", 0, EO + C + 1)
        win = A(xw, 0, 4 * XZ)

        def eq(o, a, b, c):
            ts(K(o), K(a), K(b), c, ALU.is_equal, ALU.mult)

        for m, (mult, lo, hi) in enumerate(CUTS):
            w = hi - lo
            ts(A("cm", 0, w), A("tb", lo, hi), mult, K(TH) if m else A("tb", C, C + 1), ALU.mult, ALU.is_le)
            if m == 1:
                eq(B2, OWN1, M1, GONE)
                act(K(X1), K(B2), ACT.Identity, scale=-1.0, bias=col(17))
            if m == 2:
                eq(B3, OWN2, M2, GONE)
                act(K(X3), K(B3), ACT.Identity, scale=-1.0, bias=K(X2))
            scan(A("cn", 160 * m, 160 * m + w), A("cm", 0, w), A("cm", 0, w), ALU.add, ALU.max)
            cnt, of = A("cn", 160 * m + w - 1, 160 * m + w), A("of", 2 * m, 2 * m + 2)
            if m == 0:
                act(K(OWN1), cnt, ACT.Identity, scale=2.0, bias=col(16))
                pick(S, A("ge"), A("t2"), A("pose"))
            if m == 1:
                act(K(OWN2), cnt, ACT.Identity, scale=2.0, bias=K(X1))
                act(A("c23"), A("c2", 4, 6), ACT.Identity, bias=K(B2))
                act(K(X2), K(B2), ACT.Identity, scale=-1.0, bias=col(12))
                act(K(S1), K(B2), ACT.Copy, scale=2.0 * C / GONE)
                act(K(EN2), K(B2), ACT.Identity, scale=K(M1))
                act(K(EN1), K(EN2), ACT.Copy, scale=1.0 / GONE)
            if m == 0:
                ts(of, A("c2", 0, 2), cnt, None, ALU.add)
            elif m == 1:
                scan(A("ze"), A("ge"), A("em4", 0, P), ALU.max, ALU.add)
                ts(of, A("c2", 2, 4), cnt, K(B2), ALU.add, ALU.add)
                ts(A("l3"), A("ze", 3, P, 4), col(CL1), None, ALU.add)
            else:
                act(K(OWNB), cnt, ACT.Identity, scale=2.0, bias=K(X3))
                act(K(E12), K(B3), ACT.Identity, scale=K(M2N), bias=K(EN1))
                eq(S2, OWN2, M2, K(M1))
                ts(of, A("c23"), cnt, K(B3), ALU.add, ALU.add)
                ts(K(S12), K(S1), K(S2), K(M2), ALU.max, ALU.max)
            picktt(A("pk"), tb, of, A("krow") if m < 2 else A("krd"), ALU.add if m < 2 else ALU.subtract)
            if m < 2:
                red(K(TH), A("pk", 0, 16), ALU.max)
                red(K(M1 + m), A("pk", 16, 32), ALU.max)
            if m == 1:
                act(A("krd", 0, 16), A("krd", 16, 32), ACT.Identity, bias=K(M2))
                act(K(M2N), K(M2), ACT.Copy, scale=1.0 / GONE)
        red(K(M3), A("pk", 16, 32), ALU.max)
        red(K(DD), A("pk", 0, 16), ALU.max)
        ts(A("sx"), A("cs"), K(S12), K(E12), ALU.add, ALU.max)
        eq(EN3, OWNB, M3, K(M3))
        ts(K(ZZ), K(OWNB), K(M3), K(DD), ALU.is_lt, ALU.mult)
        ts(A("pos"), A("sx"), K(ZZ), K(EN3), ALU.add, ALU.max)
        pick(V, A("g1", 0, 16 * VG), A("t2"), A("pos", 0, VG))
        if VG < 24:
            pick(S, A("g1", 16 * VG, C), A("t2"), A("pos", VG, 24))
        bq, hq = "b%d" % r, "h%d" % r

        def offsets(k):
            at = P * ((k + 3) % 4)
            scan(A("x4", at, at + P), A("g1", k, C, 4), A("em4", 0, P), ALU.max, ALU.add)

        def listed(s):
            ts(A("l1", 48 * s, 48 * s + 48), A("x4", W2 * s + 3, W2 * (s + 1), 4), col(CL1), None, ALU.add)

        def slots_by(q, a, b):
            at = 128 if a >= 72 else 0
            if a < b:
                pick(q, A("bt", at + 16 * a, at + 16 * b), win, A("l1", a, b))

        act(K(STF), K(S12), ACT.Identity, bias=K(ZZ))
        act(K(ENF), K(E12), ACT.Identity, bias=K(EN3))
        act(K(Y1), K(ENF), ACT.Identity, bias=2.0 * P)
        act(K(Y2), K(STF), ACT.Relu, scale=-1.0, bias=K(Y1))
        offsets(1)
        offsets(2)
        listed(0)
        slots_by(S, VB[0], 48)
        if r == 0:
            act(A("ebth"), A("ebt"), ACT.Copy, scale=0.5)
        act(K(LW), K(Y2), ACT.Identity, bias=-2.0 * P)
        act(K(DIF), K(Y2), ACT.Identity, scale=-1.0, bias=2.0 * P + 0.375)
        act(K(SUM), K(STF), ACT.Identity, scale=2.0, bias=K(LW))
        slots_by(V, 0, VB[0])
        offsets(3)
        quant(bq, 0, W2, A("bt", 0, 4 * W2))
        send(0, False, bq)
        offsets(0)
        if EFIRST:
            pick(S, A("e3"), win, A("l3"), scale=0.5)
        listed(1)
        slots_by(S, 48 + VB[2], 72)
        if not EFIRST:
            pick(S, A("e3"), win, A("l3"), scale=0.5)
        slots_by(S, 72 + VB[1], 96)
        slots_by(V, 48, 48 + VB[2])
        quant(bq, W2, OWN, A("bt", 4 * W2, 4 * OWN))
        send(1, False, bq)
        if r == 0:
            for b in range(4):
                quant("eh", 128 * b, 128 * b + 128, A("ebth", 3 - b, 515 - b))
        slots_by(V, 72, 72 + VB[1])
        quant(bq, R3, OWN + P, A("bt", 4 * R3, 4 * (OWN + P)))
        for b in range(4):
            mm(b, 128, "eh", 128 * b, bq, R3)
        ts(A("o2", 0, 3), A("k", SUM, SUM + 3), 0.5, None, ALU.mult)
        ts(A("sl"), A("tb", EO, EO + 2 * C + 2), 0.5, None, ALU.mult, by=A("o2", 0, 3))
        tt(A("cc", 0, 4), A("sl", 32, 36), A("crow"), ALU.add)
        for k in range(4):
            act(A("fa", 24 * k, 24 * k + 24), A("rf"), ACT.Abs, scale=-1.0, bias=A("sl", k, k + 1))
        for k in range(4):
            act(A("fb", 24 * k, 24 * k + 24), A("fa", 24 * k, 24 * k + 24), ACT.Sign, scale=-1.0, bias=A("sl", 16 + k, 17 + k))
        for k in range(4):
            act(A("ff", k, 120, 5), A("fb", 24 * k, 24 * k + 24), ACT.Relu, scale=A("cc", k, k + 1))
        if r == 0:
            for b in (2, 3):
                act(A(xp, XW * b, XW * b + C), A(xw, b, 4 * C, 4), ACT.Copy)

        bank = (4, 0)
        pw = lambda b, io, w: A("ps%d" % b, io, io + w)

        def make_z(s, parts, io):
            for b in range(4):
                for i in parts:
                    at = 4 * (W2 * s + P * i)
                    tt(A("zt", at + b, at + 4 * P, 4), pw(bank[s] + b, io + P * i * (1 - s), P), A("e3", b, 4 * P, 4), ALU.add)

        def layer(s):
            quant("z", W2 * s, W2 * (s + 1), A("zt", 4 * W2 * s, 4 * W2 * (s + 1)))
            for b in range(4):
                mm(bank[s] + b, W2, "w", 128 * b, "z", W2 * s)

        def make_h(s, on_v):
            for b in range(4):
                o = A("ht", 4 * W2 * s + b, 4 * W2 * (s + 1), 4)
                if b in on_v:
                    ts(o, ps(bank[s] + b, W2), 0.03125, None, ALU.mult)
                else:
                    act(o, ps(bank[s] + b, W2), ACT.Copy, scale=0.03125)

        def back(s):
            at = H_FROM[(1, 0)[s]]
            quant(hq, at, at + W2, A("ht", 4 * W2 * s, 4 * W2 * (s + 1)))
            send(s, True, hq)

        make_z(1, (0,), 32)
        for b in range(4):
            mm(4 + b, W2, "eh", 128 * b, bq, B_TO[1])
        for b in range(4):
            mm(b, 128, "eh", 128 * b, bq, B_TO[3] - 32)
        make_z(0, (0, 1), 0)
        layer(0)
        make_z(1, (1,), 32)
        layer(1)
        scan(A("fs"), A("rz5"), A("ff"), ALU.mult, ALU.add)
        make_h(0, H0V)
        tt(A("lg"), A("fs", 4, 120, 5), A("j24"), ALU.max)
        back(0)
        cp(A("loc"), A("lg"))
        make_h(1, H1V)
        back(1)
        if r == 0:
            for b in range(4):
                quant("e1", 128 * b, 128 * b + 128, A("ebt", 3 - b, 515 - b))

        def renew(s, b):
            bk, n_, src, at = ((b, W2, H_TO[1], 0), (4 + b, 128, H_TO[3], W2), (4 + b, 128, H_FROM[0], R3))[s]
            w, old = W2 if s == 0 else P, OWN if s == 2 else at
            mm(bk, n_, "e1", 128 * b, hq, src)
            tt(A(xp, XW * b + NB0 + at, XW * b + NB0 + at + w), ps(bk, w), A("bt", 4 * old + b, 4 * (old + w), 4), ALU.add)

        for b in range(4):
            renew(2, b)
        if last:
            pick(S, A("sl2"), A("slt"), A("loc"))
            buf, at = HOME["sl2"]
            dma(SY, T.sl[:], T[buf][0:128:16, at:at + C], [], [A("sl2")[1]])
        else:
            quant("v", 0, 128, A("vt"))
            iota(A("slt", 0, NB0), [[0, NB0]], -1, 0)
            iota(A("slt", NB0, NB0 + R3), [[1, R3]], P, 0)
            iota(A("slt", NB0 + R3, XW), [[1, P]], 0, 0)
        xn, xq = ("xf", "xf") if last else ("xw1", "x1")
        parts = END if last else VX

        def gather(q, b, lo, hi):
            pick(q, A(xn, 4 * lo + b, 4 * hi, 4), A(xp, XW * b, XW * (b + 1)), A("loc", lo // 16, hi // 16))

        for s, b in RETURN:
            renew(s, b)
        for h, (lo, hi, v) in enumerate(parts):
            for b in range(4):
                if lo + v[b] < hi:
                    gather(S, b, lo + v[b], hi)
        for h, (lo, hi, v) in enumerate(parts):
            for b in range(4):
                if v[b]:
                    gather(V, b, lo, lo + v[b])
            quant(xq, lo, hi, A(xn, 4 * lo, 4 * hi))
            if last:
                mm(3 - h, hi - lo, "v", 0, xq, lo)
                qf = A("qxf", lo, hi)
                dma(SY, T.oc[:, 4 * lo:4 * hi], qf[0].bitcast(dt.uint8), [], [qf[1]])
            elif h == 0:
                mm(0, LO, "ua", 0, xq, 0)

    RETURN = ((0, 0), (0, 1), (1, 0), (1, 1), (0, 2), (1, 2), (0, 3), (1, 3))
    END = ((0, 192, (0, 0, 96, 192)), (192, C, (0, 0, 96, 192)))
    one_round(0)
    one_round(1)

    for h, (lo, hi, v) in enumerate(END):
        y = A("yt", lo, hi)
        if h == len(END) - 1:
            for k in range(4):
                dma(SY if k < 2 else S, T.osc[4 * k:4 * k + 4, :], T["sxf"][32 * k:32 * k + 4, :], [], [A("sxf")[1]])
            cp(y, ps(3 - h, hi - lo))
            dma(SY, T.y[:, lo:hi], y[0], [], [y[1]])
        else:
            act(y, ps(3 - h, hi - lo), ACT.Copy)
            dma(S, T.y[:, lo:hi], y[0], [], [y[1]])
    for q in (V, S, PE, G):
        g.sync.wait_ge(T.sem["s" + q], count[q])
    for s in used:
        g.sync.wait_ge(T.sem[s], 16)
    for r in range(2):
        g.wait_ge(T.sem["lb%d" % r], NARR * len(STAGES))
        g.wait_ge(T.sem["lh%d" % r], NARR * len(STAGES))
